import numpy as np, ml_dtypes
CORES = [35,38,43,46]
N = 4
BF = ml_dtypes.bfloat16
def f(rng, *shape):
    return (rng.standard_normal(shape, dtype=np.float32) * np.exp2(rng.integers(-2, 3, shape[:-1] + (1,)))).astype(BF)
def wide(rng, *shape):
    v = f(rng, *shape).astype(np.float32); k = shape[:-2] + (1, shape[-1])
    return (v * np.exp2(rng.integers(-6, 7, k)) * (rng.random(k) > 0.0625)).astype(BF)
def gentries(a):
    return np.ascontiguousarray(a.reshape(8, 16, -1).transpose(0, 2, 1)).reshape(8, -1)
def gtable(e):
    e = np.asarray(e); return np.ascontiguousarray(e.reshape(8, -1, 16).transpose(0, 2, 1)).reshape(128, -1).astype(np.int32)
Q, CAPP, M, E, D = 512, 160, 4096, 8192, 4
LV, L = [1, 15, 210, 1900], 4000
EMPTY = 2 ** 24 - 1
def cut(rng, n, m, cap, s):
    u = rng.random((m, cap - 1)) + s * rng.random((m, 1))
    return 1 + np.bincount(np.argsort(u.reshape(-1))[:n - m] // (cap - 1), minlength=m)
def tree(rng, lv, n, keys, repeat=False):
    nk = np.sort(rng.integers(0, EMPTY - 16, (16, M)), axis=0) + np.arange(16)[:, None]
    nk[np.arange(16)[:, None] >= rng.integers(1, 17, (1, M))] = EMPTY
    beg = rng.integers(0, E - 15, M); kid = rng.integers(0, M, E)
    ids = np.concatenate([[0], 1 + rng.permutation(M - 1)]); a = np.cumsum([0] + list(lv))
    lev = [ids[a[l]:a[l + 1]] for l in range(D)]; nxt = lev[1:] + [rng.integers(0, M, n) if repeat else rng.permutation(M)[:n]]
    ek = np.asarray(keys); sizes = []
    for l in range(D - 1, -1, -1):
        sz = cut(rng, len(ek), lv[l], 16, 2.0); st = np.cumsum(sz) - sz
        nk[:, lev[l]] = EMPTY; nk[np.arange(len(ek)) - np.repeat(st, sz), np.repeat(lev[l], sz)] = ek
        ek = ek[st]; sizes.insert(0, sz)
    S = np.concatenate(sizes); C = np.concatenate(nxt); t = len(C); m = len(S)
    o = rng.permutation(m); so = S[o]; st = np.zeros(m, np.int64)
    st[o] = np.cumsum(so) - so + np.sort(rng.integers(0, E - 16 - t + 1, m))
    beg[ids[:m]] = st; kid[np.repeat(st - (np.cumsum(S) - S), S) + np.arange(t)] = C
    return nk, beg, kid
def make(rng, shapes=None, ends=False, full=False, alike=False, repeat=False):
    shapes = shapes or [(LV, L)] * N; I = np.int32
    spl = np.sort(rng.integers(0, EMPTY - 16384 * N + 1, (8, N - 1)), axis=1) + 16384 * np.arange(1, N)
    spl = np.concatenate([np.zeros((8, 1), np.int64), spl], axis=1); hi = np.concatenate([spl[:, 1:], np.full((8, 1), EMPTY)], axis=1)
    nk = np.zeros((N, 128, M), I); beg = np.zeros((N, 8, M), I); kid = np.zeros((N, 8, E), I); sk = np.zeros((N, 8, M), np.int64); ln = np.array([n for _, n in shapes])
    for r in range(N):
        lv, n = shapes[r]
        for g in range(8):
            w = int(hi[g, r] - spl[g, r])
            if ends: k = np.arange(n) + (w - n) * (r % 2)
            else: k = np.sort(rng.integers(0, w - n + 1, n)) + np.arange(n)
            k[0] = 0; k = k + spl[g, r]; sk[r, g, :n] = k
            nk[r, 16 * g:16 * g + 16], beg[r, g], kid[r, g] = tree(rng, lv, n, k, repeat)
    q = np.zeros((N, 8, Q), np.int64)
    for r in range(N):
        for g in range(8):
            if full: cn = np.zeros(N, np.int64); cn[rng.permutation(N)] = np.clip(Q - CAPP * np.arange(N), 0, CAPP)
            else: cn = 3 + cut(rng, Q - 3 * N, N, CAPP - 3, 0.5)
            own = np.repeat(np.arange(N), cn); st = np.cumsum(cn) - cn; occ = np.arange(Q) - st[own]
            a = spl[g, own]; b = hi[g, own]; k = sk[own, g, np.floor(rng.random(Q) * ln[own]).astype(np.int64)]
            inside = a + np.floor(rng.random(Q) * (b - a)).astype(np.int64)
            kd = 1 + occ % 4 if ends else np.array([0, 0, 0, 0, 0, 1, 1, 1, 2, 2, 2, 3, 4])[rng.integers(0, 13, Q)]
            v = np.choose(kd, [inside, k, np.maximum(k - 1, a), a, b - 1])
            if alike: v = v[st[own]]
            q[r, g] = v[rng.permutation(Q)]
    return {"nk": nk, "beg": beg, "kid": kid, "vec": f(rng, N, 128, M), "spl": np.stack([spl.astype(I)] * N), "q": np.stack([gtable(x) for x in q])}
def setup_inputs(rng):
    return make(rng)
def setup_inputs_caps(rng):
    return make(rng, full=True)
def setup_inputs_ends(rng):
    return make(rng, ends=True)
def setup_inputs_shapes(rng):
    a = []; n = M
    for l in range(D): n = -(-n // 16); a.insert(0, n)
    k = M * 3 // 8; b = [min(16 ** l, k) for l in range(D)]; s = int(rng.integers(0, 2))
    return make(rng, shapes=[(a, M) if (r + s) % 2 else (b, k) for r in range(N)], repeat=True)
def setup_inputs_alike(rng):
    return make(rng, alike=True)
def setup_inputs_spread(rng):
    d = make(rng); d["vec"] = wide(rng, N, 128, M); return d
def check_inputs(d):
    bad = []; nk, beg, kid, spl, q = [np.asarray(d[x]).astype(np.int64) for x in ("nk", "beg", "kid", "spl", "q")]
    if not np.isfinite(np.asarray(d["vec"]).astype(np.float32)).all(): bad.append("finite")
    if any(bool((a < 0).any() or (a > b).any()) for a, b in ((nk, EMPTY), (beg, E - 16), (kid, M - 1), (spl, EMPTY - 1), (q, EMPTY - 1))): return bad + ["ranges"]
    if (spl != spl[:1]).any() or (spl[:, :, 0] != 0).any() or (np.diff(spl, axis=2) <= 0).any(): return bad + ["splitters"]
    n4 = nk.reshape(N, 8, 16, M)
    if ((n4[:, :, 1:] <= n4[:, :, :-1]) & (n4[:, :, 1:] < EMPTY)).any(): bad.append("nodes")
    ok = True
    for r in range(N):
        for g in range(8):
            nd = np.zeros(1, np.int64); ek = spl[r, g, r:r + 1]; seen = [nd]
            for l in range(D):
                k = n4[r, g][:, nd].T
                if len(nd) > M or (k[:, 0] != ek).any(): ok = False; break
                use = k < EMPTY; ek = k[use]; nd = kid[r, g][(beg[r, g][nd][:, None] + np.arange(16))[use]]
                if l < D - 1:
                    seen.append(nd)
                    if len(nd) > M: ok = False; break
            if not ok: break
            s = np.concatenate(seen); top = spl[r, g, r + 1] if r + 1 < N else EMPTY
            if len(np.unique(s)) != len(s) or (np.diff(ek) <= 0).any() or ek[-1] >= top: ok = False
        if not ok: break
    if not ok: bad.append("tree")
    for r in range(N):
        x = gentries(q[r]); own = np.sum(x[:, :, None] >= spl[r][:, None, :], axis=2) - 1
        if any(np.bincount(own[g], minlength=N).max() > CAPP for g in range(8)): bad.append("caps"); break
    return bad
def reference(nk, beg, kid, vec, spl, q):
    y = np.zeros((N, 128, Q), vec.dtype); G = np.arange(8)[:, None]
    n4 = nk.reshape(N, 8, 16, M); v4 = vec.reshape(N, 8, 16, M)
    for r in range(N):
        x = gentries(q[r])
        own = np.sum(x[:, :, None] >= spl[r][:, None, :], axis=2) - 1
        at = np.zeros((8, Q), np.int64)
        for l in range(D):
            c = np.sum(n4[own, G, :, at] <= x[:, :, None], axis=2)
            at = kid[own, G, beg[own, G, at] + c - 1]
        y[r] = v4[own, G, :, at].transpose(0, 2, 1).reshape(128, Q)
    return {"y": y}

@@ -1,0 +1,361 @@
+from concourse.bass import DstId, RemoteDMATransfer
+from concourse.mybir import dt, AluOpType, AxisListType, ActivationFunctionType
+
+CAP = 160
+NS = 140
+W33 = 132
+
+SCRATCH = {
+    "spi": ("sbuf", [8, 4], "int32"),
+    "spf": ("sbuf", [8, 4], "float32"),
+    "onef": ("sbuf", [8, 128], "float32"),
+    "R8": ("sbuf", [8, 128], "float32"),
+}
+for _dt, _bufs in (
+    ("int32", "ql 32 X0 512 nks 4096 C 768 k1i 2 pid 1 pim 1 SX 640 QX 640 K2 16 K3 256"),
+    ("float32", "k1f 1 ioI 1"),
+    ("bfloat16", "vcs 4096 BK 8192 CH 768 CL 768 ones 160 BDa 128 NLa 128 NL 128 NU 128 NLm 128 NUm 128 R0 128 RBa 128 RB 128 CB 132 RST 132 "
+                 "D01 320 wt 48 WW 432 ID 128 I16 128 GE 176 MK 132 kg16 16 b2 16 kg256 256 b3w 256 "
+                 "cm1 640 cm2 640 cm3 640 cm4 640 l1b 40 bg3 640 bg4 640 kg3 640 kg4 640 AN 480 RX 640 yb 512"),
+    ("float16", "VAL 132 F1 66 SL 32 TT 32"),
+    ("uint16", "LA 32 LB 32 L16 2 LM2 2 L256 16 LM3 16 l1 40 l2 40 i3 40 m4 40 i4 40 vn 40"),
+):
+    _w = _bufs.split()
+    for _k in range(0, len(_w), 2):
+        SCRATCH[_w[_k]] = ("sbuf", [128, int(_w[_k + 1])], _dt)
+for _k in "pS pT pN pA p1 p2 pC pD".split():
+    SCRATCH[_k] = ("psum", [128, 512], "float32")
+SEMAPHORES = ["s%d" % i for i in range(NS)] + ["rq%d" % i for i in range(4)] + ["ra%d" % i for i in range(4)] + ["lq", "la"]
+
+A = AluOpType
+COPY = ActivationFunctionType.Copy
+
+PLAN = """c1o Ta l1o c1f Tb Tc l1f c2f Td Te l2f L3f c2o i3f k3f l2o L3o m4f L4f i3o k3o i4f k4f m4o L4o vnf vef send
+ i4o k4o vno veo"""
+
+
+def rank_program(g, core, T, topo):
+    me = T.rank_of(core)
+    if me is None:
+        return
+    v, s, te, sy = g.vector, g.scalar, g.tensor, g.sync
+    queues = {"g": g, "v": v, "s": s, "t": te, "y": sy}
+    used = [0]
+    seen = {}
+    waited = {}
+    every = []
+
+    def incs(*ins, n=1):
+        name = "s%d" % used[0]
+        used[0] += 1
+        for x in ins:
+            x.then_inc(T.sem[name], n)
+        tok = (name, n * len(ins))
+        every.append(tok)
+        return tok
+
+    def dmas(*calls):
+        return incs(*[q.dma_start(out, in_) for q, out, in_ in calls], n=16)
+
+    def W(key, *toks):
+        for tok in toks:
+            if (key, tok) in seen:
+                continue
+            seen[(key, tok)] = True
+            waited[tok] = True
+            queues[key].wait_ge(T.sem[tok[0]], tok[1])
+
+    def conv(out, wt, src, n, start=True, stop=True):
+        ins = None
+        for i in range(16):
+            ins = te.matmul(out, wt[:, 15 - i:143 - i], src[:, i:n:16], start and i == 0, stop and i == 15)
+        return ins
+
+    d_ql = dmas((sy, T.ql[:], T.q[:]))
+    d_sp = dmas((s, T.spi[:], T.spl[:]))
+    d_k1 = dmas((s, T.k1i[:], T.nk[:, 0:2]))
+    d_x0 = dmas(*[((sy, s)[o % 2], T.X0[o::16, :], T.q[:]) for o in range(16)])
+    d_sx = dmas((sy, T.SX[:, 0:512], T.kid[:]), (s, T.SX[:, 512:640], T.beg[:, 0:2048]))
+    d_c = dmas((sy, T.C[:, 0:512], T.kid[:]), (sy, T.C[:, 512:768], T.beg[:]))
+    d_na = dmas((sy, T.nks[0:96, :], T.nk[0:96, :]))
+
+    t_onef = incs(v.memset(T.onef[:], 1.0))
+    t_ones = incs(v.memset(T.ones[:], 1.0))
+    t_cb0 = incs(v.memset(T.CB[:], 0.0))
+    t_rs0 = incs(v.memset(T.RST[:], 1.0))
+    t_bk0 = incs(v.memset(T.BK[:, 0:2048], 0.0))
+    t_mk0 = incs(v.memset(T.GE[:, 0:1], 0.0))
+
+    def fill(a, b):
+        return incs(s.activation(T.BK[:, a:b], T.BK[:, 0:b - a], COPY))
+
+    W("s", t_ones, t_cb0)
+    s_cb = incs(*[s.activation(T.CB[:, 33 * r:33 * r + 1], T.ones[:, 0:1], COPY, scale=1.25 * r) for r in (1, 2, 3)])
+    W("s", t_rs0)
+    s_rst = incs(s.activation(T.RST[:, 0:132:33], T.ones[:, 0:4], COPY, scale=0.0))
+    s_ge0 = incs(s.activation(T.GE[:, 33:166:33], T.ones[:, 0:5], COPY, scale=0.0), s.activation(T.GE[:, 1:33], T.ones[:, 0:32], COPY),
+                 s.activation(T.GE[:, 133:165], T.ones[:, 0:32], COPY, scale=0.0))
+    W("s", t_bk0)
+    z = [fill(2048, 2560)]
+
+    def sel(out, in_, pattern, op, base, cm, *deps):
+        W("g", *deps)
+        return incs(g.affine_select(out, in_, pattern, op, 0.0, base, cm))
+
+    Wk, Wb, Wc = T.WW[:, 0:144], T.WW[:, 144:288], T.WW[:, 288:432]
+    c_r8 = sel(T.R8[:], T.onef[:], [[-1, 8], [0, 16]], A.is_equal, 0, 1, t_onef)
+    c_bda = sel(T.BDa[:], T.ones[:, 0:128], [[16, 8], [0, 16]], A.is_ge, 15, -1, t_ones)
+    c = sel(T.NLa[:], T.ones[:, 0:128], [[16, 8], [1, 16]], A.is_gt, 0, -1, t_ones)
+    c_nl = sel(T.NL[:], T.NLa[:], [[-16, 8], [0, 16]], A.is_ge, 0, 1, c)
+    c_nu = sel(T.NU[:], T.BDa[:], [[-16, 8], [-1, 16]], A.is_ge, 0, 1, c_bda)
+    W("g", t_ones)
+    c_d01 = incs(g.affine_select(T.D01[:, 0:160], T.ones[:], [[-32, 5], [-1000, 2], [-1, 16]], A.is_equal, 0.0, 1000, 1),
+                 g.affine_select(T.D01[:, 160:320], T.ones[:], [[-32, 5], [-1000, 2], [-1, 16]], A.is_equal, 0.0, 16, 1))
+    W("s", c_nl)
+    s_nl = incs(s.activation(T.NLm[:], T.NL[:], COPY, scale=-1.0))
+    W("s", c_nu)
+    s_nm = incs(s.activation(T.NUm[:], T.NU[:], COPY, scale=-1.0))
+    z += [fill(a, b) for a, b in ((2560, 4608), (4608, 6656), (6656, 8192))]
+    c_pid = incs(g.iota(T.pid[:], [[0, 1]], 0, 1))
+    c_r0 = sel(T.R0[:], T.ones[:, 0:128], [[-16, 8], [0, 16]], A.is_equal, 0, 1, t_ones)
+    c = sel(T.RBa[:], T.ones[:, 0:128], [[16, 8], [0, 16]], A.is_ge, 3, -1, t_ones)
+    c_rb = sel(T.RB[:], T.RBa[:], [[-16, 8], [0, 16]], A.is_ge, -2, 1, c)
+
+    W("v", d_sp)
+    t_spf = incs(v.tensor_copy(T.spf[:], T.spi[:]))
+    W("t", t_spf, c_r8)
+    p_sp = incs(te.matmul(T.pS[:, 0:4], T.R8[:], T.spf[:], True, True))
+    W("t", t_ones, s_cb)
+    te.matmul(T.pN[:, 0:W33], T.ones[:, 0:128], T.CB[:], True, False)
+    W("v", d_ql, p_sp)
+    t_ge = incs(*[v.tensor_scalar(T.GE[:, 33 * r + 1:33 * r + 33], T.ql[:], T.pS[:, r:r + 1], None, A.is_ge) for r in (1, 2, 3)])
+    W("t", t_ge, s_ge0, t_mk0, c_nl, c_nu)
+    te.matmul(T.pN[:, 0:W33], T.NL[:], T.GE[:, 1:133], False, False)
+    te.matmul(T.pN[:, 0:W33], T.NU[:], T.GE[:, 0:132], False, False)
+    W("t", s_nl)
+    te.matmul(T.pN[:, 0:W33], T.NLm[:], T.GE[:, 34:166], False, False)
+    W("t", s_nm)
+    p_e = incs(te.matmul(T.pN[:, 0:W33], T.NUm[:], T.GE[:, 33:165], False, True))
+    W("v", t_ge, s_ge0)
+    t_mk = incs(v.tensor_tensor(T.MK[:], T.GE[:, 1:133], T.GE[:, 34:166], A.subtract))
+    W("v", p_e, s_rst)
+    t_u = incs(v.tensor_tensor_scan(T.pT[:, 0:W33], T.RST[:], T.pN[:, 0:W33], 0.0, A.mult, A.add))
+    W("v", t_u, t_mk)
+    t_val = incs(v.tensor_tensor(T.VAL[:], T.MK[:], T.pT[:, 0:W33], A.mult))
+    W("v", t_val)
+    t_f1 = incs(v.tensor_tensor(T.F1[:], T.VAL[:, 0:66], T.VAL[:, 66:132], A.add))
+    W("v", t_f1)
+    t_sl = incs(v.tensor_tensor(T.SL[:], T.F1[:, 0:32], T.F1[:, 33:65], A.add))
+    W("v", t_sl)
+    t_tt = incs(v.transpose(T.TT[:], T.SL[:]))
+    W("t", t_tt, c_d01)
+    p_a = []
+    for w in range(2):
+        for gg in range(2):
+            sh = 160 * w + 16 + 16 * (w - gg)
+            p_a.append(te.matmul(T.pA[:, w:32:2], T.D01[:, sh:sh + 128], T.TT[:, 16 * gg:16 * gg + 16], gg == 0, gg == 1))
+    p_a = incs(*p_a[1::2])
+    t_w0 = incs(v.memset(T.WW[:], 0.0))
+    W("v", p_a)
+    t_la = incs(v.tensor_copy(T.LA[:], T.pA[:, 0:32]))
+    W("v", t_la, d_x0, d_sx)
+    t_sc = incs(v.tensor_copy(T.SX[:, 0:640].indirect(T.LA[:, 0:32]), T.X0[:]))
+
+    def engines_of(src, dst):
+        away = [d for d in T.cores if topo.chip(d) != topo.chip(src)]
+        ae = topo.engines(src, away[0])
+        if dst in away:
+            n = len(ae) // len(away)
+            return ae[away.index(dst) * n:away.index(dst) * n + n]
+        return [e for e in topo.engines(src, dst) if e not in ae][::2]
+
+    def count(r):
+        return len(engines_of(T.cores[r], core))
+
+    def order(x):
+        return sorted([r for r in range(4) if r != x], key=lambda r: topo.chip(T.cores[r]) == topo.chip(T.cores[x]))
+
+    others = order(me)
+
+    def exchange(src, dst, at, to, sem, lsem):
+        tr = []
+        for r in others:
+            d = T.cores[r]
+            a = topo.addr(d)
+            tr.append(RemoteDMATransfer(dst_ids=[DstId(rid=a[0], pnc=a[1])], dma_engine_mask=sum(1 << e for e in engines_of(core, d)),
+                                        remote_sem=T.sem["%s%d" % (sem, me)], src=src[:, CAP * at(r):CAP * at(r) + CAP],
+                                        dst=dst[:, CAP * to(r):CAP * to(r) + CAP]))
+        g.remote_dma_fused(tr, local_sem=T.sem[lsem])
+        return sum(len(engines_of(core, T.cores[r])) for r in others)
+
+    W("g", t_sc)
+    n_lq = exchange(T.SX, T.QX, lambda r: r, lambda r: order(r).index(me), "rq", "lq")
+
+    def weights(w, n, lo, hi):
+        c = sel(T.wt[:, 16 * n:16 * n + 9], T.ones[:, 0:9], [[-16, 9]], A.is_ge, -lo, 1, t_ones)
+        return sel(w[:, 15:144:16], T.wt[:, 16 * n:16 * n + 9], [[16, 9]], A.is_ge, hi, -1, c, t_w0)
+
+    c_wc = weights(Wc, 0, 1, 15)
+    c_wk = weights(Wk, 1, 0, 1)
+    c_wb = weights(Wb, 2, 2, 3)
+    W("v", d_c)
+    parts = ((512, 768), (0, 512))
+    t_ch = [incs(v.tensor_copy(T.CH[:, a:b], T.C[:, a:b])) for a, b in parts]
+    t_cl = []
+    for (a, b), t in zip(parts, t_ch):
+        W("v", t)
+        t_cl.append(incs(v.tensor_tensor(T.CL[:, a:b], T.C[:, a:b], T.CH[:, a:b], A.subtract)))
+    W("t", *t_ch[:1], *t_cl[:1], c_r0, t_la)
+    te.matmul(T.p1[:, 0:1], T.R0[:], T.CH[:, 512:513], True, False)
+    p_b0 = incs(te.matmul(T.p1[:, 0:1], T.R0[:], T.CL[:, 512:513], False, True))
+    W("y", *t_ch, *z, t_bk0)
+    b1 = [sy.dma_start(T.BK[2::16, 0:4096], T.CH[:, 512:768]), sy.dma_start(T.BK[0::16, :], T.CH[:, 0:512])]
+    W("y", *t_cl)
+    b1 += [sy.dma_start(T.BK[3::16, 0:4096], T.CL[:, 512:768]), sy.dma_start(T.BK[1::16, :], T.CL[:, 0:512])]
+    d_bk = incs(*b1, n=16)
+    d_nb = dmas((sy, T.nks[96:128, :], T.nk[96:128, :]))
+    d_vec = dmas((sy, T.vcs[:], T.vec[:]))
+    W("v", t_sc)
+    t_ox = incs(v.tensor_copy(T.QX[:, 480:640], T.SX[:, CAP * me:CAP * me + CAP]))
+    W("v", d_k1)
+    t_k1 = incs(v.tensor_copy(T.k1f[:], T.k1i[:, 0:1]))
+    W("v", c_pid)
+    t_pim = incs(v.tensor_scalar(T.pim[:], T.pid[:], 15, None, A.bitwise_and))
+    t_lb = incs(v.tensor_copy(T.LB[:], T.SL[:]))
+    W("v", t_pim)
+    t_io = incs(v.tensor_copy(T.ioI[:], T.pim[:]))
+    W("v", p_b0, t_io)
+    t_l16 = incs(v.tensor_scalar(T.L16[:, 0:1], T.p1[:, 0:1], T.ioI[:, 0:1], None, A.add))
+    c_id = sel(T.ID[:], T.ones[:, 0:128], [[-1, 128]], A.is_equal, 0, 1, t_ones)
+    W("s", c_id)
+    s_i16 = incs(s.activation(T.I16[:], T.ID[:], COPY, scale=16.0))
+
+    B = {"f": (0, 480, 224, (T.pD, T.pT), ((320, 480, tuple(others[2:])), (0, 320, tuple(others[:2])))),
+         "o": (480, 640, 480, (T.pN, T.pA), ((480, 640, ()),))}
+    tok = {}
+
+    def cols(x, b):
+        return x[:, b[0]:b[1]]
+
+    def lst(x, b):
+        return x[:, b[0] // 16:b[1] // 16]
+
+    def bank(b, k):
+        return b[3][k % 2][:, 0:(b[1] - b[0]) // 16]
+
+    def c1(b):
+        W("v", t_k1, t_ox)
+        c = []
+        for lo, hi, those in b[4]:
+            for r in those:
+                v.wait_ge(T.sem["rq%d" % r], count(r))
+            c.append(v.tensor_scalar(T.cm1[:, lo:hi], T.QX[:, lo:hi], T.k1f[:, 0:1], None, A.is_ge))
+        tok["c1", b] = incs(*c)
+        W("t", c_wc, t_la, tok["c1", b])
+        tok["p1", b] = incs(conv(bank(b, 0), Wc, cols(T.cm1, b), b[1] - b[0]))
+
+    def lists(b, pn, name, k):
+        W("v", tok[pn, b])
+        tok[name, b] = incs(v.tensor_copy(lst(T[name], b), bank(b, k)))
+
+    def c2(b):
+        W("v", tok["l1", b], tok["K2"])
+        tok["c2", b] = incs(v.tensor_tensor(cols(T.cm2, b), T.K2[:, 0:16].indirect(lst(T.l1, b)), cols(T.QX, b), A.is_le))
+        tok["lb", b] = incs(v.tensor_copy(lst(T.l1b, b), bank(b, 0)))
+        W("t", tok["c2", b])
+        conv(bank(b, 1), Wc, cols(T.cm2, b), b[1] - b[0], True, False)
+        W("t", tok["lb", b], s_i16)
+        tok["p2", b] = incs(te.matmul(bank(b, 1), T.I16[:], lst(T.l1b, b), False, True))
+
+    def level(b, lin, win, nodes, bg, cm, pn, k, *deps):
+        W("s", tok[lin, b], *deps[:1])
+        tok["b" + pn, b] = incs(s.activation(cols(bg, b), win.indirect(lst(T[lin], b)), COPY))
+        W("v", tok[lin, b], *deps[1:])
+        tok["c" + pn, b] = incs(v.tensor_tensor(cols(cm, b), nodes.indirect(lst(T[lin], b)), cols(T.QX, b), A.is_le))
+        W("t", c_wb, tok["b" + pn, b])
+        conv(bank(b, k), Wb, cols(bg, b), b[1] - b[0], True, False)
+        W("t", tok["c" + pn, b])
+        tok[pn, b] = incs(conv(bank(b, k), Wc, cols(cm, b), b[1] - b[0], False, True))
+
+    def shared(b, win, lin, out, at, *deps):
+        a = []
+        for key, lo, hi in (("s", b[2], b[1]), ("v", b[0], b[2])):
+            if lo < hi:
+                W(key, tok[lin, b], *deps)
+                x, y = out[:, lo - at:hi - at], win.indirect(T[lin][:, lo // 16:hi // 16])
+                a.append(incs(s.activation(x, y, COPY) if key == "s" else v.tensor_copy(x, y)))
+        return a
+
+    def kids(b, lin, kg, pn, k):
+        W("t", c_wk, *shared(b, T.BK[:, 0:8192], lin, kg, 0))
+        tok[pn, b] = incs(conv(bank(b, k), Wk, cols(kg, b), b[1] - b[0]))
+
+    def vectors(b):
+        own = b is B["o"]
+        tok["ve", b] = shared(b, T.vcs[:, 0:4096], "vn", T.RX[:, CAP * me:CAP * me + CAP] if own else T.AN, b[0] if own else 0, d_vec)
+
+    steps = {"c1": c1, "l1": lambda b: lists(b, "p1", "l1", 0), "c2": c2, "l2": lambda b: lists(b, "p2", "l2", 1),
+             "L3": lambda b: level(b, "l2", T.b3w[:, 0:256], T.K3[:, 0:256], T.bg3, T.cm3, "p3", 2, tok["b3"], tok["K3"]),
+             "i3": lambda b: lists(b, "p3", "i3", 2), "k3": lambda b: kids(b, "i3", T.kg3, "p4", 3),
+             "m4": lambda b: lists(b, "p4", "m4", 3),
+             "L4": lambda b: level(b, "m4", T.BK[:, 0:4096], T.nks[:, 0:4096], T.bg4, T.cm4, "p5", 4),
+             "i4": lambda b: lists(b, "p5", "i4", 4), "k4": lambda b: kids(b, "i4", T.kg4, "p6", 5),
+             "vn": lambda b: lists(b, "p6", "vn", 5), "ve": vectors}
+
+    def table(x):
+        if x == "a":
+            W("s", t_l16, d_bk)
+            c = incs(s.activation(T.kg16[:], T.BK[:, 0:8192].indirect(T.L16[:, 0:1]), COPY))
+            W("t", c, c_wk)
+            tok["p_m2"] = incs(conv(T.p2[:, 0:1], Wk, T.kg16, 16))
+        if x == "b":
+            W("v", tok["p_m2"])
+            tok["LM2"] = incs(v.tensor_copy(T.LM2[:, 0:1], T.p2[:, 0:1]))
+            W("s", tok["LM2"])
+            c = incs(s.activation(T.b2[:], T.BK[:, 0:4096].indirect(T.LM2[:, 0:1]), COPY))
+            W("t", c, t_l16, c_rb)
+            tok["p_b2"] = incs(te.matmul(T.p1[:, 0:16], T.RB[:], T.b2[:], True, True))
+            W("v", d_na, d_nb, tok["LM2"])
+            tok["K2"] = incs(v.tensor_copy(T.K2[:], T.nks[:, 0:4096].indirect(T.LM2[:, 0:1])))
+        if x == "c":
+            W("v", tok["p_b2"])
+            c = incs(v.tensor_scalar(T.L256[:], T.p1[:, 0:16], T.ioI[:, 0:1], None, A.add))
+            W("s", c)
+            c = incs(s.activation(T.kg256[:], T.BK[:, 0:8192].indirect(T.L256[:, 0:16]), COPY))
+            W("t", c, tok["LM2"])
+            tok["p_m3"] = incs(conv(T.p2[:, 0:16], Wk, T.kg256, 256))
+        if x == "d":
+            W("v", tok["p_m3"])
+            tok["LM3"] = incs(v.tensor_copy(T.LM3[:], T.p2[:, 0:16]))
+            W("s", tok["LM3"])
+            tok["b3"] = incs(s.activation(T.b3w[:], T.BK[:, 0:4096].indirect(T.LM3[:, 0:16]), COPY))
+        if x == "e":
+            W("v", tok["LM3"])
+            tok["K3"] = incs(v.tensor_copy(T.K3[:], T.nks[:, 0:4096].indirect(T.LM3[:, 0:16])))
+
+    n_la = 0
+    for x in PLAN.split():
+        if x == "send":
+            W("g", *tok["ve", B["f"]])
+            n_la = exchange(T.AN, T.RX, lambda r: others.index(r), lambda r: me, "ra", "la")
+        elif x[0] == "T":
+            table(x[1])
+        else:
+            steps[x[:2]](B[x[2]])
+
+    W("v", t_lb, *tok["ve", B["o"]])
+    W("s", t_lb, *tok["ve", B["o"]])
+    for r in others:
+        v.wait_ge(T.sem["ra%d" % r], count(r))
+        s.wait_ge(T.sem["ra%d" % r], count(r))
+    t_y = incs(v.tensor_copy(T.yb[:, 0:256], T.RX[:, 0:640].indirect(T.LB[:, 0:16])))
+    s_y = incs(s.activation(T.yb[:, 256:512], T.RX[:, 0:640].indirect(T.LB[:, 16:32]), COPY))
+    W("y", t_y)
+    d_y0 = dmas((sy, T.y[:, 0:256], T.yb[:, 0:256]))
+    W("s", s_y)
+    d_y1 = dmas((s, T.y[:, 256:512], T.yb[:, 256:512]))
+    W("y", d_y0)
+    W("s", d_y1)
+    g.wait_ge(T.sem.lq, n_lq)
+    g.wait_ge(T.sem.la, n_la)
+    W("g", *[t for t in every if t not in waited])

@@ -2,36 +2,43 @@ from concourse.bass import DstId, RemoteDMATransfer
 from concourse.mybir import dt, AluOpType, AxisListType, ActivationFunctionType
 
 CAP = 160
-NS = 140
+NS = 128
 W33 = 132
+HALF = 2048.0
 
 SCRATCH = {
     "spi": ("sbuf", [8, 4], "int32"),
     "spf": ("sbuf", [8, 4], "float32"),
+    "b0i": ("sbuf", [8, 2], "int32"),
+    "b0f": ("sbuf", [8, 2], "float32"),
     "onef": ("sbuf", [8, 128], "float32"),
     "R8": ("sbuf", [8, 128], "float32"),
+    "Z3f": ("sbuf", [128, 480, 2], "bfloat16"),
+    "Z4f": ("sbuf", [128, 480, 2], "bfloat16"),
+    "Z3o": ("sbuf", [128, 160, 2], "bfloat16"),
+    "Z4o": ("sbuf", [128, 160, 2], "bfloat16"),
 }
 for _dt, _bufs in (
-    ("int32", "ql 32 X0 512 nks 4096 C 768 k1i 2 pid 1 pim 1 SX 640 QX 640 K2 16 K3 256"),
-    ("float32", "k1f 1 ioI 1"),
-    ("bfloat16", "vcs 4096 BK 8192 CH 768 CL 768 ones 160 BDa 128 NLa 128 NL 128 NU 128 NLm 128 NUm 128 R0 128 RBa 128 RB 128 CB 132 RST 132 "
-                 "D01 320 wt 48 WW 432 ID 128 I16 128 GE 176 MK 132 kg16 16 b2 16 kg256 256 b3w 256 "
-                 "cm1 640 cm2 640 cm3 640 cm4 640 l1b 40 bg3 640 bg4 640 kg3 640 kg4 640 AN 480 RX 640 yb 512"),
-    ("float16", "VAL 132 F1 66 SL 32 TT 32"),
-    ("uint16", "LA 32 LB 32 L16 2 LM2 2 L256 16 LM3 16 l1 40 l2 40 i3 40 m4 40 i4 40 vn 40"),
+    ("int32", "ql 32 X0 512 W 8192 BC 256 BH 256 BL 256 K1A 16 QS 1120 K2 16 K3 256"),
+    ("float32", "k1f 4 ioI 1 mk0 1 mkb 1 sm3 80 sm4 80"),
+    ("bfloat16", "vcs 4096 ones 160 BD 128 BDm 128 NL 128 NLm 128 CB 132 RST 132 alt 64 "
+                 "D01 320 wt 16 WW 288 GE 176 MK 132 b2 16 b3w 256 cm1 640 cm2 640 l1b 40 AR 1120 yb 512"),
+    ("float16", "VAL 132 F1 66 SL 32 TT 32 kg16 16 kg256 256 kg3 640 kg4 640"),
+    ("uint16", "LA 32 LB 32 L16 2 LM2 2 L256 16 LM3 16 l1s 40 l1 32 l2 40 i3 40 m4 40 i4 40 vn 40"),
 ):
     _w = _bufs.split()
     for _k in range(0, len(_w), 2):
         SCRATCH[_w[_k]] = ("sbuf", [128, int(_w[_k + 1])], _dt)
-for _k in "pS pT pN pA p1 p2 pC pD".split():
+for _k in "pS pT pN pA p1 p2 pB pD".split():
     SCRATCH[_k] = ("psum", [128, 512], "float32")
-SEMAPHORES = ["s%d" % i for i in range(NS)] + ["rq%d" % i for i in range(4)] + ["ra%d" % i for i in range(4)] + ["lq", "la"]
+SEMAPHORES = ["s%d" % i for i in range(NS)] + ["%s%d" % (x, i) for x in ("rk", "rq", "rl", "ra") for i in range(4)] + ["lk", "lq", "ll", "la"]
 
 A = AluOpType
-COPY = ActivationFunctionType.Copy
+F = ActivationFunctionType
 
-PLAN = """c1o Ta l1o c1f Tb Tc l1f c2f Td Te l2f L3f c2o i3f k3f l2o L3o m4f L4f i3o k3o i4f k4f m4o L4o vnf vef send
+PLAN = """Ta Tb Tc c2f Td Te l2f L3f c2o i3f k3f l2o L3o m4f L4f i3o k3o i4f k4f m4o L4o vnf vef send
  i4o k4o vno veo"""
+NK_EARLY = 15
 
 
 def rank_program(g, core, T, topo):
@@ -65,77 +72,113 @@ def rank_program(g, core, T, topo):
             waited[tok] = True
             queues[key].wait_ge(T.sem[tok[0]], tok[1])
 
-    def conv(out, wt, src, n, start=True, stop=True):
+    def conv(out, wt, src, start=True, stop=True):
         ins = None
         for i in range(16):
-            ins = te.matmul(out, wt[:, 15 - i:143 - i], src[:, i:n:16], start and i == 0, stop and i == 15)
+            ins = te.matmul(out, wt[:, 15 - i:143 - i], src(i), start and i == 0, stop and i == 15)
         return ins
+
+    def order(x):
+        return sorted([r for r in range(4) if r != x], key=lambda r: topo.chip(T.cores[r]) == topo.chip(T.cores[x]))
+
+    others = order(me)
+    place = {r: k for k, r in enumerate([me] + others)}
+
+    def engines_of(src, dst):
+        away = [d for d in T.cores if topo.chip(d) != topo.chip(src)]
+        ae = topo.engines(src, away[0])
+        if dst in away:
+            n = len(ae) // len(away)
+            return ae[away.index(dst) * n:away.index(dst) * n + n]
+        return [e for e in topo.engines(src, dst) if e not in ae][::2]
+
+    def arrived(q, sem):
+        for r in others:
+            q.wait_ge(T.sem["%s%d" % (sem, r)], len(engines_of(T.cores[r], core)))
+
+    sent = []
+
+    def exchange(src, dst, sem, lsem):
+        tr = []
+        for r in others:
+            d = T.cores[r]
+            a = topo.addr(d)
+            tr.append(RemoteDMATransfer(dst_ids=[DstId(rid=a[0], pnc=a[1])], dma_engine_mask=sum(1 << e for e in engines_of(core, d)),
+                                        remote_sem=T.sem["%s%d" % (sem, me)], src=src(place[r]), dst=dst(1 + order(r).index(me))))
+        g.remote_dma_fused(tr, local_sem=T.sem[lsem])
+        sent.append((lsem, sum(len(engines_of(core, T.cores[r])) for r in others)))
+
+    SX = T.QS[:, 480:1120]
+    RX = T.AR[:, 480:1120]
 
     d_ql = dmas((sy, T.ql[:], T.q[:]))
     d_sp = dmas((s, T.spi[:], T.spl[:]))
-    d_k1 = dmas((s, T.k1i[:], T.nk[:, 0:2]))
-    d_x0 = dmas(*[((sy, s)[o % 2], T.X0[o::16, :], T.q[:]) for o in range(16)])
-    d_sx = dmas((sy, T.SX[:, 0:512], T.kid[:]), (s, T.SX[:, 512:640], T.beg[:, 0:2048]))
-    d_c = dmas((sy, T.C[:, 0:512], T.kid[:]), (sy, T.C[:, 512:768], T.beg[:]))
-    d_na = dmas((sy, T.nks[0:96, :], T.nk[0:96, :]))
+    d_k1 = dmas((sy, T.K1A[:, 0:2], T.nk[:, 0:2]))
+    d_b0 = dmas((s, T.b0i[:], T.beg[:, 0:2]))
+    d_bc = dmas((s, T.BC[:], T.beg[:]))
+    d_x0 = dmas(*[((sy, sy, sy, s)[o % 4], T.X0[o::16, :], T.q[:]) for o in range(16)])
+    d_w = [dmas((sy, T.W[0::16, 0:4096], T.kid[:, 0:4096]), *[(sy, T.W[o::16, 0:4096], T.nk[o::16, :]) for o in range(1, NK_EARLY + 1)])]
 
     t_onef = incs(v.memset(T.onef[:], 1.0))
     t_ones = incs(v.memset(T.ones[:], 1.0))
     t_cb0 = incs(v.memset(T.CB[:], 0.0))
     t_rs0 = incs(v.memset(T.RST[:], 1.0))
-    t_bk0 = incs(v.memset(T.BK[:, 0:2048], 0.0))
+    t_z0 = incs(v.memset(T.W[:, 4096:4608], 0))
     t_mk0 = incs(v.memset(T.GE[:, 0:1], 0.0))
+    t_sx0 = [incs(v.memset(T.QS[:, 480:800], 0))]
 
     def fill(a, b):
-        return incs(s.activation(T.BK[:, a:b], T.BK[:, 0:b - a], COPY))
-
-    W("s", t_ones, t_cb0)
-    s_cb = incs(*[s.activation(T.CB[:, 33 * r:33 * r + 1], T.ones[:, 0:1], COPY, scale=1.25 * r) for r in (1, 2, 3)])
-    W("s", t_rs0)
-    s_rst = incs(s.activation(T.RST[:, 0:132:33], T.ones[:, 0:4], COPY, scale=0.0))
-    s_ge0 = incs(s.activation(T.GE[:, 33:166:33], T.ones[:, 0:5], COPY, scale=0.0), s.activation(T.GE[:, 1:33], T.ones[:, 0:32], COPY),
-                 s.activation(T.GE[:, 133:165], T.ones[:, 0:32], COPY, scale=0.0))
-    W("s", t_bk0)
-    z = [fill(2048, 2560)]
+        return incs(s.activation(T.W[:, a:b], T.W[:, 4096:4096 + b - a], F.Copy))
 
     def sel(out, in_, pattern, op, base, cm, *deps):
         W("g", *deps)
         return incs(g.affine_select(out, in_, pattern, op, 0.0, base, cm))
 
-    Wk, Wb, Wc = T.WW[:, 0:144], T.WW[:, 144:288], T.WW[:, 288:432]
     c_r8 = sel(T.R8[:], T.onef[:], [[-1, 8], [0, 16]], A.is_equal, 0, 1, t_onef)
-    c_bda = sel(T.BDa[:], T.ones[:, 0:128], [[16, 8], [0, 16]], A.is_ge, 15, -1, t_ones)
-    c = sel(T.NLa[:], T.ones[:, 0:128], [[16, 8], [1, 16]], A.is_gt, 0, -1, t_ones)
-    c_nl = sel(T.NL[:], T.NLa[:], [[-16, 8], [0, 16]], A.is_ge, 0, 1, c)
-    c_nu = sel(T.NU[:], T.BDa[:], [[-16, 8], [-1, 16]], A.is_ge, 0, 1, c_bda)
-    W("g", t_ones)
-    c_d01 = incs(g.affine_select(T.D01[:, 0:160], T.ones[:], [[-32, 5], [-1000, 2], [-1, 16]], A.is_equal, 0.0, 1000, 1),
-                 g.affine_select(T.D01[:, 160:320], T.ones[:], [[-32, 5], [-1000, 2], [-1, 16]], A.is_equal, 0.0, 16, 1))
+    W("t", c_r8)
+    p_bd = incs(te.matmul(T.pB[:, 0:128], T.R8[:], T.R8[:], True, True))
+    W("s", t_ones, t_cb0)
+    s_cb = incs(*[s.activation(T.CB[:, 33 * r:33 * r + 1], T.ones[:, 0:1], F.Copy, scale=CAP / 16 * place[r]) for r in others])
+    W("s", t_rs0)
+    s_rst = incs(s.activation(T.RST[:, 0:132:33], T.ones[:, 0:4], F.Copy, scale=0.0))
+    s_ge0 = incs(s.activation(T.GE[:, 33:166:33], T.ones[:, 0:5], F.Copy, scale=0.0), s.activation(T.GE[:, 1:33], T.ones[:, 0:32], F.Copy),
+                 s.activation(T.GE[:, 133:165], T.ones[:, 0:32], F.Copy, scale=0.0))
+    W("s", p_bd)
+    s_bd = incs(s.activation(T.BD[:], T.pB[:, 0:128], F.Copy))
+    s_bm = incs(s.activation(T.BDm[:], T.pB[:, 0:128], F.Copy, scale=-1.0))
+    W("s", t_z0)
+    z = [fill(4608, 4864)]
+    c_d0 = sel(T.D01[:, 0:160], T.ones[:], [[-32, 5], [-1000, 2], [-1, 16]], A.is_equal, 1000, 1, t_ones)
+    c_nl = sel(T.NL[:], T.BD[:], [[1, 128]], A.is_gt, 0, -1, s_bd)
+    c_d1 = sel(T.D01[:, 160:320], T.ones[:], [[-32, 5], [-1000, 2], [-1, 16]], A.is_equal, 16, 1, t_ones)
     W("s", c_nl)
-    s_nl = incs(s.activation(T.NLm[:], T.NL[:], COPY, scale=-1.0))
-    W("s", c_nu)
-    s_nm = incs(s.activation(T.NUm[:], T.NU[:], COPY, scale=-1.0))
-    z += [fill(a, b) for a, b in ((2560, 4608), (4608, 6656), (6656, 8192))]
-    c_pid = incs(g.iota(T.pid[:], [[0, 1]], 0, 1))
-    c_r0 = sel(T.R0[:], T.ones[:, 0:128], [[-16, 8], [0, 16]], A.is_equal, 0, 1, t_ones)
-    c = sel(T.RBa[:], T.ones[:, 0:128], [[16, 8], [0, 16]], A.is_ge, 3, -1, t_ones)
-    c_rb = sel(T.RB[:], T.RBa[:], [[-16, 8], [0, 16]], A.is_ge, -2, 1, c)
+    s_nl = incs(s.activation(T.NLm[:], T.NL[:], F.Copy, scale=-1.0))
+    W("s", z[0])
+    z += [fill(4864, 5632)]
+    W("s", z[1])
+    z += [fill(5632, 7168), fill(7168, 8192)]
+
+    W("g", d_k1)
+    exchange(lambda k: T.K1A[:, 0:2], lambda k: T.K1A[:, 4 * k:4 * k + 2], "rk", "lk")
 
     W("v", d_sp)
     t_spf = incs(v.tensor_copy(T.spf[:], T.spi[:]))
+    t_sx0 += [incs(v.memset(T.QS[:, 800:1120], 0))]
     W("t", t_spf, c_r8)
     p_sp = incs(te.matmul(T.pS[:, 0:4], T.R8[:], T.spf[:], True, True))
-    W("t", t_ones, s_cb)
-    te.matmul(T.pN[:, 0:W33], T.ones[:, 0:128], T.CB[:], True, False)
+    W("t", s_bd, s_cb)
+    te.matmul(T.pN[:, 0:W33], T.BD[:], T.CB[:], True, False)
     W("v", d_ql, p_sp)
     t_ge = incs(*[v.tensor_scalar(T.GE[:, 33 * r + 1:33 * r + 33], T.ql[:], T.pS[:, r:r + 1], None, A.is_ge) for r in (1, 2, 3)])
-    W("t", t_ge, s_ge0, t_mk0, c_nl, c_nu)
+    W("t", t_ge, s_ge0, t_mk0, s_bm)
+    te.matmul(T.pN[:, 0:W33], T.BD[:], T.GE[:, 0:132], False, False)
+    te.matmul(T.pN[:, 0:W33], T.BDm[:], T.GE[:, 33:165], False, False)
+    W("t", c_nl)
     te.matmul(T.pN[:, 0:W33], T.NL[:], T.GE[:, 1:133], False, False)
-    te.matmul(T.pN[:, 0:W33], T.NU[:], T.GE[:, 0:132], False, False)
+    te.matmul(T.pN[:, 0:W33], T.NL[:], T.GE[:, 33:165], False, False)
     W("t", s_nl)
     te.matmul(T.pN[:, 0:W33], T.NLm[:], T.GE[:, 34:166], False, False)
-    W("t", s_nm)
-    p_e = incs(te.matmul(T.pN[:, 0:W33], T.NUm[:], T.GE[:, 33:165], False, True))
+    p_e = incs(te.matmul(T.pN[:, 0:W33], T.NLm[:], T.GE[:, 0:132], False, True))
     W("v", t_ge, s_ge0)
     t_mk = incs(v.tensor_tensor(T.MK[:], T.GE[:, 1:133], T.GE[:, 34:166], A.subtract))
     W("v", p_e, s_rst)
@@ -148,90 +191,69 @@ def rank_program(g, core, T, topo):
     t_sl = incs(v.tensor_tensor(T.SL[:], T.F1[:, 0:32], T.F1[:, 33:65], A.add))
     W("v", t_sl)
     t_tt = incs(v.transpose(T.TT[:], T.SL[:]))
-    W("t", t_tt, c_d01)
+    W("t", t_tt, c_d0, c_d1)
     p_a = []
     for w in range(2):
         for gg in range(2):
             sh = 160 * w + 16 + 16 * (w - gg)
             p_a.append(te.matmul(T.pA[:, w:32:2], T.D01[:, sh:sh + 128], T.TT[:, 16 * gg:16 * gg + 16], gg == 0, gg == 1))
     p_a = incs(*p_a[1::2])
-    t_w0 = incs(v.memset(T.WW[:], 0.0))
+    W("v", d_bc)
+    t_bl = incs(v.tensor_scalar(T.BL[:], T.BC[:], 127, None, A.bitwise_and))
     W("v", p_a)
     t_la = incs(v.tensor_copy(T.LA[:], T.pA[:, 0:32]))
-    W("v", t_la, d_x0, d_sx)
-    t_sc = incs(v.tensor_copy(T.SX[:, 0:640].indirect(T.LA[:, 0:32]), T.X0[:]))
+    t_bh = incs(v.tensor_scalar(T.BH[:], T.BC[:], 1, 4032, A.logical_shift_right, A.bitwise_and))
+    W("v", t_la, d_x0, *t_sx0)
+    t_sc = incs(v.tensor_copy(SX.indirect(T.LA[:, 0:32]), T.X0[:]))
+    W("y", t_z0, *z)
+    late = [sy.dma_start(T.W[0::16, 4096:8192], T.kid[:, 4096:8192])]
+    W("y", t_bl)
+    late += [sy.dma_start(T.W[14::16, 4096:8192], T.BL[:])]
+    W("y", t_bh)
+    late += [sy.dma_start(T.W[15::16, 4096:8192], T.BH[:])]
+    d_w.append(incs(*late, n=16))
 
-    def engines_of(src, dst):
-        away = [d for d in T.cores if topo.chip(d) != topo.chip(src)]
-        ae = topo.engines(src, away[0])
-        if dst in away:
-            n = len(ae) // len(away)
-            return ae[away.index(dst) * n:away.index(dst) * n + n]
-        return [e for e in topo.engines(src, dst) if e not in ae][::2]
+    W("t", c_nl, t_ones)
+    p_io = incs(te.matmul(T.p2[:, 0:1], T.NL[:], T.ones[:, 0:1], True, True))
+    W("s", d_b0)
+    s_b0 = incs(s.activation(T.b0f[:], T.b0i[:], F.Copy))
+    W("t", s_b0)
+    p_b0 = incs(te.matmul(T.p1[:, 0:2], T.R8[:], T.b0f[:], True, True))
+    W("s", p_io)
+    s_io = incs(s.activation(T.ioI[:], T.p2[:, 0:1], F.Copy))
+    s_mk = incs(s.activation(T.mk0[:], T.p2[:, 0:1], F.Relu, bias=1.0, scale=-1.0), s.activation(T.mkb[:], T.p2[:, 0:1], F.Relu, bias=-13.0))
+    W("s", s_io, p_b0)
+    s_l16 = incs(s.activation(T.L16[:, 0:1], T.p1[:, 0:1], F.Identity, bias=T.ioI[:, 0:1]))
+    s_w0 = incs(s.activation(T.WW[:, 0:144], T.ones[:, 0:144], F.Copy, scale=0.0), s.activation(T.WW[:, 144:288], T.ones[:, 0:144], F.Copy, scale=0.0))
+    s_al = incs(s.activation(T.alt[:, 0:64:2], T.ones[:, 0:32], F.Copy, scale=0.0), s.activation(T.alt[:, 1:64:2], T.ones[:, 0:32], F.Copy))
+    arrived(s, "rk")
+    W("s", d_k1)
+    s_k1 = incs(s.activation(T.k1f[:], T.K1A[:, 0:16:4], F.Copy))
+    s_lb = None
 
-    def count(r):
-        return len(engines_of(T.cores[r], core))
-
-    def order(x):
-        return sorted([r for r in range(4) if r != x], key=lambda r: topo.chip(T.cores[r]) == topo.chip(T.cores[x]))
-
-    others = order(me)
-
-    def exchange(src, dst, at, to, sem, lsem):
-        tr = []
-        for r in others:
-            d = T.cores[r]
-            a = topo.addr(d)
-            tr.append(RemoteDMATransfer(dst_ids=[DstId(rid=a[0], pnc=a[1])], dma_engine_mask=sum(1 << e for e in engines_of(core, d)),
-                                        remote_sem=T.sem["%s%d" % (sem, me)], src=src[:, CAP * at(r):CAP * at(r) + CAP],
-                                        dst=dst[:, CAP * to(r):CAP * to(r) + CAP]))
-        g.remote_dma_fused(tr, local_sem=T.sem[lsem])
-        return sum(len(engines_of(core, T.cores[r])) for r in others)
+    Wk, Wc = T.WW[:, 0:144], T.WW[:, 144:288]
+    c = sel(T.wt[:, 0:9], T.ones[:, 0:9], [[-16, 9]], A.is_ge, -1, 1, t_ones)
+    c_wc = sel(Wc[:, 15:144:16], T.wt[:, 0:9], [[16, 9]], A.is_ge, 15, -1, c, s_w0)
+    c_wk = sel(Wk[:, 15:144:16], T.ones[:, 0:9], [[-16, 9]], A.is_equal, 0, 1, s_w0)
 
     W("g", t_sc)
-    n_lq = exchange(T.SX, T.QX, lambda r: r, lambda r: order(r).index(me), "rq", "lq")
-
-    def weights(w, n, lo, hi):
-        c = sel(T.wt[:, 16 * n:16 * n + 9], T.ones[:, 0:9], [[-16, 9]], A.is_ge, -lo, 1, t_ones)
-        return sel(w[:, 15:144:16], T.wt[:, 16 * n:16 * n + 9], [[16, 9]], A.is_ge, hi, -1, c, t_w0)
-
-    c_wc = weights(Wc, 0, 1, 15)
-    c_wk = weights(Wk, 1, 0, 1)
-    c_wb = weights(Wb, 2, 2, 3)
-    W("v", d_c)
-    parts = ((512, 768), (0, 512))
-    t_ch = [incs(v.tensor_copy(T.CH[:, a:b], T.C[:, a:b])) for a, b in parts]
-    t_cl = []
-    for (a, b), t in zip(parts, t_ch):
-        W("v", t)
-        t_cl.append(incs(v.tensor_tensor(T.CL[:, a:b], T.C[:, a:b], T.CH[:, a:b], A.subtract)))
-    W("t", *t_ch[:1], *t_cl[:1], c_r0, t_la)
-    te.matmul(T.p1[:, 0:1], T.R0[:], T.CH[:, 512:513], True, False)
-    p_b0 = incs(te.matmul(T.p1[:, 0:1], T.R0[:], T.CL[:, 512:513], False, True))
-    W("y", *t_ch, *z, t_bk0)
-    b1 = [sy.dma_start(T.BK[2::16, 0:4096], T.CH[:, 512:768]), sy.dma_start(T.BK[0::16, :], T.CH[:, 0:512])]
-    W("y", *t_cl)
-    b1 += [sy.dma_start(T.BK[3::16, 0:4096], T.CL[:, 512:768]), sy.dma_start(T.BK[1::16, :], T.CL[:, 0:512])]
-    d_bk = incs(*b1, n=16)
-    d_nb = dmas((sy, T.nks[96:128, :], T.nk[96:128, :]))
-    d_vec = dmas((sy, T.vcs[:], T.vec[:]))
-    W("v", t_sc)
-    t_ox = incs(v.tensor_copy(T.QX[:, 480:640], T.SX[:, CAP * me:CAP * me + CAP]))
-    W("v", d_k1)
-    t_k1 = incs(v.tensor_copy(T.k1f[:], T.k1i[:, 0:1]))
-    W("v", c_pid)
-    t_pim = incs(v.tensor_scalar(T.pim[:], T.pid[:], 15, None, A.bitwise_and))
+    exchange(lambda k: SX[:, CAP * k:CAP * k + CAP], lambda k: T.QS[:, CAP * k - CAP:CAP * k], "rq", "lq")
+    if NK_EARLY < 15:
+        W("y", t_sc)
+        d_w.append(dmas(*[(sy, T.W[o::16, 0:4096], T.nk[o::16, :]) for o in range(NK_EARLY + 1, 16)]))
+    W("v", t_sc, s_k1)
+    t_c1 = incs(*[v.tensor_scalar(T.cm1[:, CAP * k:CAP * k + CAP], SX[:, CAP * k:CAP * k + CAP], T.k1f[:, k:k + 1], None, A.is_ge) for k in range(4)])
+    W("t", c_wc, t_c1, t_ge)
+    p_c1 = incs(conv(T.pS[:, 0:40], Wc, lambda i: T.cm1[:, i:640:16]))
     t_lb = incs(v.tensor_copy(T.LB[:], T.SL[:]))
-    W("v", t_pim)
-    t_io = incs(v.tensor_copy(T.ioI[:], T.pim[:]))
-    W("v", p_b0, t_io)
-    t_l16 = incs(v.tensor_scalar(T.L16[:, 0:1], T.p1[:, 0:1], T.ioI[:, 0:1], None, A.add))
-    c_id = sel(T.ID[:], T.ones[:, 0:128], [[-1, 128]], A.is_equal, 0, 1, t_ones)
-    W("s", c_id)
-    s_i16 = incs(s.activation(T.I16[:], T.ID[:], COPY, scale=16.0))
+    W("v", p_c1)
+    t_l1 = incs(v.tensor_copy(T.l1s[:], T.pS[:, 0:40]))
+    W("g", t_l1)
+    exchange(lambda k: T.l1s[:, 10 * k:10 * k + 10], lambda k: T.l1[:, 10 * k - 10:10 * k], "rl", "ll")
+    W("y", t_l1)
+    d_vec = dmas((sy, T.vcs[:], T.vec[:]))
 
-    B = {"f": (0, 480, 224, (T.pD, T.pT), ((320, 480, tuple(others[2:])), (0, 320, tuple(others[:2])))),
-         "o": (480, 640, 480, (T.pN, T.pA), ((480, 640, ()),))}
+    B = {"f": (0, 480, 256, (T.pD, T.pT), "f"), "o": (480, 640, 480, (T.pN, T.pA), "o")}
     tok = {}
 
     def cols(x, b):
@@ -240,104 +262,105 @@ def rank_program(g, core, T, topo):
     def lst(x, b):
         return x[:, b[0] // 16:b[1] // 16]
 
-    def bank(b, k):
-        return b[3][k % 2][:, 0:(b[1] - b[0]) // 16]
+    def bank(b, k, n=1):
+        return b[3][k % 2][:, 0:n * (b[1] - b[0]) // 16]
 
-    def c1(b):
-        W("v", t_k1, t_ox)
-        c = []
-        for lo, hi, those in b[4]:
-            for r in those:
-                v.wait_ge(T.sem["rq%d" % r], count(r))
-            c.append(v.tensor_scalar(T.cm1[:, lo:hi], T.QX[:, lo:hi], T.k1f[:, 0:1], None, A.is_ge))
-        tok["c1", b] = incs(*c)
-        W("t", c_wc, t_la, tok["c1", b])
-        tok["p1", b] = incs(conv(bank(b, 0), Wc, cols(T.cm1, b), b[1] - b[0]))
-
-    def lists(b, pn, name, k):
+    def lists(b, pn, name, k, add=0.0):
         W("v", tok[pn, b])
-        tok[name, b] = incs(v.tensor_copy(lst(T[name], b), bank(b, k)))
+        tok[name, b] = incs(v.tensor_scalar(lst(T[name], b), bank(b, k), add, None, A.add))
+
+    def sums(b, pn, name, k, sm):
+        n = (b[1] - b[0]) // 8
+        W("v", tok[pn, b], s_al)
+        x = sm[:, b[0] // 8:b[1] // 8]
+        c = incs(v.tensor_tensor_scan(x, T.alt[:, 0:n], bank(b, k, 2), 0.0, A.mult, A.add))
+        W("v", c)
+        tok[name, b] = incs(v.tensor_copy(lst(T[name], b), x[:, 1:n:2]))
 
     def c2(b):
-        W("v", tok["l1", b], tok["K2"])
-        tok["c2", b] = incs(v.tensor_tensor(cols(T.cm2, b), T.K2[:, 0:16].indirect(lst(T.l1, b)), cols(T.QX, b), A.is_le))
-        tok["lb", b] = incs(v.tensor_copy(lst(T.l1b, b), bank(b, 0)))
-        W("t", tok["c2", b])
-        conv(bank(b, 1), Wc, cols(T.cm2, b), b[1] - b[0], True, False)
-        W("t", tok["lb", b], s_i16)
-        tok["p2", b] = incs(te.matmul(bank(b, 1), T.I16[:], lst(T.l1b, b), False, True))
+        l1 = T.l1[:, 0:30] if b[4] == "f" else T.l1s[:, 0:10]
+        W("v", t_l1, tok["K2"])
+        if b[4] == "f":
+            arrived(v, "rq")
+            arrived(v, "rl")
+        tok["c2", b] = incs(v.tensor_tensor(cols(T.cm2, b), T.K2[:, 0:16].indirect(l1), cols(T.QS, b), A.is_le))
+        tok["lb", b] = incs(v.tensor_scalar(lst(T.l1b, b), l1, 16.0, None, A.mult))
+        W("t", tok["c2", b], t_la, t_val)
+        conv(bank(b, 1), Wc, lambda i: T.cm2[:, b[0] + i:b[1]:16], True, False)
+        W("t", tok["lb", b])
+        te.matmul(bank(b, 1), T.D01[:, 16:144], lst(T.l1b, b), False, False)
+        tok["p2", b] = incs(te.matmul(bank(b, 1), T.D01[:, 176:304], lst(T.l1b, b), False, True))
 
-    def level(b, lin, win, nodes, bg, cm, pn, k, *deps):
+    def level(b, lin, win, scale, nodes, Z, pn, k, *deps):
         W("s", tok[lin, b], *deps[:1])
-        tok["b" + pn, b] = incs(s.activation(cols(bg, b), win.indirect(lst(T[lin], b)), COPY))
+        x = incs(s.activation(Z[:, :, 1], win.indirect(lst(T[lin], b)), F.Copy, scale=scale))
         W("v", tok[lin, b], *deps[1:])
-        tok["c" + pn, b] = incs(v.tensor_tensor(cols(cm, b), nodes.indirect(lst(T[lin], b)), cols(T.QX, b), A.is_le))
-        W("t", c_wb, tok["b" + pn, b])
-        conv(bank(b, k), Wb, cols(bg, b), b[1] - b[0], True, False)
-        W("t", tok["c" + pn, b])
-        tok[pn, b] = incs(conv(bank(b, k), Wc, cols(cm, b), b[1] - b[0], False, True))
+        y = incs(v.tensor_tensor(Z[:, :, 0], nodes.indirect(lst(T[lin], b)), cols(T.QS, b), A.is_le))
+        W("t", x, y)
+        tok[pn, b] = incs(conv(bank(b, k, 2), Wc, lambda i: Z[:, i::16, :]))
 
-    def shared(b, win, lin, out, at, *deps):
+    def kid_s(out, l):
+        return s.activation(out, T.W[:, 0:8192].indirect(l), F.Copy, bias=-HALF, scale=T.mk0[:, 0:1])
+
+    def shared(b, lin, out, on_s, on_v, *deps):
         a = []
         for key, lo, hi in (("s", b[2], b[1]), ("v", b[0], b[2])):
             if lo < hi:
                 W(key, tok[lin, b], *deps)
-                x, y = out[:, lo - at:hi - at], win.indirect(T[lin][:, lo // 16:hi // 16])
-                a.append(incs(s.activation(x, y, COPY) if key == "s" else v.tensor_copy(x, y)))
+                a.append(incs((on_s if key == "s" else on_v)(out[:, lo:hi], T[lin][:, lo // 16:hi // 16])))
         return a
 
     def kids(b, lin, kg, pn, k):
-        W("t", c_wk, *shared(b, T.BK[:, 0:8192], lin, kg, 0))
-        tok[pn, b] = incs(conv(bank(b, k), Wk, cols(kg, b), b[1] - b[0]))
+        W("t", c_wk, *shared(b, lin, kg, kid_s, lambda x, l: v.tensor_scalar(x, T.W[:, 0:8192].indirect(l), T.mk0[:, 0:1], -HALF, A.mult, A.add), s_mk))
+        tok[pn, b] = incs(conv(bank(b, k), Wk, lambda i: kg[:, b[0] + i:b[1]:16]))
 
     def vectors(b):
-        own = b is B["o"]
-        tok["ve", b] = shared(b, T.vcs[:, 0:4096], "vn", T.RX[:, CAP * me:CAP * me + CAP] if own else T.AN, b[0] if own else 0, d_vec)
+        win = T.vcs[:, 0:4096]
+        tok["ve", b] = shared(b, "vn", T.AR, lambda x, l: s.activation(x, win.indirect(l), F.Copy), lambda x, l: v.tensor_copy(x, win.indirect(l)), d_vec)
 
-    steps = {"c1": c1, "l1": lambda b: lists(b, "p1", "l1", 0), "c2": c2, "l2": lambda b: lists(b, "p2", "l2", 1),
-             "L3": lambda b: level(b, "l2", T.b3w[:, 0:256], T.K3[:, 0:256], T.bg3, T.cm3, "p3", 2, tok["b3"], tok["K3"]),
-             "i3": lambda b: lists(b, "p3", "i3", 2), "k3": lambda b: kids(b, "i3", T.kg3, "p4", 3),
-             "m4": lambda b: lists(b, "p4", "m4", 3),
-             "L4": lambda b: level(b, "m4", T.BK[:, 0:4096], T.nks[:, 0:4096], T.bg4, T.cm4, "p5", 4),
-             "i4": lambda b: lists(b, "p5", "i4", 4), "k4": lambda b: kids(b, "i4", T.kg4, "p6", 5),
-             "vn": lambda b: lists(b, "p6", "vn", 5), "ve": vectors}
+    steps = {"c2": c2, "l2": lambda b: lists(b, "p2", "l2", 1),
+             "L3": lambda b: level(b, "l2", T.b3w[:, 0:256], 1.0, T.K3[:, 0:256], T["Z3" + b[4]], "p3", 2, tok["b3"], tok["K3"]),
+             "i3": lambda b: sums(b, "p3", "i3", 2, T.sm3), "k3": lambda b: kids(b, "i3", T.kg3, "p4", 3),
+             "m4": lambda b: lists(b, "p4", "m4", 3, HALF),
+             "L4": lambda b: level(b, "m4", T.W[:, 4096:8192], T.mkb[:, 0:1], T.W[:, 0:4096], T["Z4" + b[4]], "p5", 4),
+             "i4": lambda b: sums(b, "p5", "i4", 4, T.sm4), "k4": lambda b: kids(b, "i4", T.kg4, "p6", 5),
+             "vn": lambda b: lists(b, "p6", "vn", 5, HALF), "ve": vectors}
 
     def table(x):
         if x == "a":
-            W("s", t_l16, d_bk)
-            c = incs(s.activation(T.kg16[:], T.BK[:, 0:8192].indirect(T.L16[:, 0:1]), COPY))
+            W("s", s_l16, s_mk, *d_w)
+            c = incs(kid_s(T.kg16[:], T.L16[:, 0:1]))
             W("t", c, c_wk)
-            tok["p_m2"] = incs(conv(T.p2[:, 0:1], Wk, T.kg16, 16))
+            tok["p_m2"] = incs(conv(T.p2[:, 0:1], Wk, lambda i: T.kg16[:, i:i + 1]))
         if x == "b":
-            W("v", tok["p_m2"])
-            tok["LM2"] = incs(v.tensor_copy(T.LM2[:, 0:1], T.p2[:, 0:1]))
+            W("s", tok["p_m2"])
+            tok["LM2"] = incs(s.activation(T.LM2[:, 0:1], T.p2[:, 0:1], F.Copy, bias=HALF))
             W("s", tok["LM2"])
-            c = incs(s.activation(T.b2[:], T.BK[:, 0:4096].indirect(T.LM2[:, 0:1]), COPY))
-            W("t", c, t_l16, c_rb)
-            tok["p_b2"] = incs(te.matmul(T.p1[:, 0:16], T.RB[:], T.b2[:], True, True))
-            W("v", d_na, d_nb, tok["LM2"])
-            tok["K2"] = incs(v.tensor_copy(T.K2[:], T.nks[:, 0:4096].indirect(T.LM2[:, 0:1])))
+            c = incs(s.activation(T.b2[:], T.W[:, 4096:8192].indirect(T.LM2[:, 0:1]), F.Copy, scale=T.mkb[:, 0:1]))
+            W("t", c)
+            tok["p_b2"] = incs(te.matmul(T.p1[:, 0:16], T.BD[:], T.b2[:], True, True))
+            W("v", tok["LM2"], *d_w)
+            tok["K2"] = incs(v.tensor_copy(T.K2[:], T.W[:, 0:4096].indirect(T.LM2[:, 0:1])))
         if x == "c":
-            W("v", tok["p_b2"])
-            c = incs(v.tensor_scalar(T.L256[:], T.p1[:, 0:16], T.ioI[:, 0:1], None, A.add))
+            W("s", tok["p_b2"])
+            c = incs(s.activation(T.L256[:], T.p1[:, 0:16], F.Identity, bias=T.ioI[:, 0:1]))
             W("s", c)
-            c = incs(s.activation(T.kg256[:], T.BK[:, 0:8192].indirect(T.L256[:, 0:16]), COPY))
-            W("t", c, tok["LM2"])
-            tok["p_m3"] = incs(conv(T.p2[:, 0:16], Wk, T.kg256, 256))
+            c = incs(kid_s(T.kg256[:], T.L256[:, 0:16]))
+            W("t", c)
+            tok["p_m3"] = incs(conv(T.p2[:, 0:16], Wk, lambda i: T.kg256[:, i:256:16]))
         if x == "d":
-            W("v", tok["p_m3"])
-            tok["LM3"] = incs(v.tensor_copy(T.LM3[:], T.p2[:, 0:16]))
+            W("s", tok["p_m3"])
+            tok["LM3"] = incs(s.activation(T.LM3[:], T.p2[:, 0:16], F.Copy, bias=HALF))
             W("s", tok["LM3"])
-            tok["b3"] = incs(s.activation(T.b3w[:], T.BK[:, 0:4096].indirect(T.LM3[:, 0:16]), COPY))
+            tok["b3"] = incs(s.activation(T.b3w[:], T.W[:, 4096:8192].indirect(T.LM3[:, 0:16]), F.Copy, scale=T.mkb[:, 0:1]))
         if x == "e":
             W("v", tok["LM3"])
-            tok["K3"] = incs(v.tensor_copy(T.K3[:], T.nks[:, 0:4096].indirect(T.LM3[:, 0:16])))
+            tok["K3"] = incs(v.tensor_copy(T.K3[:], T.W[:, 0:4096].indirect(T.LM3[:, 0:16])))
 
-    n_la = 0
     for x in PLAN.split():
         if x == "send":
             W("g", *tok["ve", B["f"]])
-            n_la = exchange(T.AN, T.RX, lambda r: others.index(r), lambda r: me, "ra", "la")
+            exchange(lambda k: T.AR[:, CAP * k - CAP:CAP * k], lambda k: RX[:, CAP * k:CAP * k + CAP], "ra", "la")
         elif x[0] == "T":
             table(x[1])
         else:
@@ -345,17 +368,16 @@ def rank_program(g, core, T, topo):
 
     W("v", t_lb, *tok["ve", B["o"]])
     W("s", t_lb, *tok["ve", B["o"]])
-    for r in others:
-        v.wait_ge(T.sem["ra%d" % r], count(r))
-        s.wait_ge(T.sem["ra%d" % r], count(r))
-    t_y = incs(v.tensor_copy(T.yb[:, 0:256], T.RX[:, 0:640].indirect(T.LB[:, 0:16])))
-    s_y = incs(s.activation(T.yb[:, 256:512], T.RX[:, 0:640].indirect(T.LB[:, 16:32]), COPY))
+    arrived(v, "ra")
+    arrived(s, "ra")
+    t_y = incs(v.tensor_copy(T.yb[:, 0:256], RX.indirect(T.LB[:, 0:16])))
+    s_y = incs(s.activation(T.yb[:, 256:512], RX.indirect(T.LB[:, 16:32]), F.Copy))
     W("y", t_y)
     d_y0 = dmas((sy, T.y[:, 0:256], T.yb[:, 0:256]))
     W("s", s_y)
     d_y1 = dmas((s, T.y[:, 256:512], T.yb[:, 256:512]))
     W("y", d_y0)
     W("s", d_y1)
-    g.wait_ge(T.sem.lq, n_lq)
-    g.wait_ge(T.sem.la, n_la)
+    for name, n in sent:
+        g.wait_ge(T.sem[name], n)
     W("g", *[t for t in every if t not in waited])

@@ -2,7 +2,7 @@ from concourse.bass import DstId, RemoteDMATransfer
 from concourse.mybir import dt, AluOpType, AxisListType, ActivationFunctionType
 
 CAP = 160
-NS = 128
+NS = 144
 W33 = 132
 HALF = 2048.0
 
@@ -11,34 +11,37 @@ SCRATCH = {
     "spf": ("sbuf", [8, 4], "float32"),
     "b0i": ("sbuf", [8, 2], "int32"),
     "b0f": ("sbuf", [8, 2], "float32"),
-    "onef": ("sbuf", [8, 128], "float32"),
+    "R8b": ("sbuf", [8, 128], "bfloat16"),
     "R8": ("sbuf", [8, 128], "float32"),
-    "Z3f": ("sbuf", [128, 480, 2], "bfloat16"),
-    "Z4f": ("sbuf", [128, 480, 2], "bfloat16"),
-    "Z3o": ("sbuf", [128, 160, 2], "bfloat16"),
-    "Z4o": ("sbuf", [128, 160, 2], "bfloat16"),
+    "Z3o": ("sbuf", [128, 128, 2], "float16"),
+    "Z4o": ("sbuf", [128, 128, 2], "float16"),
 }
 for _dt, _bufs in (
-    ("int32", "ql 32 X0 512 W 8192 BC 256 BH 256 BL 256 K1A 16 QS 1120 K2 16 K3 256"),
-    ("float32", "k1f 4 ioI 1 mk0 1 mkb 1 sm3 80 sm4 80"),
+    ("int32", "ql 32 X0 512 W 8208 k1i 2 QS 1120 K2 16 K3 256 b3w 256 sm3 80 sm4 80"),
+    ("float32", "K1A 16 kgx 128 onef 1 e0 1 ioI 1 ioB 1 mk0 1 mku 1 mkb 1 mkt 1 bib 1"),
     ("bfloat16", "vcs 4096 ones 160 BD 128 BDm 128 NL 128 NLm 128 CB 132 RST 132 alt 64 "
-                 "D01 320 wt 16 WW 288 GE 176 MK 132 b2 16 b3w 256 cm1 640 cm2 640 l1b 40 AR 1120 yb 512"),
-    ("float16", "VAL 132 F1 66 SL 32 TT 32 kg16 16 kg256 256 kg3 640 kg4 640"),
-    ("uint16", "LA 32 LB 32 L16 2 LM2 2 L256 16 LM3 16 l1s 40 l1 32 l2 40 i3 40 m4 40 i4 40 vn 40"),
+                 "D01 320 WW 288 W16 144 GE 176 MK 132 wt 16 cm1 640 cm2 640 l1b 40 AR 1120 yb 512"),
+    ("float16", "VAL 132 F1 66 SL 32 TT 32 b2 16 Z3f 1024 Z4f 1024 kg256 256 G3 640 G4 640"),
+    ("uint16", "LA 32 LB 32 L16 8 LM2 2 L256 16 LM3 16 l1s 40 l1 32 l2 40 i3 40 m4 40 i4 40 vn 40"),
 ):
     _w = _bufs.split()
     for _k in range(0, len(_w), 2):
         SCRATCH[_w[_k]] = ("sbuf", [128, int(_w[_k + 1])], _dt)
 for _k in "pS pT pN pA p1 p2 pB pD".split():
     SCRATCH[_k] = ("psum", [128, 512], "float32")
-SEMAPHORES = ["s%d" % i for i in range(NS)] + ["%s%d" % (x, i) for x in ("rk", "rq", "rl", "ra") for i in range(4)] + ["lk", "lq", "ll", "la"]
+SEMAPHORES = ["s%d" % i for i in range(NS)] + ["rk", "rq", "rl", "ra", "left"]
 
 A = AluOpType
 F = ActivationFunctionType
 
-PLAN = """Ta Tb Tc c2f Td Te l2f L3f c2o i3f k3f l2o L3o m4f L4f i3o k3o i4f k4f m4o L4o vnf vef send
- i4o k4o vno veo"""
+PLAN = """Ta Tb c2o Tc c2f l2o Td Te l2f L3f L3o i3f k3f i3o k3o m4f L4f m4o L4o i4f k4f i4o k4o vnf vef send
+ vno veo"""
+CUT_L = (0, 8, 13, 16)
+CUT_K = (0, 6, 12, 16)
+SHARE = {}
 NK_EARLY = 15
+MID = 6656
+FILL_V = 256
 
 
 def rank_program(g, core, T, topo):
@@ -52,12 +55,12 @@ def rank_program(g, core, T, topo):
     waited = {}
     every = []
 
-    def incs(*ins, n=1):
-        name = "s%d" % used[0]
-        used[0] += 1
+    def incs(*ins, n=1, on=None):
+        name, base = on or ("s%d" % used[0], 0)
+        used[0] += on is None
         for x in ins:
             x.then_inc(T.sem[name], n)
-        tok = (name, n * len(ins))
+        tok = (name, base + n * len(ins))
         every.append(tok)
         return tok
 
@@ -72,9 +75,10 @@ def rank_program(g, core, T, topo):
             waited[tok] = True
             queues[key].wait_ge(T.sem[tok[0]], tok[1])
 
-    def conv(out, wt, src, start=True, stop=True):
+    def conv(out, wt, src, start=True, stop=True, before=lambda i: (), turn=range(16)):
         ins = None
-        for i in range(16):
+        for i in turn:
+            W("t", *before(i))
             ins = te.matmul(out, wt[:, 15 - i:143 - i], src(i), start and i == 0, stop and i == 15)
         return ins
 
@@ -84,93 +88,91 @@ def rank_program(g, core, T, topo):
     others = order(me)
     place = {r: k for k, r in enumerate([me] + others)}
 
-    def engines_of(src, dst):
+    def engines_of(src, dst, sem):
         away = [d for d in T.cores if topo.chip(d) != topo.chip(src)]
         ae = topo.engines(src, away[0])
         if dst in away:
             n = len(ae) // len(away)
-            return ae[away.index(dst) * n:away.index(dst) * n + n]
+            return ae[away.index(dst) * n:away.index(dst) * n + n][SHARE.get(sem, slice(None))]
         return [e for e in topo.engines(src, dst) if e not in ae][::2]
 
     def arrived(q, sem):
-        for r in others:
-            q.wait_ge(T.sem["%s%d" % (sem, r)], len(engines_of(T.cores[r], core)))
+        q.wait_ge(T.sem[sem], sum(len(engines_of(T.cores[r], core, sem)) for r in others))
 
     sent = []
 
-    def exchange(src, dst, sem, lsem):
+    def exchange(src, dst, sem):
         tr = []
         for r in others:
             d = T.cores[r]
             a = topo.addr(d)
-            tr.append(RemoteDMATransfer(dst_ids=[DstId(rid=a[0], pnc=a[1])], dma_engine_mask=sum(1 << e for e in engines_of(core, d)),
-                                        remote_sem=T.sem["%s%d" % (sem, me)], src=src(place[r]), dst=dst(1 + order(r).index(me))))
-        g.remote_dma_fused(tr, local_sem=T.sem[lsem])
-        sent.append((lsem, sum(len(engines_of(core, T.cores[r])) for r in others)))
+            tr.append(RemoteDMATransfer(dst_ids=[DstId(rid=a[0], pnc=a[1])], dma_engine_mask=sum(1 << e for e in engines_of(core, d, sem)),
+                                        remote_sem=T.sem[sem], src=src(place[r]), dst=dst(1 + order(r).index(me))))
+        g.remote_dma_fused(tr, local_sem=T.sem.left)
+        sent.append(sum(len(engines_of(core, T.cores[r], sem)) for r in others))
 
     SX = T.QS[:, 480:1120]
     RX = T.AR[:, 480:1120]
 
-    d_ql = dmas((sy, T.ql[:], T.q[:]))
     d_sp = dmas((s, T.spi[:], T.spl[:]))
-    d_k1 = dmas((sy, T.K1A[:, 0:2], T.nk[:, 0:2]))
-    d_b0 = dmas((s, T.b0i[:], T.beg[:, 0:2]))
-    d_bc = dmas((s, T.BC[:], T.beg[:]))
+    d_ql = dmas((sy, T.ql[:], T.q[:]))
+    d_k1 = dmas((sy, T.k1i[:], T.nk[:, 0:2]))
     d_x0 = dmas(*[((sy, sy, sy, s)[o % 4], T.X0[o::16, :], T.q[:]) for o in range(16)])
+    d_b0 = dmas((sy, T.b0i[:], T.beg[:, 0:2]))
     d_w = [dmas((sy, T.W[0::16, 0:4096], T.kid[:, 0:4096]), *[(sy, T.W[o::16, 0:4096], T.nk[o::16, :]) for o in range(1, NK_EARLY + 1)])]
 
-    t_onef = incs(v.memset(T.onef[:], 1.0))
     t_ones = incs(v.memset(T.ones[:], 1.0))
     t_cb0 = incs(v.memset(T.CB[:], 0.0))
     t_rs0 = incs(v.memset(T.RST[:], 1.0))
-    t_z0 = incs(v.memset(T.W[:, 4096:4608], 0))
-    t_mk0 = incs(v.memset(T.GE[:, 0:1], 0.0))
-    t_sx0 = [incs(v.memset(T.QS[:, 480:800], 0))]
+    t_mk0 = incs(v.memset(T.GE[:], 0.0))
+    t_z0 = incs(v.memset(T.W[:, 7680:8208], 0))
+    t_sx0 = [incs(v.memset(T.QS[:, 480:864], 0))]
 
     def fill(a, b):
-        return incs(s.activation(T.W[:, a:b], T.W[:, 4096:4096 + b - a], F.Copy))
+        return incs(*[s.activation(T.W[:, c:min(b, c + 512)], T.W[:, 7680:7680 + min(b, c + 512) - c], F.Copy) for c in range(a, b, 512)])
 
     def sel(out, in_, pattern, op, base, cm, *deps):
         W("g", *deps)
         return incs(g.affine_select(out, in_, pattern, op, 0.0, base, cm))
 
-    c_r8 = sel(T.R8[:], T.onef[:], [[-1, 8], [0, 16]], A.is_equal, 0, 1, t_onef)
-    W("t", c_r8)
-    p_bd = incs(te.matmul(T.pB[:, 0:128], T.R8[:], T.R8[:], True, True))
+    c_rb = sel(T.R8b[:], T.ones[0:8, 0:128], [[-1, 8], [0, 16]], A.is_equal, 0, 1, t_ones)
+    W("t", c_rb)
+    p_bd = incs(te.matmul(T.pB[:, 0:128], T.R8b[:], T.R8b[:], True, True))
     W("s", t_ones, t_cb0)
     s_cb = incs(*[s.activation(T.CB[:, 33 * r:33 * r + 1], T.ones[:, 0:1], F.Copy, scale=CAP / 16 * place[r]) for r in others])
     W("s", t_rs0)
     s_rst = incs(s.activation(T.RST[:, 0:132:33], T.ones[:, 0:4], F.Copy, scale=0.0))
-    s_ge0 = incs(s.activation(T.GE[:, 33:166:33], T.ones[:, 0:5], F.Copy, scale=0.0), s.activation(T.GE[:, 1:33], T.ones[:, 0:32], F.Copy),
-                 s.activation(T.GE[:, 133:165], T.ones[:, 0:32], F.Copy, scale=0.0))
+    W("s", t_mk0)
+    s_ge0 = incs(s.activation(T.GE[:, 1:33], T.ones[:, 0:32], F.Copy))
+    W("s", c_rb)
+    c_r8 = incs(s.activation(T.R8[:], T.R8b[:], F.Copy))
     W("s", p_bd)
     s_bd = incs(s.activation(T.BD[:], T.pB[:, 0:128], F.Copy))
     s_bm = incs(s.activation(T.BDm[:], T.pB[:, 0:128], F.Copy, scale=-1.0))
     W("s", t_z0)
-    z = [fill(4608, 4864)]
+    z = [fill(4096, 4544)]
     c_d0 = sel(T.D01[:, 0:160], T.ones[:], [[-32, 5], [-1000, 2], [-1, 16]], A.is_equal, 1000, 1, t_ones)
     c_nl = sel(T.NL[:], T.BD[:], [[1, 128]], A.is_gt, 0, -1, s_bd)
-    c_d1 = sel(T.D01[:, 160:320], T.ones[:], [[-32, 5], [-1000, 2], [-1, 16]], A.is_equal, 16, 1, t_ones)
     W("s", c_nl)
     s_nl = incs(s.activation(T.NLm[:], T.NL[:], F.Copy, scale=-1.0))
-    W("s", z[0])
-    z += [fill(4864, 5632)]
-    W("s", z[1])
-    z += [fill(5632, 7168), fill(7168, 8192)]
+    z += [fill(4544, MID), fill(MID, 7680 - FILL_V)]
 
-    W("g", d_k1)
-    exchange(lambda k: T.K1A[:, 0:2], lambda k: T.K1A[:, 4 * k:4 * k + 2], "rk", "lk")
 
     W("v", d_sp)
     t_spf = incs(v.tensor_copy(T.spf[:], T.spi[:]))
-    t_sx0 += [incs(v.memset(T.QS[:, 800:1120], 0))]
+    t_sx0 += [incs(v.memset(T.QS[:, 864:1120], 0))]
+    W("v", d_k1)
+    t_k1 = incs(v.tensor_copy(T.K1A[:, 0:2], T.k1i[:]))
+    c_d1 = sel(T.D01[:, 160:320], T.ones[:], [[-32, 5], [-1000, 2], [-1, 16]], A.is_equal, 16, 1, t_ones)
+    W("g", t_k1)
+    exchange(lambda k: T.K1A[:, 0:2], lambda k: T.K1A[:, 4 * k:4 * k + 2], "rk")
     W("t", t_spf, c_r8)
     p_sp = incs(te.matmul(T.pS[:, 0:4], T.R8[:], T.spf[:], True, True))
     W("t", s_bd, s_cb)
     te.matmul(T.pN[:, 0:W33], T.BD[:], T.CB[:], True, False)
-    W("v", d_ql, p_sp)
+    W("v", d_ql, p_sp, t_mk0)
     t_ge = incs(*[v.tensor_scalar(T.GE[:, 33 * r + 1:33 * r + 33], T.ql[:], T.pS[:, r:r + 1], None, A.is_ge) for r in (1, 2, 3)])
-    W("t", t_ge, s_ge0, t_mk0, s_bm)
+    W("t", t_ge, s_ge0, s_bm)
     te.matmul(T.pN[:, 0:W33], T.BD[:], T.GE[:, 0:132], False, False)
     te.matmul(T.pN[:, 0:W33], T.BDm[:], T.GE[:, 33:165], False, False)
     W("t", c_nl)
@@ -181,6 +183,11 @@ def rank_program(g, core, T, topo):
     p_e = incs(te.matmul(T.pN[:, 0:W33], T.NLm[:], T.GE[:, 0:132], False, True))
     W("v", t_ge, s_ge0)
     t_mk = incs(v.tensor_tensor(T.MK[:], T.GE[:, 1:133], T.GE[:, 34:166], A.subtract))
+    t_w0 = incs(v.memset(T.WW[:], 0.0))
+    Wk, Wc = T.WW[:, 0:144], T.WW[:, 144:288]
+    c = sel(T.wt[:, 0:9], T.ones[:, 0:9], [[-16, 9]], A.is_ge, -1, 1)
+    c_wc = sel(Wc[:, 15:144:16], T.wt[:, 0:9], [[16, 9]], A.is_ge, 15, -1, c, t_w0)
+    c_wk = sel(Wk[:, 15:144:16], T.ones[:, 0:9], [[-16, 9]], A.is_equal, 0, 1)
     W("v", p_e, s_rst)
     t_u = incs(v.tensor_tensor_scan(T.pT[:, 0:W33], T.RST[:], T.pN[:, 0:W33], 0.0, A.mult, A.add))
     W("v", t_u, t_mk)
@@ -198,20 +205,16 @@ def rank_program(g, core, T, topo):
             sh = 160 * w + 16 + 16 * (w - gg)
             p_a.append(te.matmul(T.pA[:, w:32:2], T.D01[:, sh:sh + 128], T.TT[:, 16 * gg:16 * gg + 16], gg == 0, gg == 1))
     p_a = incs(*p_a[1::2])
-    W("v", d_bc)
-    t_bl = incs(v.tensor_scalar(T.BL[:], T.BC[:], 127, None, A.bitwise_and))
+    z.append(incs(v.memset(T.W[:, 7680 - FILL_V:7680], 0)))
     W("v", p_a)
     t_la = incs(v.tensor_copy(T.LA[:], T.pA[:, 0:32]))
-    t_bh = incs(v.tensor_scalar(T.BH[:], T.BC[:], 1, 4032, A.logical_shift_right, A.bitwise_and))
     W("v", t_la, d_x0, *t_sx0)
     t_sc = incs(v.tensor_copy(SX.indirect(T.LA[:, 0:32]), T.X0[:]))
-    W("y", t_z0, *z)
-    late = [sy.dma_start(T.W[0::16, 4096:8192], T.kid[:, 4096:8192])]
-    W("y", t_bl)
-    late += [sy.dma_start(T.W[14::16, 4096:8192], T.BL[:])]
-    W("y", t_bh)
-    late += [sy.dma_start(T.W[15::16, 4096:8192], T.BH[:])]
-    d_w.append(incs(*late, n=16))
+    late = []
+    for (a, b), fills in (((4096, MID), z[:2]), ((MID, 8192), z)):
+        W("y", t_z0, *fills)
+        late += [(sy, T.W[0::16, a:b], T.kid[:, a:b])] + [(sy, T.W[o::16, a:b], T.beg[:, a - 4096:b - 4096]) for o in (14, 15)]
+        d_w.append(dmas(*late[-3:]))
 
     W("t", c_nl, t_ones)
     p_io = incs(te.matmul(T.p2[:, 0:1], T.NL[:], T.ones[:, 0:1], True, True))
@@ -220,40 +223,39 @@ def rank_program(g, core, T, topo):
     W("t", s_b0)
     p_b0 = incs(te.matmul(T.p1[:, 0:2], T.R8[:], T.b0f[:], True, True))
     W("s", p_io)
-    s_io = incs(s.activation(T.ioI[:], T.p2[:, 0:1], F.Copy))
-    s_mk = incs(s.activation(T.mk0[:], T.p2[:, 0:1], F.Relu, bias=1.0, scale=-1.0), s.activation(T.mkb[:], T.p2[:, 0:1], F.Relu, bias=-13.0))
+    s_io = incs(s.activation(T.ioI[:], T.p2[:, 0:1], F.Copy, bias=-8192.0), s.activation(T.onef[:], T.ones[:, 0:1], F.Copy))
+    c = incs(s.activation(T.mku[:], T.p2[:, 0:1], F.Relu, bias=14.0, scale=-1.0), s.activation(T.mkt[:], T.p2[:, 0:1], F.Copy, bias=-4110.5),
+             s.activation(T.ioB[:], T.p2[:, 0:1], F.Copy, bias=2 * HALF))
+    s_mk = incs(s.activation(T.mk0[:], T.p2[:, 0:1], F.Relu, bias=1.0, scale=-1.0))
+    W("s", c)
+    c = incs(s.activation(T.mkb[:], T.mku[:], F.Relu, bias=0.5, scale=-1.0), on=c)
+    W("s", c)
+    s_bi = incs(s.activation(T.bib[:], T.mkt[:], F.Copy, scale=T.mkb[:, 0:1]), on=c)
     W("s", s_io, p_b0)
-    s_l16 = incs(s.activation(T.L16[:, 0:1], T.p1[:, 0:1], F.Identity, bias=T.ioI[:, 0:1]))
-    s_w0 = incs(s.activation(T.WW[:, 0:144], T.ones[:, 0:144], F.Copy, scale=0.0), s.activation(T.WW[:, 144:288], T.ones[:, 0:144], F.Copy, scale=0.0))
+    c = incs(s.activation(T.e0[:], T.p1[:, 0:1], F.Identity, bias=T.ioI[:, 0:1]))
+    W("s", c)
+    s_l16 = incs(s.activation(T.L16[:], T.BD[:, 0:128:16], F.Copy, bias=8192.0, scale=T.e0[:, 0:1]), on=c)
+    W("s", c_wc, t_sl)
+    s_16 = incs(s.activation(T.W16[:], Wc, F.Copy, scale=16.0))
+    s_lb = incs(s.activation(T.LB[:], T.SL[:], F.Copy))
     s_al = incs(s.activation(T.alt[:, 0:64:2], T.ones[:, 0:32], F.Copy, scale=0.0), s.activation(T.alt[:, 1:64:2], T.ones[:, 0:32], F.Copy))
-    arrived(s, "rk")
-    W("s", d_k1)
-    s_k1 = incs(s.activation(T.k1f[:], T.K1A[:, 0:16:4], F.Copy))
-    s_lb = None
-
-    Wk, Wc = T.WW[:, 0:144], T.WW[:, 144:288]
-    c = sel(T.wt[:, 0:9], T.ones[:, 0:9], [[-16, 9]], A.is_ge, -1, 1, t_ones)
-    c_wc = sel(Wc[:, 15:144:16], T.wt[:, 0:9], [[16, 9]], A.is_ge, 15, -1, c, s_w0)
-    c_wk = sel(Wk[:, 15:144:16], T.ones[:, 0:9], [[-16, 9]], A.is_equal, 0, 1, s_w0)
 
     W("g", t_sc)
-    exchange(lambda k: SX[:, CAP * k:CAP * k + CAP], lambda k: T.QS[:, CAP * k - CAP:CAP * k], "rq", "lq")
-    if NK_EARLY < 15:
-        W("y", t_sc)
-        d_w.append(dmas(*[(sy, T.W[o::16, 0:4096], T.nk[o::16, :]) for o in range(NK_EARLY + 1, 16)]))
-    W("v", t_sc, s_k1)
-    t_c1 = incs(*[v.tensor_scalar(T.cm1[:, CAP * k:CAP * k + CAP], SX[:, CAP * k:CAP * k + CAP], T.k1f[:, k:k + 1], None, A.is_ge) for k in range(4)])
-    W("t", c_wc, t_c1, t_ge)
-    p_c1 = incs(conv(T.pS[:, 0:40], Wc, lambda i: T.cm1[:, i:640:16]))
-    t_lb = incs(v.tensor_copy(T.LB[:], T.SL[:]))
+    exchange(lambda k: SX[:, CAP * k:CAP * k + CAP], lambda k: T.QS[:, CAP * k - CAP:CAP * k], "rq")
+    W("v", t_sc)
+    arrived(v, "rk")
+    t_c1 = [incs(*[v.tensor_scalar(T.cm1[:, CAP * k + u:CAP * k + CAP:2], SX[:, CAP * k + u:CAP * k + CAP:2], T.K1A[:, 4 * k:4 * k + 1], None, A.is_ge)
+                   for k in range(4)]) for u in range(2)]
+    W("t", c_wc, t_ge)
+    p_c1 = incs(conv(T.pS[:, 0:40], Wc, lambda i: T.cm1[:, i:640:16], before=lambda i: [t_c1[i % 2]], turn=[*range(0, 16, 2), *range(1, 16, 2)]))
     W("v", p_c1)
-    t_l1 = incs(v.tensor_copy(T.l1s[:], T.pS[:, 0:40]))
+    t_l1 = incs(v.tensor_copy(T.l1s[:], T.pS[:, 0:40]), on=p_c1)
     W("g", t_l1)
-    exchange(lambda k: T.l1s[:, 10 * k:10 * k + 10], lambda k: T.l1[:, 10 * k - 10:10 * k], "rl", "ll")
-    W("y", t_l1)
+    exchange(lambda k: T.l1s[:, 10 * k:10 * k + 10], lambda k: T.l1[:, 10 * k - 10:10 * k], "rl")
+    arrived(sy, "rl")
     d_vec = dmas((sy, T.vcs[:], T.vec[:]))
 
-    B = {"f": (0, 480, 256, (T.pD, T.pT), "f"), "o": (480, 640, 480, (T.pN, T.pA), "o")}
+    B = {"f": (0, 512, (T.pD, T.pT), "f"), "o": (512, 640, (T.pN, T.pA), "o")}
     tok = {}
 
     def cols(x, b):
@@ -263,96 +265,119 @@ def rank_program(g, core, T, topo):
         return x[:, b[0] // 16:b[1] // 16]
 
     def bank(b, k, n=1):
-        return b[3][k % 2][:, 0:n * (b[1] - b[0]) // 16]
+        return b[2][k % 2][:, 0:n * (b[1] - b[0]) // 16]
 
     def lists(b, pn, name, k, add=0.0):
         W("v", tok[pn, b])
-        tok[name, b] = incs(v.tensor_scalar(lst(T[name], b), bank(b, k), add, None, A.add))
+        tok[name, b] = [incs(v.tensor_scalar(lst(T[name], b), bank(b, k), add, None, A.add), on=tok[pn, b])]
 
     def sums(b, pn, name, k, sm):
         n = (b[1] - b[0]) // 8
         W("v", tok[pn, b], s_al)
-        x = sm[:, b[0] // 8:b[1] // 8]
-        c = incs(v.tensor_tensor_scan(x, T.alt[:, 0:n], bank(b, k, 2), 0.0, A.mult, A.add))
+        c = incs(v.tensor_tensor_scan(sm[:, b[0] // 8:b[1] // 8], T.alt[:, 0:n], bank(b, k, 2), 0.0, A.mult, A.add), on=tok[pn, b])
         W("v", c)
-        tok[name, b] = incs(v.tensor_copy(lst(T[name], b), x[:, 1:n:2]))
+        tok[name, b] = [incs(v.tensor_scalar(lst(T[name], b), sm[:, b[0] // 8 + 1:b[1] // 8:2], 2 * HALF, None, A.add), on=c)]
 
     def c2(b):
-        l1 = T.l1[:, 0:30] if b[4] == "f" else T.l1s[:, 0:10]
+        parts = ((480, 512, T.l1s[:, 0:2]), (0, 480, T.l1[:, 0:30])) if b[3] == "f" else ((512, 640, T.l1s[:, 2:10]),)
         W("v", t_l1, tok["K2"])
-        if b[4] == "f":
-            arrived(v, "rq")
-            arrived(v, "rl")
-        tok["c2", b] = incs(v.tensor_tensor(cols(T.cm2, b), T.K2[:, 0:16].indirect(l1), cols(T.QS, b), A.is_le))
-        tok["lb", b] = incs(v.tensor_scalar(lst(T.l1b, b), l1, 16.0, None, A.mult))
-        W("t", tok["c2", b], t_la, t_val)
-        conv(bank(b, 1), Wc, lambda i: T.cm2[:, b[0] + i:b[1]:16], True, False)
+        c = []
+        for lo, hi, l1 in parts:
+            if lo == 0:
+                arrived(v, "rq")
+                arrived(v, "rl")
+            c.append(v.tensor_tensor(T.cm2[:, lo:hi], T.K2[:, 0:16].indirect(l1), T.QS[:, lo:hi], A.is_le))
+        tok["c2", b] = incs(*c)
+        tok["lb", b] = incs(*[v.tensor_copy(T.l1b[:, lo // 16:hi // 16], l1) for lo, hi, l1 in parts])
+        W("t", tok["c2", b], t_la, t_val, s_16)
+        conv(bank(b, 1), T.W16, lambda i: T.cm2[:, b[0] + i:b[1]:16], True, False)
         W("t", tok["lb", b])
         te.matmul(bank(b, 1), T.D01[:, 16:144], lst(T.l1b, b), False, False)
         tok["p2", b] = incs(te.matmul(bank(b, 1), T.D01[:, 176:304], lst(T.l1b, b), False, True))
 
-    def level(b, lin, win, scale, nodes, Z, pn, k, *deps):
-        W("s", tok[lin, b], *deps[:1])
-        x = incs(s.activation(Z[:, :, 1], win.indirect(lst(T[lin], b)), F.Copy, scale=scale))
-        W("v", tok[lin, b], *deps[1:])
-        y = incs(v.tensor_tensor(Z[:, :, 0], nodes.indirect(lst(T[lin], b)), cols(T.QS, b), A.is_le))
+    def part(cut, i):
+        return max(k for k in range(len(cut)) if cut[k] <= i)
+
+    def starts(out, win, l):
+        return s.activation(out, win.indirect(l), F.Identity, bias=T.bib[:, 0:1], scale=T.mkb[:, 0:1])
+
+    def level(b, lin, win, nodes, Z, pn, k, *deps):
+        W("s", *tok[lin, b], *deps[:1])
+        W("v", *tok[lin, b], *deps[1:])
+        L = T[lin]
+        if b[3] == "f":
+            c = [(incs(starts(Z[:, 64 * lo + 1:64 * hi:2], win, L[:, 2 * lo:2 * hi])),
+                  incs(v.tensor_tensor(Z[:, 64 * lo:64 * hi:2], nodes.indirect(L[:, 2 * lo:2 * hi]), T.QS[:, 32 * lo:32 * hi], A.is_le)))
+                 for lo, hi in zip(CUT_L, CUT_L[1:])]
+            tok[pn, b] = incs(conv(bank(b, k, 2), Wc, lambda i: Z[:, 64 * i:64 * i + 64], before=lambda i: c[part(CUT_L, i)]))
+            return
+        x = incs(starts(Z[:, :, 1], win, lst(L, b)))
+        y = incs(v.tensor_tensor(Z[:, :, 0], nodes.indirect(lst(L, b)), cols(T.QS, b), A.is_le))
         W("t", x, y)
         tok[pn, b] = incs(conv(bank(b, k, 2), Wc, lambda i: Z[:, i::16, :]))
 
     def kid_s(out, l):
         return s.activation(out, T.W[:, 0:8192].indirect(l), F.Copy, bias=-HALF, scale=T.mk0[:, 0:1])
 
-    def shared(b, lin, out, on_s, on_v, *deps):
-        a = []
-        for key, lo, hi in (("s", b[2], b[1]), ("v", b[0], b[2])):
-            if lo < hi:
-                W(key, tok[lin, b], *deps)
-                a.append(incs((on_s if key == "s" else on_v)(out[:, lo:hi], T[lin][:, lo // 16:hi // 16])))
-        return a
+    def kid_v(out, l):
+        return v.tensor_scalar(out, T.W[:, 0:8192].indirect(l), T.mk0[:, 0:1], -HALF, A.mult, A.add)
 
-    def kids(b, lin, kg, pn, k):
-        W("t", c_wk, *shared(b, lin, kg, kid_s, lambda x, l: v.tensor_scalar(x, T.W[:, 0:8192].indirect(l), T.mk0[:, 0:1], -HALF, A.mult, A.add), s_mk))
-        tok[pn, b] = incs(conv(bank(b, k), Wk, lambda i: kg[:, b[0] + i:b[1]:16]))
+    def kids(b, lin, G, pn, k):
+        W("s", *tok[lin, b])
+        W("t", c_wk)
+        L = T[lin]
+        if b[3] == "f":
+            W("v", *tok[lin, b], s_mk)
+            c = [[incs((kid_v, kid_s)[u](G[:, 32 * lo + u:32 * hi:2], L[:, 16 * u + lo:16 * u + hi])) for u in range(2)] for lo, hi in zip(CUT_K, CUT_K[1:])]
+            tok[pn, b] = incs(conv(bank(b, k), Wk, lambda i: G[:, 32 * i:32 * i + 32], before=lambda i: c[part(CUT_K, i)]))
+            return
+        W("t", incs(kid_s(cols(G, b), lst(L, b))))
+        tok[pn, b] = incs(conv(bank(b, k), Wk, lambda i: G[:, b[0] + i:b[1]:16]))
 
     def vectors(b):
         win = T.vcs[:, 0:4096]
-        tok["ve", b] = shared(b, "vn", T.AR, lambda x, l: s.activation(x, win.indirect(l), F.Copy), lambda x, l: v.tensor_copy(x, win.indirect(l)), d_vec)
+        W("s", *tok["vn", b], d_vec)
+        lo = 256 if b[3] == "f" else b[0]
+        tok["ve", b] = [incs(s.activation(T.AR[:, lo:b[1]], win.indirect(T.vn[:, lo // 16:b[1] // 16]), F.Copy))]
+        if b[3] == "f":
+            W("v", *tok["vn", b], d_vec)
+            tok["ve", b].append(incs(v.tensor_copy(T.AR[:, 0:256], win.indirect(T.vn[:, 0:16]))))
 
     steps = {"c2": c2, "l2": lambda b: lists(b, "p2", "l2", 1),
-             "L3": lambda b: level(b, "l2", T.b3w[:, 0:256], 1.0, T.K3[:, 0:256], T["Z3" + b[4]], "p3", 2, tok["b3"], tok["K3"]),
-             "i3": lambda b: sums(b, "p3", "i3", 2, T.sm3), "k3": lambda b: kids(b, "i3", T.kg3, "p4", 3),
+             "L3": lambda b: level(b, "l2", T.b3w[:, 0:256], T.K3[:, 0:256], T["Z3" + b[3]], "p3", 2, tok["b3"], tok["K3"]),
+             "i3": lambda b: sums(b, "p3", "i3", 2, T.sm3), "k3": lambda b: kids(b, "i3", T.G3, "p4", 3),
              "m4": lambda b: lists(b, "p4", "m4", 3, HALF),
-             "L4": lambda b: level(b, "m4", T.W[:, 4096:8192], T.mkb[:, 0:1], T.W[:, 0:4096], T["Z4" + b[4]], "p5", 4),
-             "i4": lambda b: sums(b, "p5", "i4", 4, T.sm4), "k4": lambda b: kids(b, "i4", T.kg4, "p6", 5),
+             "L4": lambda b: level(b, "m4", T.W[:, 4096:8192], T.W[:, 0:4096], T["Z4" + b[3]], "p5", 4),
+             "i4": lambda b: sums(b, "p5", "i4", 4, T.sm4), "k4": lambda b: kids(b, "i4", T.G4, "p6", 5),
              "vn": lambda b: lists(b, "p6", "vn", 5, HALF), "ve": vectors}
 
     def table(x):
         if x == "a":
             W("s", s_l16, s_mk, *d_w)
-            c = incs(kid_s(T.kg16[:], T.L16[:, 0:1]))
-            W("t", c, c_wk)
-            tok["p_m2"] = incs(conv(T.p2[:, 0:1], Wk, lambda i: T.kg16[:, i:i + 1]))
+            c = incs(s.activation(T.kgx[:], T.W[:, 0:8208].indirect(T.L16[:]), F.Copy, scale=T.mk0[:, 0:1]))
+            W("t", c)
+            tok["p_m2"] = incs(te.matmul(T.p2[:, 0:1], T.kgx[:], T.onef[:], True, True), on=c)
         if x == "b":
             W("s", tok["p_m2"])
-            tok["LM2"] = incs(s.activation(T.LM2[:, 0:1], T.p2[:, 0:1], F.Copy, bias=HALF))
-            W("s", tok["LM2"])
-            c = incs(s.activation(T.b2[:], T.W[:, 4096:8192].indirect(T.LM2[:, 0:1]), F.Copy, scale=T.mkb[:, 0:1]))
+            tok["LM2"] = incs(s.activation(T.LM2[:, 0:1], T.p2[:, 0:1], F.Copy), on=tok["p_m2"])
+            W("s", tok["LM2"], s_bi)
+            c = incs(starts(T.b2[:], T.W[:, 4096:8192], T.LM2[:, 0:1]))
             W("t", c)
-            tok["p_b2"] = incs(te.matmul(T.p1[:, 0:16], T.BD[:], T.b2[:], True, True))
+            tok["p_b2"] = incs(te.matmul(T.p1[:, 0:16], T.BD[:], T.b2[:], True, True), on=c)
             W("v", tok["LM2"], *d_w)
             tok["K2"] = incs(v.tensor_copy(T.K2[:], T.W[:, 0:4096].indirect(T.LM2[:, 0:1])))
         if x == "c":
             W("s", tok["p_b2"])
-            c = incs(s.activation(T.L256[:], T.p1[:, 0:16], F.Identity, bias=T.ioI[:, 0:1]))
+            c = incs(s.activation(T.L256[:], T.p1[:, 0:16], F.Identity, bias=T.ioB[:, 0:1]), on=tok["p_b2"])
             W("s", c)
-            c = incs(kid_s(T.kg256[:], T.L256[:, 0:16]))
-            W("t", c)
-            tok["p_m3"] = incs(conv(T.p2[:, 0:16], Wk, lambda i: T.kg256[:, i:256:16]))
+            c = [incs(kid_s(T.kg256[:, 16 * lo:16 * hi], T.L256[:, lo:hi])) for lo, hi in ((0, 6), (6, 16))]
+            W("t", c_wk)
+            tok["p_m3"] = incs(conv(T.p2[:, 0:16], Wk, lambda i: T.kg256[:, 16 * i:16 * i + 16], before=lambda i: [c[i >= 6]]))
         if x == "d":
             W("s", tok["p_m3"])
-            tok["LM3"] = incs(s.activation(T.LM3[:], T.p2[:, 0:16], F.Copy, bias=HALF))
+            tok["LM3"] = incs(s.activation(T.LM3[:], T.p2[:, 0:16], F.Copy, bias=HALF), on=tok["p_m3"])
             W("s", tok["LM3"])
-            tok["b3"] = incs(s.activation(T.b3w[:], T.W[:, 4096:8192].indirect(T.LM3[:, 0:16]), F.Copy, scale=T.mkb[:, 0:1]))
+            tok["b3"] = incs(s.activation(T.b3w[:], T.W[:, 4096:8192].indirect(T.LM3[:, 0:16]), F.Copy))
         if x == "e":
             W("v", tok["LM3"])
             tok["K3"] = incs(v.tensor_copy(T.K3[:], T.W[:, 0:4096].indirect(T.LM3[:, 0:16])))
@@ -360,24 +385,19 @@ def rank_program(g, core, T, topo):
     for x in PLAN.split():
         if x == "send":
             W("g", *tok["ve", B["f"]])
-            exchange(lambda k: T.AR[:, CAP * k - CAP:CAP * k], lambda k: RX[:, CAP * k:CAP * k + CAP], "ra", "la")
+            exchange(lambda k: T.AR[:, CAP * k - CAP:CAP * k], lambda k: RX[:, CAP * k:CAP * k + CAP], "ra")
         elif x[0] == "T":
             table(x[1])
         else:
             steps[x[:2]](B[x[2]])
 
-    W("v", t_lb, *tok["ve", B["o"]])
-    W("s", t_lb, *tok["ve", B["o"]])
+    W("v", s_lb, *tok["ve", B["o"]], *tok["ve", B["f"]])
+    W("s", s_lb, *tok["ve", B["o"]], *tok["ve", B["f"]])
     arrived(v, "ra")
     arrived(s, "ra")
-    t_y = incs(v.tensor_copy(T.yb[:, 0:256], RX.indirect(T.LB[:, 0:16])))
-    s_y = incs(s.activation(T.yb[:, 256:512], RX.indirect(T.LB[:, 16:32]), F.Copy))
-    W("y", t_y)
-    d_y0 = dmas((sy, T.y[:, 0:256], T.yb[:, 0:256]))
-    W("s", s_y)
-    d_y1 = dmas((s, T.y[:, 256:512], T.yb[:, 256:512]))
-    W("y", d_y0)
-    W("s", d_y1)
-    for name, n in sent:
-        g.wait_ge(T.sem[name], n)
+    for a in (0, 256):
+        W("y", incs(v.tensor_copy(T.yb[:, a:a + 128], RX.indirect(T.LB[:, a // 16:a // 16 + 8]))),
+          incs(s.activation(T.yb[:, a + 128:a + 256], RX.indirect(T.LB[:, a // 16 + 8:a // 16 + 16]), F.Copy)))
+        dmas((sy, T.y[:, a:a + 256], T.yb[:, a:a + 256]))
+    g.wait_ge(T.sem.left, sum(sent))
     W("g", *[t for t in every if t not in waited])

@@ -2,8 +2,7 @@ from concourse.bass import DstId, RemoteDMATransfer
 from concourse.mybir import dt, AluOpType, AxisListType, ActivationFunctionType
 
 CAP = 160
-NS = 144
-W33 = 132
+NS = 145
 HALF = 2048.0
 
 SCRATCH = {
@@ -13,15 +12,15 @@ SCRATCH = {
     "b0f": ("sbuf", [8, 2], "float32"),
     "R8b": ("sbuf", [8, 128], "bfloat16"),
     "R8": ("sbuf", [8, 128], "float32"),
-    "Z3o": ("sbuf", [128, 128, 2], "float16"),
-    "Z4o": ("sbuf", [128, 128, 2], "float16"),
+    "GE": ("sbuf", [128, 5, 33], "bfloat16"),
+    "CB": ("sbuf", [128, 4, 32], "bfloat16"),
+    "RST": ("sbuf", [128, 128], "bfloat16"),
 }
 for _dt, _bufs in (
-    ("int32", "ql 32 X0 512 W 8208 k1i 2 QS 1120 K2 16 K3 256 b3w 256 sm3 80 sm4 80"),
+    ("int32", "ql 32 X0 512 W 8208 k1i 2 QS 1120 K2 16 K3 256 b3w 256"),
     ("float32", "K1A 16 kgx 128 onef 1 e0 1 ioI 1 ioB 1 mk0 1 mku 1 mkb 1 mkt 1 bib 1"),
-    ("bfloat16", "vcs 4096 ones 160 BD 128 BDm 128 NL 128 NLm 128 CB 132 RST 132 alt 64 "
-                 "D01 320 WW 288 W16 144 GE 176 MK 132 wt 16 cm1 640 cm2 640 l1b 40 AR 1120 yb 512"),
-    ("float16", "VAL 132 F1 66 SL 32 TT 32 b2 16 Z3f 1024 Z4f 1024 kg256 256 G3 640 G4 640"),
+    ("bfloat16", "vcs 4096 ones 160 BD 128 BDm 128 NL 128 NLm 128 D01 320 WW 288 W16 144 MK 128 wt 16 cm1 640 cm2 640 l1b 40 AR 1120 yb 512"),
+    ("float16", "VAL 128 TT 128 b2 16 C3 640 S3 640 C4 640 S4 640 kg256 256 G3 640 G4 640"),
     ("uint16", "LA 32 LB 32 L16 8 LM2 2 L256 16 LM3 16 l1s 40 l1 32 l2 40 i3 40 m4 40 i4 40 vn 40"),
 ):
     _w = _bufs.split()
@@ -38,10 +37,13 @@ PLAN = """Ta Tb c2o Tc c2f l2o Td Te l2f L3f L3o i3f k3f i3o k3o m4f L4f m4o L4o
  vno veo"""
 CUT_L = (0, 8, 13, 16)
 CUT_K = (0, 6, 12, 16)
-SHARE = {}
-NK_EARLY = 15
-MID = 6656
-FILL_V = 256
+NK_LATE = [(4, 8), (8, 16)]
+NK = [(1, 2), (2, 4)]
+FILL_S = (256, 448, 512, 512, 512)
+FILL_G = 384
+FILL_V = (0, 256, 512, 192)
+FILL_Q = (192, 384)
+MID = 5312
 
 
 def rank_program(g, core, T, topo):
@@ -79,7 +81,7 @@ def rank_program(g, core, T, topo):
         ins = None
         for i in turn:
             W("t", *before(i))
-            ins = te.matmul(out, wt[:, 15 - i:143 - i], src(i), start and i == 0, stop and i == 15)
+            ins = te.matmul(out, wt[:, 15 - i:143 - i], src(i), start and i == turn[0], stop and i == turn[-1])
         return ins
 
     def order(x):
@@ -88,16 +90,16 @@ def rank_program(g, core, T, topo):
     others = order(me)
     place = {r: k for k, r in enumerate([me] + others)}
 
-    def engines_of(src, dst, sem):
+    def engines_of(src, dst):
         away = [d for d in T.cores if topo.chip(d) != topo.chip(src)]
         ae = topo.engines(src, away[0])
         if dst in away:
             n = len(ae) // len(away)
-            return ae[away.index(dst) * n:away.index(dst) * n + n][SHARE.get(sem, slice(None))]
+            return ae[away.index(dst) * n:away.index(dst) * n + n]
         return [e for e in topo.engines(src, dst) if e not in ae][::2]
 
     def arrived(q, sem):
-        q.wait_ge(T.sem[sem], sum(len(engines_of(T.cores[r], core, sem)) for r in others))
+        q.wait_ge(T.sem[sem], sum(len(engines_of(T.cores[r], core)) for r in others))
 
     sent = []
 
@@ -106,10 +108,10 @@ def rank_program(g, core, T, topo):
         for r in others:
             d = T.cores[r]
             a = topo.addr(d)
-            tr.append(RemoteDMATransfer(dst_ids=[DstId(rid=a[0], pnc=a[1])], dma_engine_mask=sum(1 << e for e in engines_of(core, d, sem)),
+            tr.append(RemoteDMATransfer(dst_ids=[DstId(rid=a[0], pnc=a[1])], dma_engine_mask=sum(1 << e for e in engines_of(core, d)),
                                         remote_sem=T.sem[sem], src=src(place[r]), dst=dst(1 + order(r).index(me))))
         g.remote_dma_fused(tr, local_sem=T.sem.left)
-        sent.append(sum(len(engines_of(core, T.cores[r], sem)) for r in others))
+        sent.append(sum(len(engines_of(core, T.cores[r])) for r in others))
 
     SX = T.QS[:, 480:1120]
     RX = T.AR[:, 480:1120]
@@ -119,17 +121,25 @@ def rank_program(g, core, T, topo):
     d_k1 = dmas((sy, T.k1i[:], T.nk[:, 0:2]))
     d_x0 = dmas(*[((sy, sy, sy, s)[o % 4], T.X0[o::16, :], T.q[:]) for o in range(16)])
     d_b0 = dmas((sy, T.b0i[:], T.beg[:, 0:2]))
-    d_w = [dmas((sy, T.W[0::16, 0:4096], T.kid[:, 0:4096]), *[(sy, T.W[o::16, 0:4096], T.nk[o::16, :]) for o in range(1, NK_EARLY + 1)])]
+    d_w = [dmas((sy, T.W[0::16, 0:4096], T.kid[:, 0:4096]), *[(sy, T.W[o::st, 0:4096], T.nk[o::st, :]) for o, st in NK])]
 
     t_ones = incs(v.memset(T.ones[:], 1.0))
-    t_cb0 = incs(v.memset(T.CB[:], 0.0))
-    t_rs0 = incs(v.memset(T.RST[:], 1.0))
-    t_mk0 = incs(v.memset(T.GE[:], 0.0))
     t_z0 = incs(v.memset(T.W[:, 7680:8208], 0))
-    t_sx0 = [incs(v.memset(T.QS[:, 480:864], 0))]
+    t_ge0 = incs(v.memset(T.GE[:, 0, 1:33], 1.0), v.memset(T.GE[:, :, 0:1], 0.0), v.memset(T.GE[:, 4, 1:33], 0.0))
+    t_cb = incs(v.memset(T.CB[:, :, 1:32], 0.0), *[v.memset(T.CB[:, r, 0:1], CAP / 16 * place[r]) for r in range(4)])
+    t_rst = incs(v.memset(T.RST[:], 1.0))
+    t_sx0 = [incs(v.memset(T.QS[:, 480:480 + FILL_Q[0]], 0))]
+    z = []
+    ends = {"s": 4096, "g": 4096 + sum(FILL_S), "v": 4096 + sum(FILL_S) + FILL_G}
+    assert ends["v"] + sum(FILL_V) == 7680
 
-    def fill(a, b):
-        return incs(*[s.activation(T.W[:, c:min(b, c + 512)], T.W[:, 7680:7680 + min(b, c + 512) - c], F.Copy) for c in range(a, b, 512)])
+    def fill(q, n):
+        a = ends[q]
+        ends[q] += n
+        if n:
+            out = T.W[:, a:a + n]
+            z.append((a, a + n, incs(v.memset(out, 0) if q == "v" else g.iota(out, [[0, n]], 0, 0) if q == "g" else
+                                     s.activation(out, T.W[:, 7680:7680 + n], F.Copy))))
 
     def sel(out, in_, pattern, op, base, cm, *deps):
         W("g", *deps)
@@ -138,124 +148,128 @@ def rank_program(g, core, T, topo):
     c_rb = sel(T.R8b[:], T.ones[0:8, 0:128], [[-1, 8], [0, 16]], A.is_equal, 0, 1, t_ones)
     W("t", c_rb)
     p_bd = incs(te.matmul(T.pB[:, 0:128], T.R8b[:], T.R8b[:], True, True))
-    W("s", t_ones, t_cb0)
-    s_cb = incs(*[s.activation(T.CB[:, 33 * r:33 * r + 1], T.ones[:, 0:1], F.Copy, scale=CAP / 16 * place[r]) for r in others])
-    W("s", t_rs0)
-    s_rst = incs(s.activation(T.RST[:, 0:132:33], T.ones[:, 0:4], F.Copy, scale=0.0))
-    W("s", t_mk0)
-    s_ge0 = incs(s.activation(T.GE[:, 1:33], T.ones[:, 0:32], F.Copy))
+    W("s", t_z0)
+    fill("s", FILL_S[0])
     W("s", c_rb)
     c_r8 = incs(s.activation(T.R8[:], T.R8b[:], F.Copy))
     W("s", p_bd)
     s_bd = incs(s.activation(T.BD[:], T.pB[:, 0:128], F.Copy))
     s_bm = incs(s.activation(T.BDm[:], T.pB[:, 0:128], F.Copy, scale=-1.0))
-    W("s", t_z0)
-    z = [fill(4096, 4544)]
+    fill("s", FILL_S[1])
     c_d0 = sel(T.D01[:, 0:160], T.ones[:], [[-32, 5], [-1000, 2], [-1, 16]], A.is_equal, 1000, 1, t_ones)
     c_nl = sel(T.NL[:], T.BD[:], [[1, 128]], A.is_gt, 0, -1, s_bd)
     W("s", c_nl)
     s_nl = incs(s.activation(T.NLm[:], T.NL[:], F.Copy, scale=-1.0))
-    z += [fill(4544, MID), fill(MID, 7680 - FILL_V)]
-
 
     W("v", d_sp)
     t_spf = incs(v.tensor_copy(T.spf[:], T.spi[:]))
-    t_sx0 += [incs(v.memset(T.QS[:, 864:1120], 0))]
+    W("v", t_rst)
+    t_rst = incs(v.memset(T.RST[:, 0:128:32], 0.0), on=t_rst)
+    t_sx0 += [incs(v.memset(T.QS[:, 480 + FILL_Q[0]:480 + FILL_Q[1]], 0))]
     W("v", d_k1)
     t_k1 = incs(v.tensor_copy(T.K1A[:, 0:2], T.k1i[:]))
-    c_d1 = sel(T.D01[:, 160:320], T.ones[:], [[-32, 5], [-1000, 2], [-1, 16]], A.is_equal, 16, 1, t_ones)
     W("g", t_k1)
     exchange(lambda k: T.K1A[:, 0:2], lambda k: T.K1A[:, 4 * k:4 * k + 2], "rk")
+    c_d1 = sel(T.D01[:, 160:320], T.ones[:], [[-32, 5], [-1000, 2], [-1, 16]], A.is_equal, 16, 1, t_ones)
+    fill("g", FILL_G)
     W("t", t_spf, c_r8)
     p_sp = incs(te.matmul(T.pS[:, 0:4], T.R8[:], T.spf[:], True, True))
-    W("t", s_bd, s_cb)
-    te.matmul(T.pN[:, 0:W33], T.BD[:], T.CB[:], True, False)
-    W("v", d_ql, p_sp, t_mk0)
-    t_ge = incs(*[v.tensor_scalar(T.GE[:, 33 * r + 1:33 * r + 33], T.ql[:], T.pS[:, r:r + 1], None, A.is_ge) for r in (1, 2, 3)])
-    W("t", t_ge, s_ge0, s_bm)
-    te.matmul(T.pN[:, 0:W33], T.BD[:], T.GE[:, 0:132], False, False)
-    te.matmul(T.pN[:, 0:W33], T.BDm[:], T.GE[:, 33:165], False, False)
-    W("t", c_nl)
-    te.matmul(T.pN[:, 0:W33], T.NL[:], T.GE[:, 1:133], False, False)
-    te.matmul(T.pN[:, 0:W33], T.NL[:], T.GE[:, 33:165], False, False)
+    W("t", s_bd, t_cb)
+    te.matmul(T.pN[:, 0:128], T.BD[:], T.CB[:], True, False)
+    W("v", t_ge0, d_ql, p_sp)
+    t_ge = incs(*[v.tensor_scalar(T.GE[:, r, 1:33], T.ql[:], T.pS[:, r:r + 1], None, A.is_ge) for r in (1, 2, 3)])
+    now, nxt, now0, nxt0 = T.GE[:, 0:4, 1:33], T.GE[:, 1:5, 1:33], T.GE[:, 0:4, 0:32], T.GE[:, 1:5, 0:32]
+    W("t", t_ge0, s_bm, c_nl, t_ge)
+    for wt, x in ((T.BD, now0), (T.BDm, nxt0), (T.NL, now), (T.NL, nxt0)):
+        te.matmul(T.pN[:, 0:128], wt[:], x, False, False)
     W("t", s_nl)
-    te.matmul(T.pN[:, 0:W33], T.NLm[:], T.GE[:, 34:166], False, False)
-    p_e = incs(te.matmul(T.pN[:, 0:W33], T.NLm[:], T.GE[:, 0:132], False, True))
-    W("v", t_ge, s_ge0)
-    t_mk = incs(v.tensor_tensor(T.MK[:], T.GE[:, 1:133], T.GE[:, 34:166], A.subtract))
-    t_w0 = incs(v.memset(T.WW[:], 0.0))
-    Wk, Wc = T.WW[:, 0:144], T.WW[:, 144:288]
-    c = sel(T.wt[:, 0:9], T.ones[:, 0:9], [[-16, 9]], A.is_ge, -1, 1)
-    c_wc = sel(Wc[:, 15:144:16], T.wt[:, 0:9], [[16, 9]], A.is_ge, 15, -1, c, t_w0)
-    c_wk = sel(Wk[:, 15:144:16], T.ones[:, 0:9], [[-16, 9]], A.is_equal, 0, 1)
-    W("v", p_e, s_rst)
-    t_u = incs(v.tensor_tensor_scan(T.pT[:, 0:W33], T.RST[:], T.pN[:, 0:W33], 0.0, A.mult, A.add))
-    W("v", t_u, t_mk)
-    t_val = incs(v.tensor_tensor(T.VAL[:], T.MK[:], T.pT[:, 0:W33], A.mult))
-    W("v", t_val)
-    t_f1 = incs(v.tensor_tensor(T.F1[:], T.VAL[:, 0:66], T.VAL[:, 66:132], A.add))
-    W("v", t_f1)
-    t_sl = incs(v.tensor_tensor(T.SL[:], T.F1[:, 0:32], T.F1[:, 33:65], A.add))
-    W("v", t_sl)
-    t_tt = incs(v.transpose(T.TT[:], T.SL[:]))
-    W("t", t_tt, c_d0, c_d1)
-    p_a = []
-    for w in range(2):
-        for gg in range(2):
-            sh = 160 * w + 16 + 16 * (w - gg)
-            p_a.append(te.matmul(T.pA[:, w:32:2], T.D01[:, sh:sh + 128], T.TT[:, 16 * gg:16 * gg + 16], gg == 0, gg == 1))
-    p_a = incs(*p_a[1::2])
-    z.append(incs(v.memset(T.W[:, 7680 - FILL_V:7680], 0)))
-    W("v", p_a)
-    t_la = incs(v.tensor_copy(T.LA[:], T.pA[:, 0:32]))
-    W("v", t_la, d_x0, *t_sx0)
-    t_sc = incs(v.tensor_copy(SX.indirect(T.LA[:, 0:32]), T.X0[:]))
-    late = []
-    for (a, b), fills in (((4096, MID), z[:2]), ((MID, 8192), z)):
-        W("y", t_z0, *fills)
-        late += [(sy, T.W[0::16, a:b], T.kid[:, a:b])] + [(sy, T.W[o::16, a:b], T.beg[:, a - 4096:b - 4096]) for o in (14, 15)]
-        d_w.append(dmas(*late[-3:]))
-
-    W("t", c_nl, t_ones)
+    te.matmul(T.pN[:, 0:128], T.NLm[:], nxt, False, False)
+    p_e = incs(te.matmul(T.pN[:, 0:128], T.NLm[:], now0, False, True))
+    W("t", t_ones)
     p_io = incs(te.matmul(T.p2[:, 0:1], T.NL[:], T.ones[:, 0:1], True, True))
     W("s", d_b0)
     s_b0 = incs(s.activation(T.b0f[:], T.b0i[:], F.Copy))
     W("t", s_b0)
     p_b0 = incs(te.matmul(T.p1[:, 0:2], T.R8[:], T.b0f[:], True, True))
-    W("s", p_io)
+    t_w0 = incs(v.memset(T.WW[:], 0.0))
+    W("v", t_ge)
+    t_mk = incs(v.tensor_tensor(T.MK[:], now, nxt, A.subtract))
+    Wk, Wc = T.WW[:, 0:144], T.WW[:, 144:288]
+    c = sel(T.wt[:, 0:9], T.ones[:, 0:9], [[-16, 9]], A.is_ge, -1, 1)
+    c_wk = sel(Wk[:, 15:144:16], T.ones[:, 0:9], [[-16, 9]], A.is_equal, 0, 1, t_w0)
+    c_wc = sel(Wc[:, 15:144:16], T.wt[:, 0:9], [[16, 9]], A.is_ge, 15, -1, c)
+    W("v", t_rst, p_e)
+    t_u = incs(v.tensor_tensor_scan(T.pT[:, 0:128], T.RST[:], T.pN[:, 0:128], 0.0, A.mult, A.add))
+    t_sx0 += [incs(v.memset(T.QS[:, 480 + FILL_Q[1]:1120], 0))]
+    fill("v", FILL_V[0])
+    W("v", t_mk, t_u)
+    t_val = incs(v.tensor_tensor(T.VAL[:], T.MK[:], T.pT[:, 0:128], A.mult))
+    fill("v", FILL_V[1])
+    W("v", t_val)
+    t_tt = incs(v.transpose(T.TT[:], T.VAL[:]))
+    fill("v", FILL_V[2])
+    W("t", c_d0, c_d1, t_tt)
+    p_a = []
+    for w in range(2):
+        for r in range(4):
+            for gg in range(2):
+                sh = 160 * w + 16 + 16 * (w - gg)
+                ins = te.matmul(T.pA[:, w:32:2], T.D01[:, sh:sh + 128], T.TT[:, 32 * r + 16 * gg:32 * r + 16 * gg + 16], r + gg == 0, r + gg == 4)
+        p_a.append(ins)
+    p_a = incs(*p_a)
+    W("v", p_a)
+    t_la = incs(v.tensor_copy(T.LA[:], T.pA[:, 0:32]))
+    fill("v", FILL_V[3])
+    W("v", d_x0, *t_sx0, t_la)
+    t_sc = incs(v.tensor_copy(SX.indirect(T.LA[:, 0:32]), T.X0[:]))
+    for r in range(4):
+        te.matmul(T.pB[:, 0:32], T.D01[:, 16:144], T.VAL[:, 32 * r:32 * r + 32], r == 0, False)
+        ins = te.matmul(T.pB[:, 0:32], T.D01[:, 176:304], T.VAL[:, 32 * r:32 * r + 32], False, r == 3)
+    p_lb = incs(ins)
+
+    fill("s", FILL_S[2])
+    W("s", t_ones, p_io)
     s_io = incs(s.activation(T.ioI[:], T.p2[:, 0:1], F.Copy, bias=-8192.0), s.activation(T.onef[:], T.ones[:, 0:1], F.Copy))
     c = incs(s.activation(T.mku[:], T.p2[:, 0:1], F.Relu, bias=14.0, scale=-1.0), s.activation(T.mkt[:], T.p2[:, 0:1], F.Copy, bias=-4110.5),
              s.activation(T.ioB[:], T.p2[:, 0:1], F.Copy, bias=2 * HALF))
     s_mk = incs(s.activation(T.mk0[:], T.p2[:, 0:1], F.Relu, bias=1.0, scale=-1.0))
-    W("s", c)
+    fill("s", FILL_S[3])
+    W("s", c, s_io, p_b0)
     c = incs(s.activation(T.mkb[:], T.mku[:], F.Relu, bias=0.5, scale=-1.0), on=c)
-    W("s", c)
+    e = incs(s.activation(T.e0[:], T.p1[:, 0:1], F.Identity, bias=T.ioI[:, 0:1]))
+    fill("s", FILL_S[4])
+    W("s", c, e)
     s_bi = incs(s.activation(T.bib[:], T.mkt[:], F.Copy, scale=T.mkb[:, 0:1]), on=c)
-    W("s", s_io, p_b0)
-    c = incs(s.activation(T.e0[:], T.p1[:, 0:1], F.Identity, bias=T.ioI[:, 0:1]))
-    W("s", c)
-    s_l16 = incs(s.activation(T.L16[:], T.BD[:, 0:128:16], F.Copy, bias=8192.0, scale=T.e0[:, 0:1]), on=c)
-    W("s", c_wc, t_sl)
+    s_l16 = incs(s.activation(T.L16[:], T.BD[:, 0:128:16], F.Copy, bias=8192.0, scale=T.e0[:, 0:1]), on=e)
+    W("s", p_lb)
+    s_lb = incs(s.activation(T.LB[:], T.pB[:, 0:32], F.Copy), on=p_lb)
+    W("s", c_wc)
     s_16 = incs(s.activation(T.W16[:], Wc, F.Copy, scale=16.0))
-    s_lb = incs(s.activation(T.LB[:], T.SL[:], F.Copy))
-    s_al = incs(s.activation(T.alt[:, 0:64:2], T.ones[:, 0:32], F.Copy, scale=0.0), s.activation(T.alt[:, 1:64:2], T.ones[:, 0:32], F.Copy))
+    for a, b in ((4096, MID), (MID, 8192)):
+        W("y", t_z0, *[tk for lo, hi, tk in z if lo < b and hi > a])
+        d_w.append(dmas((sy, T.W[0::16, a:b], T.kid[:, a:b]), *[(sy, T.W[o::16, a:b], T.beg[:, a - 4096:b - 4096]) for o in (14, 15)],
+                        *[(sy, T.W[o::st, 0:4096], T.nk[o::st, :]) for o, st in NK_LATE if a == 4096]))
 
     W("g", t_sc)
     exchange(lambda k: SX[:, CAP * k:CAP * k + CAP], lambda k: T.QS[:, CAP * k - CAP:CAP * k], "rq")
-    W("v", t_sc)
     arrived(v, "rk")
-    t_c1 = [incs(*[v.tensor_scalar(T.cm1[:, CAP * k + u:CAP * k + CAP:2], SX[:, CAP * k + u:CAP * k + CAP:2], T.K1A[:, 4 * k:4 * k + 1], None, A.is_ge)
-                   for k in range(4)]) for u in range(2)]
+    W("v", t_k1, t_sc)
+
+    def level1(k, u, n):
+        return v.tensor_scalar(T.cm1[:, CAP * k + u:CAP * k + CAP:n], SX[:, CAP * k + u:CAP * k + CAP:n], T.K1A[:, 4 * k:4 * k + 1], None, A.is_ge)
+
+    t_c1 = [incs(*[level1(k, u, 2) for k in (1, 2, 3)]) for u in range(2)]
+    t_c0 = incs(level1(0, 0, 1))
     W("t", c_wc, t_ge)
-    p_c1 = incs(conv(T.pS[:, 0:40], Wc, lambda i: T.cm1[:, i:640:16], before=lambda i: [t_c1[i % 2]], turn=[*range(0, 16, 2), *range(1, 16, 2)]))
+    p_c1 = incs(conv(T.pS[:, 0:30], Wc, lambda i: T.cm1[:, CAP + i:640:16], before=lambda i: [t_c1[i % 2]], turn=[*range(0, 16, 2), *range(1, 16, 2)]))
     W("v", p_c1)
-    t_l1 = incs(v.tensor_copy(T.l1s[:], T.pS[:, 0:40]), on=p_c1)
+    t_l1 = incs(v.tensor_copy(T.l1s[:, 10:40], T.pS[:, 0:30]), on=p_c1)
     W("g", t_l1)
     exchange(lambda k: T.l1s[:, 10 * k:10 * k + 10], lambda k: T.l1[:, 10 * k - 10:10 * k], "rl")
     arrived(sy, "rl")
     d_vec = dmas((sy, T.vcs[:], T.vec[:]))
 
-    B = {"f": (0, 512, (T.pD, T.pT), "f"), "o": (512, 640, (T.pN, T.pA), "o")}
+    B = {"f": (0, 512, T.pD, "f"), "o": (512, 640, T.pN, "o")}
     tok = {}
 
     def cols(x, b):
@@ -264,57 +278,51 @@ def rank_program(g, core, T, topo):
     def lst(x, b):
         return x[:, b[0] // 16:b[1] // 16]
 
-    def bank(b, k, n=1):
-        return b[2][k % 2][:, 0:n * (b[1] - b[0]) // 16]
+    def bank(b):
+        return b[2][:, 0:(b[1] - b[0]) // 16]
 
-    def lists(b, pn, name, k, add=0.0):
-        W("v", tok[pn, b])
-        tok[name, b] = [incs(v.tensor_scalar(lst(T[name], b), bank(b, k), add, None, A.add), on=tok[pn, b])]
+    def rhs(x, b, i):
+        return x[:, b[0] + i:b[1]:16] if b[3] == "o" else x[:, 32 * i:32 * i + 32]
 
-    def sums(b, pn, name, k, sm):
-        n = (b[1] - b[0]) // 8
-        W("v", tok[pn, b], s_al)
-        c = incs(v.tensor_tensor_scan(sm[:, b[0] // 8:b[1] // 8], T.alt[:, 0:n], bank(b, k, 2), 0.0, A.mult, A.add), on=tok[pn, b])
-        W("v", c)
-        tok[name, b] = [incs(v.tensor_scalar(lst(T[name], b), sm[:, b[0] // 8 + 1:b[1] // 8:2], 2 * HALF, None, A.add), on=c)]
+    def lists(b, name, add):
+        W("v", tok["p", b])
+        tok[name, b] = incs(v.tensor_scalar(lst(T[name], b), bank(b), add, None, A.add), on=tok["p", b])
 
     def c2(b):
         parts = ((480, 512, T.l1s[:, 0:2]), (0, 480, T.l1[:, 0:30])) if b[3] == "f" else ((512, 640, T.l1s[:, 2:10]),)
-        W("v", t_l1, tok["K2"])
+        W("v", tok["l0"], tok["K2"])
         c = []
         for lo, hi, l1 in parts:
             if lo == 0:
                 arrived(v, "rq")
                 arrived(v, "rl")
             c.append(v.tensor_tensor(T.cm2[:, lo:hi], T.K2[:, 0:16].indirect(l1), T.QS[:, lo:hi], A.is_le))
-        tok["c2", b] = incs(*c)
-        tok["lb", b] = incs(*[v.tensor_copy(T.l1b[:, lo // 16:hi // 16], l1) for lo, hi, l1 in parts])
-        W("t", tok["c2", b], t_la, t_val, s_16)
-        conv(bank(b, 1), T.W16, lambda i: T.cm2[:, b[0] + i:b[1]:16], True, False)
-        W("t", tok["lb", b])
-        te.matmul(bank(b, 1), T.D01[:, 16:144], lst(T.l1b, b), False, False)
-        tok["p2", b] = incs(te.matmul(bank(b, 1), T.D01[:, 176:304], lst(T.l1b, b), False, True))
-
-    def part(cut, i):
-        return max(k for k in range(len(cut)) if cut[k] <= i)
+        c = incs(*c)
+        lb = incs(*[v.tensor_copy(T.l1b[:, lo // 16:hi // 16], l1) for lo, hi, l1 in parts])
+        W("t", t_u, s_16, c)
+        conv(bank(b), T.W16, lambda i: T.cm2[:, b[0] + i:b[1]:16], True, False)
+        W("t", lb)
+        te.matmul(bank(b), T.D01[:, 16:144], lst(T.l1b, b), False, False)
+        tok["p", b] = incs(te.matmul(bank(b), T.D01[:, 176:304], lst(T.l1b, b), False, True), on=c)
 
     def starts(out, win, l):
         return s.activation(out, win.indirect(l), F.Identity, bias=T.bib[:, 0:1], scale=T.mkb[:, 0:1])
 
-    def level(b, lin, win, nodes, Z, pn, k, *deps):
-        W("s", *tok[lin, b], *deps[:1])
-        W("v", *tok[lin, b], *deps[1:])
-        L = T[lin]
-        if b[3] == "f":
-            c = [(incs(starts(Z[:, 64 * lo + 1:64 * hi:2], win, L[:, 2 * lo:2 * hi])),
-                  incs(v.tensor_tensor(Z[:, 64 * lo:64 * hi:2], nodes.indirect(L[:, 2 * lo:2 * hi]), T.QS[:, 32 * lo:32 * hi], A.is_le)))
-                 for lo, hi in zip(CUT_L, CUT_L[1:])]
-            tok[pn, b] = incs(conv(bank(b, k, 2), Wc, lambda i: Z[:, 64 * i:64 * i + 64], before=lambda i: c[part(CUT_L, i)]))
-            return
-        x = incs(starts(Z[:, :, 1], win, lst(L, b)))
-        y = incs(v.tensor_tensor(Z[:, :, 0], nodes.indirect(lst(L, b)), cols(T.QS, b), A.is_le))
-        W("t", x, y)
-        tok[pn, b] = incs(conv(bank(b, k, 2), Wc, lambda i: Z[:, i::16, :]))
+    def level(b, lin, win, nodes, C, S, *deps):
+        W("s", *deps[:1], tok[lin, b])
+        W("v", *deps[1:], tok[lin, b])
+        cut = (0, 16) if b[3] == "o" else CUT_L
+        n = (b[1] - b[0]) // 16
+        for lo, hi in zip(cut, cut[1:]):
+            c0, c1 = b[0] + n * lo, b[0] + n * hi
+            l = T[lin][:, c0 // 16:c1 // 16]
+            x = incs(starts(S[:, c0:c1], win, l))
+            y = incs(v.tensor_tensor(C[:, c0:c1], nodes.indirect(l), T.QS[:, c0:c1], A.is_le), on=tok[lin, b] if lo == 0 else None)
+            W("t", y)
+            conv(bank(b), Wc, lambda i: rhs(C, b, i), lo == 0, False, turn=range(lo, hi))
+            W("t", x)
+            ins = conv(bank(b), Wc, lambda i: rhs(S, b, i), False, hi == 16, turn=range(lo, hi))
+        tok["p", b] = incs(ins, on=x)
 
     def kid_s(out, l):
         return s.activation(out, T.W[:, 0:8192].indirect(l), F.Copy, bias=-HALF, scale=T.mk0[:, 0:1])
@@ -322,34 +330,35 @@ def rank_program(g, core, T, topo):
     def kid_v(out, l):
         return v.tensor_scalar(out, T.W[:, 0:8192].indirect(l), T.mk0[:, 0:1], -HALF, A.mult, A.add)
 
-    def kids(b, lin, G, pn, k):
-        W("s", *tok[lin, b])
+    def kids(b, lin, G):
+        W("s", tok[lin, b])
         W("t", c_wk)
         L = T[lin]
         if b[3] == "f":
-            W("v", *tok[lin, b], s_mk)
+            W("v", s_mk, tok[lin, b])
             c = [[incs((kid_v, kid_s)[u](G[:, 32 * lo + u:32 * hi:2], L[:, 16 * u + lo:16 * u + hi])) for u in range(2)] for lo, hi in zip(CUT_K, CUT_K[1:])]
-            tok[pn, b] = incs(conv(bank(b, k), Wk, lambda i: G[:, 32 * i:32 * i + 32], before=lambda i: c[part(CUT_K, i)]))
+            tok["p", b] = incs(conv(bank(b), Wk, lambda i: rhs(G, b, i), before=lambda i: c[max(k for k in range(len(CUT_K)) if CUT_K[k] <= i)]), on=c[-1][1])
             return
-        W("t", incs(kid_s(cols(G, b), lst(L, b))))
-        tok[pn, b] = incs(conv(bank(b, k), Wk, lambda i: G[:, b[0] + i:b[1]:16]))
+        c = incs(kid_s(cols(G, b), lst(L, b)), on=tok[lin, b])
+        W("t", c)
+        tok["p", b] = incs(conv(bank(b), Wk, lambda i: rhs(G, b, i)), on=c)
 
     def vectors(b):
         win = T.vcs[:, 0:4096]
-        W("s", *tok["vn", b], d_vec)
-        lo = 256 if b[3] == "f" else b[0]
-        tok["ve", b] = [incs(s.activation(T.AR[:, lo:b[1]], win.indirect(T.vn[:, lo // 16:b[1] // 16]), F.Copy))]
-        if b[3] == "f":
-            W("v", *tok["vn", b], d_vec)
-            tok["ve", b].append(incs(v.tensor_copy(T.AR[:, 0:256], win.indirect(T.vn[:, 0:16]))))
+        W("s", d_vec, tok["vn", b])
+        mid = b[0] if b[3] == "o" else b[0] + 256
+        tok["ve", b] = [incs(s.activation(T.AR[:, mid:b[1]], win.indirect(T.vn[:, mid // 16:b[1] // 16]), F.Copy))]
+        if mid > b[0]:
+            W("v", d_vec, tok["vn", b])
+            tok["ve", b].append(incs(v.tensor_copy(T.AR[:, b[0]:mid], win.indirect(T.vn[:, b[0] // 16:mid // 16])), on=tok["vn", b]))
 
-    steps = {"c2": c2, "l2": lambda b: lists(b, "p2", "l2", 1),
-             "L3": lambda b: level(b, "l2", T.b3w[:, 0:256], T.K3[:, 0:256], T["Z3" + b[3]], "p3", 2, tok["b3"], tok["K3"]),
-             "i3": lambda b: sums(b, "p3", "i3", 2, T.sm3), "k3": lambda b: kids(b, "i3", T.G3, "p4", 3),
-             "m4": lambda b: lists(b, "p4", "m4", 3, HALF),
-             "L4": lambda b: level(b, "m4", T.W[:, 4096:8192], T.W[:, 0:4096], T["Z4" + b[3]], "p5", 4),
-             "i4": lambda b: sums(b, "p5", "i4", 4, T.sm4), "k4": lambda b: kids(b, "i4", T.G4, "p6", 5),
-             "vn": lambda b: lists(b, "p6", "vn", 5, HALF), "ve": vectors}
+    steps = {"c2": c2, "l2": lambda b: lists(b, "l2", 0.0),
+             "L3": lambda b: level(b, "l2", T.b3w[:, 0:256], T.K3[:, 0:256], T.C3, T.S3, tok["b3"], tok["K3"]),
+             "i3": lambda b: lists(b, "i3", 2 * HALF), "k3": lambda b: kids(b, "i3", T.G3),
+             "m4": lambda b: lists(b, "m4", HALF),
+             "L4": lambda b: level(b, "m4", T.W[:, 4096:8192], T.W[:, 0:4096], T.C4, T.S4),
+             "i4": lambda b: lists(b, "i4", 2 * HALF), "k4": lambda b: kids(b, "i4", T.G4),
+             "vn": lambda b: lists(b, "vn", HALF), "ve": vectors}
 
     def table(x):
         if x == "a":
@@ -357,22 +366,26 @@ def rank_program(g, core, T, topo):
             c = incs(s.activation(T.kgx[:], T.W[:, 0:8208].indirect(T.L16[:]), F.Copy, scale=T.mk0[:, 0:1]))
             W("t", c)
             tok["p_m2"] = incs(te.matmul(T.p2[:, 0:1], T.kgx[:], T.onef[:], True, True), on=c)
+            W("t", t_la, t_c0)
+            c = incs(conv(T.pA[:, 0:10], Wc, lambda i: T.cm1[:, i:CAP:16]), on=t_c0)
+            W("v", c)
+            tok["l0"] = incs(v.tensor_copy(T.l1s[:, 0:10], T.pA[:, 0:10]), on=c)
         if x == "b":
             W("s", tok["p_m2"])
             tok["LM2"] = incs(s.activation(T.LM2[:, 0:1], T.p2[:, 0:1], F.Copy), on=tok["p_m2"])
-            W("s", tok["LM2"], s_bi)
+            W("s", s_bi, tok["LM2"])
             c = incs(starts(T.b2[:], T.W[:, 4096:8192], T.LM2[:, 0:1]))
             W("t", c)
             tok["p_b2"] = incs(te.matmul(T.p1[:, 0:16], T.BD[:], T.b2[:], True, True), on=c)
-            W("v", tok["LM2"], *d_w)
+            W("v", *d_w, tok["LM2"])
             tok["K2"] = incs(v.tensor_copy(T.K2[:], T.W[:, 0:4096].indirect(T.LM2[:, 0:1])))
         if x == "c":
             W("s", tok["p_b2"])
             c = incs(s.activation(T.L256[:], T.p1[:, 0:16], F.Identity, bias=T.ioB[:, 0:1]), on=tok["p_b2"])
             W("s", c)
-            c = [incs(kid_s(T.kg256[:, 16 * lo:16 * hi], T.L256[:, lo:hi])) for lo, hi in ((0, 6), (6, 16))]
+            c = [incs(kid_s(T.kg256[:, 16 * lo:16 * hi], T.L256[:, lo:hi])) for lo, hi in ((0, 10), (10, 16))]
             W("t", c_wk)
-            tok["p_m3"] = incs(conv(T.p2[:, 0:16], Wk, lambda i: T.kg256[:, 16 * i:16 * i + 16], before=lambda i: [c[i >= 6]]))
+            tok["p_m3"] = incs(conv(T.p2[:, 0:16], Wk, lambda i: T.kg256[:, 16 * i:16 * i + 16], before=lambda i: [c[i >= 10]]))
         if x == "d":
             W("s", tok["p_m3"])
             tok["LM3"] = incs(s.activation(T.LM3[:], T.p2[:, 0:16], F.Copy, bias=HALF), on=tok["p_m3"])

@@ -8,6 +8,8 @@ HALF = 2048.0
 SCRATCH = {
     "spi": ("sbuf", [8, 4], "int32"),
     "spf": ("sbuf", [8, 4], "float32"),
+    "q8i": ("sbuf", [8, 512], "int32"),
+    "q8f": ("sbuf", [8, 512], "float32"),
     "b0i": ("sbuf", [8, 2], "int32"),
     "b0f": ("sbuf", [8, 2], "float32"),
     "R8b": ("sbuf", [8, 128], "bfloat16"),
@@ -17,11 +19,11 @@ SCRATCH = {
     "RST": ("sbuf", [128, 128], "bfloat16"),
 }
 for _dt, _bufs in (
-    ("int32", "ql 32 X0 512 W 8208 k1i 2 QS 1120 K2 16 K3 256 b3w 256"),
-    ("float32", "K1A 16 kgx 128 onef 1 e0 1 ioI 1 ioB 1 mk0 1 mku 1 mkb 1 mkt 1 bib 1"),
-    ("bfloat16", "vcs 4096 ones 160 BD 128 BDm 128 NL 128 NLm 128 D01 320 WW 288 W16 144 MK 128 wt 16 cm1 640 cm2 640 l1b 40 AR 1120 yb 512"),
-    ("float16", "VAL 128 TT 128 b2 16 C3 640 S3 640 C4 640 S4 640 kg256 256 G3 640 G4 640"),
-    ("uint16", "LA 32 LB 32 L16 8 LM2 2 L256 16 LM3 16 l1s 40 l1 32 l2 40 i3 40 m4 40 i4 40 vn 40"),
+    ("int32", "ql 32 qT 32 X0 512 W 8208 k1i 2 QS 1120 K2 16 K3 256 b3w 256"),
+    ("float32", "K1A 16 kgx 128 onef 1 e0 1 ioI 1 ioB 1 mk0 1 mka 1 mku 1 mkb 1 mkt 1 bib 1"),
+    ("bfloat16", "vcs 4096 ones 160 src 512 BD 128 BDm 128 NL 128 NLm 128 E01 320 ID 128 WW 288 W16 144 MK 128 wt 16 cm1 640 cm2 640 l1b 42 AR 1120 yb 512"),
+    ("float16", "VAL 128 TT 32 SL 32 b2 16 C3 640 S3 640 C4 640 S4 640 kg256 256 G3 672 G4 672 sm1 10"),
+    ("uint16", "LA 32 LB 32 L16 8 LM2 2 L256 16 LM3 16 l1s 40 l1 32 l2 42 i3 42 m4 42 i4 42 vn 42"),
 ):
     _w = _bufs.split()
     for _k in range(0, len(_w), 2):
@@ -33,17 +35,43 @@ SEMAPHORES = ["s%d" % i for i in range(NS)] + ["rk", "rq", "rl", "ra", "left"]
 A = AluOpType
 F = ActivationFunctionType
 
-PLAN = """Ta Tb c2o Tc c2f l2o Td Te l2f L3f L3o i3f k3f i3o k3o m4f L4f m4o L4o i4f k4f i4o k4o vnf vef send
- vno veo"""
-CUT_L = (0, 8, 13, 16)
-CUT_K = (0, 6, 12, 16)
+PLAN = """Ta Tb c2o Tc c2a c2b Td Te l2a l2o l2b L3a L3b L3o i3a k3a i3b i3o k3b k3o m4a L4a m4b m4o L4b
+ i4a L4o k4a i4b k4b vna i4o vea vnb k4o veb send Tl vno veo"""
+QL_Q = "sysysysy"
+G_FIRST = 0
+CUT_L = (0, 7, 12, 15)
+CUT_S = (0, 7, 12, 15)
+CUT_K = (0, 10, 16)
 NK_LATE = [(4, 8), (8, 16)]
 NK = [(1, 2), (2, 4)]
-FILL_S = (256, 448, 512, 512, 512)
-FILL_G = 384
-FILL_V = (0, 256, 512, 192)
-FILL_Q = (192, 384)
-MID = 5312
+FILL_0 = (160, 160)
+FILL_S = (224, 512, 416, 448)
+FILL_E = 512
+K3V = 256
+X0_AT = 3
+LATE_AT = 3
+X0_PE = 1
+X0_S = 0
+NK_PRE = 1
+FILL_1 = 192
+STORE = 1
+X0_PRE = 256
+FILL_G = 832
+FILL_V = (128, 512)
+FILL_Q = (256, 512)
+LATE_Q = "yys"
+L1_S = 1
+RA2 = 0
+Q8_S = 320
+DELAY_W = 0
+DELAY_Q = 0
+KG = 12
+KV = 8
+CUT_A = ((0, 10, 16), (0, 10, 16))
+CUT_B = ((0, 10, 14), (0, 10, 14))
+FILL_D = 0
+NK_WAIT = 0
+INSIDE = ()
 
 
 def rank_program(g, core, T, topo):
@@ -103,7 +131,7 @@ def rank_program(g, core, T, topo):
 
     sent = []
 
-    def exchange(src, dst, sem):
+    def exchange(src, dst, sem, others=others):
         tr = []
         for r in others:
             d = T.cores[r]
@@ -117,29 +145,35 @@ def rank_program(g, core, T, topo):
     RX = T.AR[:, 480:1120]
 
     d_sp = dmas((s, T.spi[:], T.spl[:]))
-    d_ql = dmas((sy, T.ql[:], T.q[:]))
+    if X0_PE:
+        d_q8 = dmas((sy, T.q8i[:], T.q[:]))
+    d_ql = dmas(*[(queues[QL_Q[G]], T.ql[32 * (G // 2):32 * (G // 2) + 32, 16 * (G % 2):16 * (G % 2) + 16], T.q[16 * G:16 * G + 16, :]) for G in range(8)])
     d_k1 = dmas((sy, T.k1i[:], T.nk[:, 0:2]))
-    d_x0 = dmas(*[((sy, sy, sy, s)[o % 4], T.X0[o::16, :], T.q[:]) for o in range(16)])
     d_b0 = dmas((sy, T.b0i[:], T.beg[:, 0:2]))
-    d_w = [dmas((sy, T.W[0::16, 0:4096], T.kid[:, 0:4096]), *[(sy, T.W[o::st, 0:4096], T.nk[o::st, :]) for o, st in NK])]
+    d_w = [dmas((sy, T.W[0::16, 0:4096], T.kid[:, 0:4096]), *[(sy, T.W[o::st, 0:4096], T.nk[o::st, :]) for o, st in NK[:NK_PRE]])]
+    if not X0_PE:
+        d_x0 = dmas(*[(s if o < X0_S else sy, T.X0[o::16, :], T.q[:]) for o in range(16)])
+    if not NK_WAIT:
+        d_w += [dmas(*[(sy, T.W[o::st, 0:4096], T.nk[o::st, :]) for o, st in NK[NK_PRE:]])]
 
     t_ones = incs(v.memset(T.ones[:], 1.0))
-    t_z0 = incs(v.memset(T.W[:, 7680:8208], 0))
-    t_ge0 = incs(v.memset(T.GE[:, 0, 1:33], 1.0), v.memset(T.GE[:, :, 0:1], 0.0), v.memset(T.GE[:, 4, 1:33], 0.0))
-    t_cb = incs(v.memset(T.CB[:, :, 1:32], 0.0), *[v.memset(T.CB[:, r, 0:1], CAP / 16 * place[r]) for r in range(4)])
-    t_rst = incs(v.memset(T.RST[:], 1.0))
+    t_src = t_z0 = incs(v.memset(T.W[:, 8192 - FILL_E:8208], 0))
+    t_rst = incs(v.memset(T.GE[:], 0.0), v.memset(T.CB[:], 0.0), v.memset(T.RST[:], 1.0))
     t_sx0 = [incs(v.memset(T.QS[:, 480:480 + FILL_Q[0]], 0))]
     z = []
-    ends = {"s": 4096, "g": 4096 + sum(FILL_S), "v": 4096 + sum(FILL_S) + FILL_G}
-    assert ends["v"] + sum(FILL_V) == 7680
+    MID = 4096 + FILL_G + FILL_V[-1] + sum(FILL_S[LATE_AT:])
+    ends = {False: MID + FILL_D, True: 4096}
+    assert FILL_1 + sum(FILL_0 + FILL_S + FILL_V) + FILL_G + FILL_E + FILL_D == 4096
+    if FILL_D:
+        d_w.append(dmas(*[(sy, T.W[o::st, MID:MID + FILL_D], T.nk[o::st, 0:FILL_D]) for o, st in ((1, 2), (2, 4), (8, 16))]))
 
-    def fill(q, n):
-        a = ends[q]
-        ends[q] += n
+    def fill(q, n, late=False):
+        a = ends[late]
+        ends[late] += n
         if n:
             out = T.W[:, a:a + n]
             z.append((a, a + n, incs(v.memset(out, 0) if q == "v" else g.iota(out, [[0, n]], 0, 0) if q == "g" else
-                                     s.activation(out, T.W[:, 7680:7680 + n], F.Copy))))
+                                     s.activation(out, T.ones[:, 0:n] if n <= 160 else T.pD[:, 0:n] if late else T.W[:, 7680:7680 + n], F.Copy))))
 
     def sel(out, in_, pattern, op, base, cm, *deps):
         W("g", *deps)
@@ -148,36 +182,57 @@ def rank_program(g, core, T, topo):
     c_rb = sel(T.R8b[:], T.ones[0:8, 0:128], [[-1, 8], [0, 16]], A.is_equal, 0, 1, t_ones)
     W("t", c_rb)
     p_bd = incs(te.matmul(T.pB[:, 0:128], T.R8b[:], T.R8b[:], True, True))
-    W("s", t_z0)
+    c_r8 = sel(T.R8[:], T.ones[0:8, 0:128], [[-1, 8], [0, 16]], A.is_equal, 0, 1)
+    W("s", t_ones)
+    for n in FILL_0:
+        fill("s", n)
+    W("s", t_src)
     fill("s", FILL_S[0])
-    W("s", c_rb)
-    c_r8 = incs(s.activation(T.R8[:], T.R8b[:], F.Copy))
     W("s", p_bd)
     s_bd = incs(s.activation(T.BD[:], T.pB[:, 0:128], F.Copy))
     s_bm = incs(s.activation(T.BDm[:], T.pB[:, 0:128], F.Copy, scale=-1.0))
-    fill("s", FILL_S[1])
-    c_d0 = sel(T.D01[:, 0:160], T.ones[:], [[-32, 5], [-1000, 2], [-1, 16]], A.is_equal, 1000, 1, t_ones)
+    if X0_PE:
+        W("s", d_q8)
+        s_q8 = incs(s.activation(T.q8f[:, 0:Q8_S], T.q8i[:, 0:Q8_S], F.Copy))
+    fill("s", FILL_1)
+    c_id = sel(T.ID[:], T.ones[:, 0:128], [[-1, 128]], A.is_equal, 0, 1)
     c_nl = sel(T.NL[:], T.BD[:], [[1, 128]], A.is_gt, 0, -1, s_bd)
     W("s", c_nl)
     s_nl = incs(s.activation(T.NLm[:], T.NL[:], F.Copy, scale=-1.0))
+    W("s", d_b0)
+    s_b0 = incs(s.activation(T.b0f[:], T.b0i[:], F.Copy))
 
+    W("v", t_rst)
+    t_rst = t_ge0 = incs(v.memset(T.RST[:, 0:128:32], 0.0), v.memset(T.GE[:, 0, 1:33], 1.0), on=t_rst)
     W("v", d_sp)
     t_spf = incs(v.tensor_copy(T.spf[:], T.spi[:]))
-    W("v", t_rst)
-    t_rst = incs(v.memset(T.RST[:, 0:128:32], 0.0), on=t_rst)
-    t_sx0 += [incs(v.memset(T.QS[:, 480 + FILL_Q[0]:480 + FILL_Q[1]], 0))]
+    t_cb = incs(*[v.memset(T.CB[:, r, 0:1], CAP / 16 * place[r]) for r in others])
+    t_q8 = []
+    if X0_PE and Q8_S < 512:
+        W("v", d_q8)
+        t_q8 = [incs(v.tensor_copy(T.q8f[:, Q8_S:512], T.q8i[:, Q8_S:512]))]
+    W("v", d_ql)
+    t_qt = incs(v.transpose(T.qT[:], T.ql[:]))
     W("v", d_k1)
     t_k1 = incs(v.tensor_copy(T.K1A[:, 0:2], T.k1i[:]))
+    if NK_WAIT:
+        W("y", t_k1)
+        d_w += [dmas(*[(sy, T.W[o::st, 0:4096], T.nk[o::st, :]) for o, st in NK[NK_PRE:]])]
+    fill("g", G_FIRST, True)
     W("g", t_k1)
     exchange(lambda k: T.K1A[:, 0:2], lambda k: T.K1A[:, 4 * k:4 * k + 2], "rk")
-    c_d1 = sel(T.D01[:, 160:320], T.ones[:], [[-32, 5], [-1000, 2], [-1, 16]], A.is_equal, 16, 1, t_ones)
-    fill("g", FILL_G)
+    fill("g", FILL_G - G_FIRST, True)
     W("t", t_spf, c_r8)
     p_sp = incs(te.matmul(T.pS[:, 0:4], T.R8[:], T.spf[:], True, True))
     W("t", s_bd, t_cb)
     te.matmul(T.pN[:, 0:128], T.BD[:], T.CB[:], True, False)
-    W("v", t_ge0, d_ql, p_sp)
-    t_ge = incs(*[v.tensor_scalar(T.GE[:, r, 1:33], T.ql[:], T.pS[:, r:r + 1], None, A.is_ge) for r in (1, 2, 3)])
+    if X0_PRE and X0_PE:
+        W("t", s_q8, *(t_q8 if X0_PRE > Q8_S else []))
+        p_x0 = te.matmul(T.pD[:, 0:X0_PRE], T.R8[:], T.q8f[:, 0:X0_PRE], True, True)
+        if X0_PRE == 512:
+            p_x0 = incs(p_x0)
+    W("v", t_ge0, p_sp, t_qt)
+    t_ge = incs(*[v.tensor_scalar(T.GE[:, r, 1:33], T.qT[:], T.pS[:, r:r + 1], None, A.is_ge) for r in (1, 2, 3)])
     now, nxt, now0, nxt0 = T.GE[:, 0:4, 1:33], T.GE[:, 1:5, 1:33], T.GE[:, 0:4, 0:32], T.GE[:, 1:5, 0:32]
     W("t", t_ge0, s_bm, c_nl, t_ge)
     for wt, x in ((T.BD, now0), (T.BDm, nxt0), (T.NL, now), (T.NL, nxt0)):
@@ -185,70 +240,65 @@ def rank_program(g, core, T, topo):
     W("t", s_nl)
     te.matmul(T.pN[:, 0:128], T.NLm[:], nxt, False, False)
     p_e = incs(te.matmul(T.pN[:, 0:128], T.NLm[:], now0, False, True))
+    if X0_PE and X0_PRE < 512:
+        W("t", s_q8, *t_q8)
+        p_x0 = incs(te.matmul(T.pD[:, X0_PRE:512], T.R8[:], T.q8f[:, X0_PRE:512], True, True))
     W("t", t_ones)
     p_io = incs(te.matmul(T.p2[:, 0:1], T.NL[:], T.ones[:, 0:1], True, True))
-    W("s", d_b0)
-    s_b0 = incs(s.activation(T.b0f[:], T.b0i[:], F.Copy))
     W("t", s_b0)
     p_b0 = incs(te.matmul(T.p1[:, 0:2], T.R8[:], T.b0f[:], True, True))
-    t_w0 = incs(v.memset(T.WW[:], 0.0))
+    for n in FILL_S[1:X0_AT]:
+        fill("s", n)
+    if X0_PE:
+        W("s", p_x0)
+        d_x0 = incs(s.activation(T.X0[:], T.pD[:], F.Copy), on=p_x0)
+    t_sx0 += [incs(v.memset(T.QS[:, 480 + FILL_Q[0]:480 + FILL_Q[1]], 0))]
     W("v", t_ge)
     t_mk = incs(v.tensor_tensor(T.MK[:], now, nxt, A.subtract))
     Wk, Wc = T.WW[:, 0:144], T.WW[:, 144:288]
-    c = sel(T.wt[:, 0:9], T.ones[:, 0:9], [[-16, 9]], A.is_ge, -1, 1)
-    c_wk = sel(Wk[:, 15:144:16], T.ones[:, 0:9], [[-16, 9]], A.is_equal, 0, 1, t_w0)
-    c_wc = sel(Wc[:, 15:144:16], T.wt[:, 0:9], [[16, 9]], A.is_ge, 15, -1, c)
     W("v", t_rst, p_e)
     t_u = incs(v.tensor_tensor_scan(T.pT[:, 0:128], T.RST[:], T.pN[:, 0:128], 0.0, A.mult, A.add))
     t_sx0 += [incs(v.memset(T.QS[:, 480 + FILL_Q[1]:1120], 0))]
     fill("v", FILL_V[0])
     W("v", t_mk, t_u)
     t_val = incs(v.tensor_tensor(T.VAL[:], T.MK[:], T.pT[:, 0:128], A.mult))
-    fill("v", FILL_V[1])
-    W("v", t_val)
-    t_tt = incs(v.transpose(T.TT[:], T.VAL[:]))
-    fill("v", FILL_V[2])
-    W("t", c_d0, c_d1, t_tt)
-    p_a = []
-    for w in range(2):
-        for r in range(4):
-            for gg in range(2):
-                sh = 160 * w + 16 + 16 * (w - gg)
-                ins = te.matmul(T.pA[:, w:32:2], T.D01[:, sh:sh + 128], T.TT[:, 32 * r + 16 * gg:32 * r + 16 * gg + 16], r + gg == 0, r + gg == 4)
-        p_a.append(ins)
-    p_a = incs(*p_a)
+    fill("v", FILL_V[1], True)
+    W("t", c_id, t_val)
+    p_a = incs([te.matmul(T.pA[:, 0:32], T.ID[:], T.VAL[:, 32 * r:32 * r + 32], r == 0, r == 3) for r in range(4)][-1])
     W("v", p_a)
     t_la = incs(v.tensor_copy(T.LA[:], T.pA[:, 0:32]))
-    fill("v", FILL_V[3])
-    W("v", d_x0, *t_sx0, t_la)
+    t_w0 = incs(v.memset(T.WW[:], 0.0))
+    c = sel(T.wt[:, 0:9], T.ones[:, 0:9], [[-16, 9]], A.is_ge, -1, 1)
+    c_wc = sel(Wc[:, 15:144:16], T.wt[:, 0:9], [[16, 9]], A.is_ge, 15, -1, c, t_w0)
+    c_wk = sel(Wk[:, 15:144:16], T.ones[:, 0:9], [[-16, 9]], A.is_equal, 0, 1)
+    W("v", d_x0, t_la, *t_sx0)
     t_sc = incs(v.tensor_copy(SX.indirect(T.LA[:, 0:32]), T.X0[:]))
-    for r in range(4):
-        te.matmul(T.pB[:, 0:32], T.D01[:, 16:144], T.VAL[:, 32 * r:32 * r + 32], r == 0, False)
-        ins = te.matmul(T.pB[:, 0:32], T.D01[:, 176:304], T.VAL[:, 32 * r:32 * r + 32], False, r == 3)
-    p_lb = incs(ins)
 
-    fill("s", FILL_S[2])
+    for n in FILL_S[X0_AT:LATE_AT]:
+        fill("s", n)
+    for n in FILL_S[LATE_AT:]:
+        fill("s", n, True)
+    for a, b in ((MID, 8192), (4096, MID)):
+        qs = "yyy" if a == MID else LATE_Q
+        for q in set(qs):
+            W(q, t_z0, *[tk for lo, hi, tk in z if lo < b and hi > a])
+        d_w.append(dmas((queues[qs[0]], T.W[0::16, a:b], T.kid[:, a:b]), *[(queues[qs[o - 13]], T.W[o::16, a:b], T.beg[:, a - 4096:b - 4096]) for o in (14, 15)],
+                        *[(sy, T.W[o::st, 0:4096], T.nk[o::st, :]) for o, st in NK_LATE if a == MID]))
     W("s", t_ones, p_io)
     s_io = incs(s.activation(T.ioI[:], T.p2[:, 0:1], F.Copy, bias=-8192.0), s.activation(T.onef[:], T.ones[:, 0:1], F.Copy))
     c = incs(s.activation(T.mku[:], T.p2[:, 0:1], F.Relu, bias=14.0, scale=-1.0), s.activation(T.mkt[:], T.p2[:, 0:1], F.Copy, bias=-4110.5),
              s.activation(T.ioB[:], T.p2[:, 0:1], F.Copy, bias=2 * HALF))
     s_mk = incs(s.activation(T.mk0[:], T.p2[:, 0:1], F.Relu, bias=1.0, scale=-1.0))
-    fill("s", FILL_S[3])
+    W("s", t_la)
+    s_sl = incs(s.activation(T.SL[:], T.LA[:], F.Copy))
     W("s", c, s_io, p_b0)
     c = incs(s.activation(T.mkb[:], T.mku[:], F.Relu, bias=0.5, scale=-1.0), on=c)
     e = incs(s.activation(T.e0[:], T.p1[:, 0:1], F.Identity, bias=T.ioI[:, 0:1]))
-    fill("s", FILL_S[4])
+    W("s", c_wc)
+    s_16 = incs(s.activation(T.W16[:], Wc, F.Copy, scale=16.0))
     W("s", c, e)
     s_bi = incs(s.activation(T.bib[:], T.mkt[:], F.Copy, scale=T.mkb[:, 0:1]), on=c)
     s_l16 = incs(s.activation(T.L16[:], T.BD[:, 0:128:16], F.Copy, bias=8192.0, scale=T.e0[:, 0:1]), on=e)
-    W("s", p_lb)
-    s_lb = incs(s.activation(T.LB[:], T.pB[:, 0:32], F.Copy), on=p_lb)
-    W("s", c_wc)
-    s_16 = incs(s.activation(T.W16[:], Wc, F.Copy, scale=16.0))
-    for a, b in ((4096, MID), (MID, 8192)):
-        W("y", t_z0, *[tk for lo, hi, tk in z if lo < b and hi > a])
-        d_w.append(dmas((sy, T.W[0::16, a:b], T.kid[:, a:b]), *[(sy, T.W[o::16, a:b], T.beg[:, a - 4096:b - 4096]) for o in (14, 15)],
-                        *[(sy, T.W[o::st, 0:4096], T.nk[o::st, :]) for o, st in NK_LATE if a == 4096]))
 
     W("g", t_sc)
     exchange(lambda k: SX[:, CAP * k:CAP * k + CAP], lambda k: T.QS[:, CAP * k - CAP:CAP * k], "rq")
@@ -256,54 +306,69 @@ def rank_program(g, core, T, topo):
     W("v", t_k1, t_sc)
 
     def level1(k, u, n):
-        return v.tensor_scalar(T.cm1[:, CAP * k + u:CAP * k + CAP:n], SX[:, CAP * k + u:CAP * k + CAP:n], T.K1A[:, 4 * k:4 * k + 1], None, A.is_ge)
+        return v.tensor_scalar(T.cm1[:, CAP * k + u:CAP * k + CAP:n], SX[:, CAP * k + u:CAP * k + CAP:n], T.K1A[:, 4 * k:4 * k + 1],
+                               -2.0 if k else 1.0, A.is_ge, A.mult)
 
-    t_c1 = [incs(*[level1(k, u, 2) for k in (1, 2, 3)]) for u in range(2)]
+    nv = 3 - L1_S
+    t_c1 = [incs(*[level1(k, u, 2) for k in range(1, nv + 1)]) for u in range(2)]
     t_c0 = incs(level1(0, 0, 1))
     W("t", c_wc, t_ge)
-    p_c1 = incs(conv(T.pS[:, 0:30], Wc, lambda i: T.cm1[:, CAP + i:640:16], before=lambda i: [t_c1[i % 2]], turn=[*range(0, 16, 2), *range(1, 16, 2)]))
+    if L1_S:
+        arrived(s, "rk")
+        W("s", t_sc)
+        c = incs(s.activation(T.cm1[:, 480:640], SX[:, 480:640], F.Sign, bias=T.K1A[:, 12:13], scale=-1.0))
+        W("t", c, t_c1[0])
+    conv(T.pS[:, 0:30], Wc, lambda i: T.cm1[:, CAP + i:640:16], True, False, turn=range(0, 16, 2))
+    te.matmul(T.pS[:, 0:20], T.BD[:], T.ones[:, 0:20], False, False)
+    W("t", t_c1[1])
+    p_c1 = incs(conv(T.pS[:, 0:30], Wc, lambda i: T.cm1[:, CAP + i:640:16], False, True, turn=range(1, 16, 2)))
     W("v", p_c1)
-    t_l1 = incs(v.tensor_copy(T.l1s[:, 10:40], T.pS[:, 0:30]), on=p_c1)
+    for k in range(DELAY_Q):
+        W("v", incs(v.tensor_copy(T.sm1[:, k:k + 1], T.ones[:, 0:1])))
+    t_l1 = incs(v.tensor_scalar(T.l1s[:, 10:40], T.pS[:, 0:30], -0.5, 7.75, A.mult, A.add), on=p_c1)
     W("g", t_l1)
     exchange(lambda k: T.l1s[:, 10 * k:10 * k + 10], lambda k: T.l1[:, 10 * k - 10:10 * k], "rl")
+    W("v", s_sl)
+    t_tt = incs(v.transpose(T.TT[:], T.SL[:]))
+    c_e = [sel(T.E01[:, 160 * h:160 * h + 160], T.ones[:], [[-32, 5], [1000, 2], [-2, 16]], A.is_equal, -1000 - h, 1) for h in range(2)]
     arrived(sy, "rl")
     d_vec = dmas((sy, T.vcs[:], T.vec[:]))
 
-    B = {"f": (0, 512, T.pD, "f"), "o": (512, 640, T.pN, "o")}
+    B = {"f": (0, 480, T.pD, "f"), "o": (480, 640, T.pN, "o"), "a": (0, 256, T.pD, "a"), "b": (256, 480, T.pT, "b")}
     tok = {}
 
     def cols(x, b):
         return x[:, b[0]:b[1]]
 
-    def lst(x, b):
-        return x[:, b[0] // 16:b[1] // 16]
+    def wide(b, n):
+        return {"f": n, "o": 10, "a": 16, "b": n - 16}[b[3]]
 
-    def bank(b):
-        return b[2][:, 0:(b[1] - b[0]) // 16]
+    def lst(x, b, n=30):
+        a = 32 if b[3] == "o" else b[0] // 16
+        return x[:, a:a + wide(b, n)]
+
+    def bank(b, n=30):
+        return b[2][:, 0:wide(b, n)]
 
     def rhs(x, b, i):
-        return x[:, b[0] + i:b[1]:16] if b[3] == "o" else x[:, 32 * i:32 * i + 32]
+        return x[:, b[0] + i:b[1]:16] if b[3] == "o" else x[:, 32 * i:32 * i + 32] if b[3] == "f" else x[:, b[0] + 16 * i:b[0] + 16 * i + 16]
 
-    def lists(b, name, add):
+    def lists(b, name, add, n=30):
         W("v", tok["p", b])
-        tok[name, b] = incs(v.tensor_scalar(lst(T[name], b), bank(b), add, None, A.add), on=tok["p", b])
+        tok[name, b] = incs(v.tensor_scalar(lst(T[name], b, n), bank(b, n), add, None, A.add), on=tok["p", b])
 
     def c2(b):
-        parts = ((480, 512, T.l1s[:, 0:2]), (0, 480, T.l1[:, 0:30])) if b[3] == "f" else ((512, 640, T.l1s[:, 2:10]),)
+        l1 = lst(T.l1, b) if b[3] != "o" else T.l1s[:, 0:10]
         W("v", tok["l0"], tok["K2"])
-        c = []
-        for lo, hi, l1 in parts:
-            if lo == 0:
-                arrived(v, "rq")
-                arrived(v, "rl")
-            c.append(v.tensor_tensor(T.cm2[:, lo:hi], T.K2[:, 0:16].indirect(l1), T.QS[:, lo:hi], A.is_le))
-        c = incs(*c)
-        lb = incs(*[v.tensor_copy(T.l1b[:, lo // 16:hi // 16], l1) for lo, hi, l1 in parts])
-        W("t", t_u, s_16, c)
+        if b[3] in "fa":
+            arrived(v, "rq")
+            arrived(v, "rl")
+        c = incs(v.tensor_tensor(cols(T.cm2, b), T.K2[:, 0:16].indirect(l1), cols(T.QS, b), A.is_le))
+        lb = incs(v.tensor_copy(lst(T.l1b, b), l1))
+        W("t", t_val, s_16, c)
         conv(bank(b), T.W16, lambda i: T.cm2[:, b[0] + i:b[1]:16], True, False)
         W("t", lb)
-        te.matmul(bank(b), T.D01[:, 16:144], lst(T.l1b, b), False, False)
-        tok["p", b] = incs(te.matmul(bank(b), T.D01[:, 176:304], lst(T.l1b, b), False, True), on=c)
+        tok["p", b] = incs(te.matmul(bank(b), T.ID[:], lst(T.l1b, b), False, True), on=c)
 
     def starts(out, win, l):
         return s.activation(out, win.indirect(l), F.Identity, bias=T.bib[:, 0:1], scale=T.mkb[:, 0:1])
@@ -311,17 +376,19 @@ def rank_program(g, core, T, topo):
     def level(b, lin, win, nodes, C, S, *deps):
         W("s", *deps[:1], tok[lin, b])
         W("v", *deps[1:], tok[lin, b])
-        cut = (0, 16) if b[3] == "o" else CUT_L
-        n = (b[1] - b[0]) // 16
-        for lo, hi in zip(cut, cut[1:]):
-            c0, c1 = b[0] + n * lo, b[0] + n * hi
-            l = T[lin][:, c0 // 16:c1 // 16]
-            x = incs(starts(S[:, c0:c1], win, l))
-            y = incs(v.tensor_tensor(C[:, c0:c1], nodes.indirect(l), T.QS[:, c0:c1], A.is_le), on=tok[lin, b] if lo == 0 else None)
-            W("t", y)
-            conv(bank(b), Wc, lambda i: rhs(C, b, i), lo == 0, False, turn=range(lo, hi))
+        parts = []
+        for u, cut in enumerate({"o": ((0, 16), (0, 16)), "f": (CUT_L, CUT_S), "a": CUT_A, "b": CUT_B}[b[3]]):
+            for lo, hi in zip(cut, cut[1:]):
+                c0, c1 = (32 * lo, 32 * hi) if b[3] == "f" else b[0:2] if b[3] == "o" else (b[0] + 16 * lo, b[0] + 16 * hi)
+                l = lst(T[lin], b) if b[3] == "o" else T[lin][:, c0 // 16:c1 // 16]
+                x = incs(starts(S[:, c0:c1], win, l)) if u else incs(v.tensor_tensor(C[:, c0:c1], nodes.indirect(l), T.QS[:, c0:c1], A.is_le), on=tok[lin, b] if lo == 0 else None)
+                parts.append((hi, -lo, x, (C, S)[u]))
+                if u == 0 and b[3] == "f" and hi == cut[-2] and lin in INSIDE:
+                    steps[lin](B["o"])
+        parts.sort(key=lambda p: (p[0], -p[1]))
+        for k, (hi, lo, x, Z) in enumerate(parts):
             W("t", x)
-            ins = conv(bank(b), Wc, lambda i: rhs(S, b, i), False, hi == 16, turn=range(lo, hi))
+            ins = conv(bank(b, 32), Wc, lambda i: rhs(Z, b, i), k == 0, k == len(parts) - 1, turn=range(-lo, hi))
         tok["p", b] = incs(ins, on=x)
 
     def kid_s(out, l):
@@ -337,32 +404,50 @@ def rank_program(g, core, T, topo):
         if b[3] == "f":
             W("v", s_mk, tok[lin, b])
             c = [[incs((kid_v, kid_s)[u](G[:, 32 * lo + u:32 * hi:2], L[:, 16 * u + lo:16 * u + hi])) for u in range(2)] for lo, hi in zip(CUT_K, CUT_K[1:])]
-            tok["p", b] = incs(conv(bank(b), Wk, lambda i: rhs(G, b, i), before=lambda i: c[max(k for k in range(len(CUT_K)) if CUT_K[k] <= i)]), on=c[-1][1])
+            tok["p", b] = incs(conv(bank(b), Wk, lambda i: G[:, 32 * i:32 * i + 30], before=lambda i: c[max(k for k in range(len(CUT_K)) if CUT_K[k] <= i)]), on=c[-1][1])
             return
-        c = incs(kid_s(cols(G, b), lst(L, b)), on=tok[lin, b])
+        if b[3] != "o":
+            a, m = b[0], b[0] + 16 * KV
+            W("v", s_mk, tok[lin, b])
+            c = [incs(kid_v(G[:, a:m], L[:, a // 16:m // 16]), on=tok[lin, b]), incs(kid_s(G[:, m:a + 256], L[:, m // 16:a // 16 + 16]))]
+            tok["p", b] = incs(conv(bank(b), Wk, lambda i: G[:, a + 16 * i:a + 16 * i + wide(b, 30)], before=lambda i: [c[i >= KV]]), on=c[1])
+            return
+        c = incs(kid_s(G[:, 512:672], lst(L, b)), on=tok[lin, b])
         W("t", c)
-        tok["p", b] = incs(conv(bank(b), Wk, lambda i: rhs(G, b, i)), on=c)
+        tok["p", b] = incs(conv(bank(b), Wk, lambda i: G[:, 512 + i:672:16]), on=c)
 
     def vectors(b):
         win = T.vcs[:, 0:4096]
         W("s", d_vec, tok["vn", b])
-        mid = b[0] if b[3] == "o" else b[0] + 256
-        tok["ve", b] = [incs(s.activation(T.AR[:, mid:b[1]], win.indirect(T.vn[:, mid // 16:b[1] // 16]), F.Copy))]
-        if mid > b[0]:
-            W("v", d_vec, tok["vn", b])
-            tok["ve", b].append(incs(v.tensor_copy(T.AR[:, b[0]:mid], win.indirect(T.vn[:, b[0] // 16:mid // 16])), on=tok["vn", b]))
+        if b[3] == "o":
+            tok["ve", b] = [incs(s.activation(cols(T.AR, b), win.indirect(lst(T.vn, b)), F.Copy))]
+            return
+        W("v", d_vec, tok["vn", b])
+        if b[3] != "f":
+            m = b[0] + 128
+            tok["ve", b] = [incs(s.activation(T.AR[:, m:b[1]], win.indirect(T.vn[:, m // 16:b[1] // 16]), F.Copy)),
+                            incs(v.tensor_copy(T.AR[:, b[0]:m], win.indirect(T.vn[:, b[0] // 16:m // 16])), on=tok["vn", b])]
+            return
+        if RA2:
+            tok["ve", b] = [incs(v.tensor_copy(T.AR[:, 0:160], win.indirect(T.vn[:, 0:10])), s.activation(T.AR[:, 160:320], win.indirect(T.vn[:, 10:20]), F.Copy)),
+                            incs(v.tensor_copy(T.AR[:, 320:416], win.indirect(T.vn[:, 20:26])), s.activation(T.AR[:, 416:480], win.indirect(T.vn[:, 26:30]), F.Copy))]
+            return
+        tok["ve", b] = [incs(s.activation(T.AR[:, 256:480], win.indirect(T.vn[:, 16:30]), F.Copy)),
+                        incs(v.tensor_copy(T.AR[:, 0:256], win.indirect(T.vn[:, 0:16])), on=tok["vn", b])]
 
     steps = {"c2": c2, "l2": lambda b: lists(b, "l2", 0.0),
-             "L3": lambda b: level(b, "l2", T.b3w[:, 0:256], T.K3[:, 0:256], T.C3, T.S3, tok["b3"], tok["K3"]),
-             "i3": lambda b: lists(b, "i3", 2 * HALF), "k3": lambda b: kids(b, "i3", T.G3),
+             "L3": lambda b: level(b, "l2", T.b3w[:, 0:256], T.K3[:, 0:256], T.C3, T.S3, tok["b3"], *tok["K3"]),
+             "i3": lambda b: lists(b, "i3", 2 * HALF, 32), "k3": lambda b: kids(b, "i3", T.G3),
              "m4": lambda b: lists(b, "m4", HALF),
              "L4": lambda b: level(b, "m4", T.W[:, 4096:8192], T.W[:, 0:4096], T.C4, T.S4),
-             "i4": lambda b: lists(b, "i4", 2 * HALF), "k4": lambda b: kids(b, "i4", T.G4),
+             "i4": lambda b: lists(b, "i4", 2 * HALF, 32), "k4": lambda b: kids(b, "i4", T.G4),
              "vn": lambda b: lists(b, "vn", HALF), "ve": vectors}
 
     def table(x):
         if x == "a":
             W("s", s_l16, s_mk, *d_w)
+            for k in range(DELAY_W):
+                W("s", incs(s.activation(T.sm1[:, k:k + 1], T.ones[:, 0:1], F.Copy)))
             c = incs(s.activation(T.kgx[:], T.W[:, 0:8208].indirect(T.L16[:]), F.Copy, scale=T.mk0[:, 0:1]))
             W("t", c)
             tok["p_m2"] = incs(te.matmul(T.p2[:, 0:1], T.kgx[:], T.onef[:], True, True), on=c)
@@ -383,34 +468,48 @@ def rank_program(g, core, T, topo):
             W("s", tok["p_b2"])
             c = incs(s.activation(T.L256[:], T.p1[:, 0:16], F.Identity, bias=T.ioB[:, 0:1]), on=tok["p_b2"])
             W("s", c)
-            c = [incs(kid_s(T.kg256[:, 16 * lo:16 * hi], T.L256[:, lo:hi])) for lo, hi in ((0, 10), (10, 16))]
+            c = [incs(kid_s(T.kg256[:, 16 * lo:16 * hi], T.L256[:, lo:hi])) for lo, hi in ((0, KG), (KG, 16))]
             W("t", c_wk)
-            tok["p_m3"] = incs(conv(T.p2[:, 0:16], Wk, lambda i: T.kg256[:, 16 * i:16 * i + 16], before=lambda i: [c[i >= 10]]))
+            tok["p_m3"] = incs(conv(T.p2[:, 0:16], Wk, lambda i: T.kg256[:, 16 * i:16 * i + 16], before=lambda i: [c[i >= KG]]))
         if x == "d":
             W("s", tok["p_m3"])
             tok["LM3"] = incs(s.activation(T.LM3[:], T.p2[:, 0:16], F.Copy, bias=HALF), on=tok["p_m3"])
             W("s", tok["LM3"])
             tok["b3"] = incs(s.activation(T.b3w[:], T.W[:, 4096:8192].indirect(T.LM3[:, 0:16]), F.Copy))
-        if x == "e":
+            tok["K3"] = [incs(s.activation(T.K3[:, K3V:256], T.W[:, 0:4096].indirect(T.LM3[:, K3V // 16:16]), F.Copy))] if K3V < 256 else []
+        if x == "l":
+            W("t", t_tt, *c_e)
+            c = incs(*[te.matmul(T.pB[:, 16 * h:16 * h + 16], T.E01[:, 160 * h + 16 - 16 * u:160 * h + 144 - 16 * u], T.TT[:, 16 * u:16 * u + 16], u == 0, u == 1)
+                       for h in range(2) for u in range(2)][1::2])
+            W("s", c)
+            tok["LB"] = incs(s.activation(T.LB[:], T.pB[:, 0:32], F.Copy), on=c)
+        if x == "e" and K3V:
             W("v", tok["LM3"])
-            tok["K3"] = incs(v.tensor_copy(T.K3[:], T.W[:, 0:4096].indirect(T.LM3[:, 0:16])))
+            tok["K3"].append(incs(v.tensor_copy(T.K3[:, 0:K3V], T.W[:, 0:4096].indirect(T.LM3[:, 0:K3V // 16]))))
 
     for x in PLAN.split():
         if x == "send":
-            W("g", *tok["ve", B["f"]])
-            exchange(lambda k: T.AR[:, CAP * k - CAP:CAP * k], lambda k: RX[:, CAP * k:CAP * k + CAP], "ra")
+            if ("ve", B["a"]) in tok:
+                tok["ve", B["f"]] = tok["ve", B["a"]] + tok["ve", B["b"]]
+            for tk, to in zip(tok["ve", B["f"]], (others[:2], others[2:])) if RA2 else ((tok["ve", B["f"]][0], others),):
+                W("g", tk, *([] if RA2 else tok["ve", B["f"]]))
+                exchange(lambda k: T.AR[:, CAP * k - CAP:CAP * k], lambda k: RX[:, CAP * k:CAP * k + CAP], "ra", to)
         elif x[0] == "T":
             table(x[1])
         else:
             steps[x[:2]](B[x[2]])
 
-    W("v", s_lb, *tok["ve", B["o"]], *tok["ve", B["f"]])
-    W("s", s_lb, *tok["ve", B["o"]], *tok["ve", B["f"]])
+    W("v", tok["LB"], *tok["ve", B["o"]], *tok["ve", B["f"]])
+    W("s", tok["LB"], *tok["ve", B["o"]], *tok["ve", B["f"]])
     arrived(v, "ra")
     arrived(s, "ra")
-    for a in (0, 256):
-        W("y", incs(v.tensor_copy(T.yb[:, a:a + 128], RX.indirect(T.LB[:, a // 16:a // 16 + 8]))),
-          incs(s.activation(T.yb[:, a + 128:a + 256], RX.indirect(T.LB[:, a // 16 + 8:a // 16 + 16]), F.Copy)))
-        dmas((sy, T.y[:, a:a + 256], T.yb[:, a:a + 256]))
+    if STORE == 2:
+        for a in (0, 256):
+            W("y", incs(v.tensor_copy(T.yb[:, a:a + 128], RX.indirect(T.LB[:, a // 16:a // 16 + 8]))),
+              incs(s.activation(T.yb[:, a + 128:a + 256], RX.indirect(T.LB[:, a // 16 + 8:a // 16 + 16]), F.Copy)))
+            dmas((sy, T.y[:, a:a + 256], T.yb[:, a:a + 256]))
+    else:
+        W("y", incs(v.tensor_copy(T.yb[:, 0:256], RX.indirect(T.LB[:, 0:16])), s.activation(T.yb[:, 256:512], RX.indirect(T.LB[:, 16:32]), F.Copy)))
+        dmas((sy, T.y[:], T.yb[:]))
     g.wait_ge(T.sem.left, sum(sent))
     W("g", *[t for t in every if t not in waited])

@@ -2,7 +2,7 @@ from concourse.bass import DstId, RemoteDMATransfer
 from concourse.mybir import dt, AluOpType, AxisListType, ActivationFunctionType
 
 CAP = 160
-NS = 145
+NS = 140
 HALF = 2048.0
 
 SCRATCH = {
@@ -16,62 +16,49 @@ SCRATCH = {
     "R8": ("sbuf", [8, 128], "float32"),
     "GE": ("sbuf", [128, 5, 33], "bfloat16"),
     "CB": ("sbuf", [128, 4, 32], "bfloat16"),
-    "RST": ("sbuf", [128, 128], "bfloat16"),
 }
 for _dt, _bufs in (
     ("int32", "ql 32 qT 32 X0 512 W 8208 k1i 2 QS 1120 K2 16 K3 256 b3w 256"),
-    ("float32", "K1A 16 kgx 128 onef 1 e0 1 ioI 1 ioB 1 mk0 1 mka 1 mku 1 mkb 1 mkt 1 bib 1"),
-    ("bfloat16", "vcs 4096 ones 160 src 512 BD 128 BDm 128 NL 128 NLm 128 E01 320 ID 128 WW 288 W16 144 MK 128 wt 16 cm1 640 cm2 640 l1b 42 AR 1120 yb 512"),
-    ("float16", "VAL 128 TT 32 SL 32 b2 16 C3 640 S3 640 C4 640 S4 640 kg256 256 G3 672 G4 672 sm1 10"),
-    ("uint16", "LA 32 LB 32 L16 8 LM2 2 L256 16 LM3 16 l1s 40 l1 32 l2 42 i3 42 m4 42 i4 42 vn 42"),
+    ("float32", "K1A 16 kgx 128 onef 1 e0 1 ioI 1 ioB 1 mk0 1 mku 1 mkb 1 mkt 1 bib 1"),
+    ("bfloat16", "vcs 4096 ones 160 RST 128 BD 128 BDm 128 NL 128 NLm 128 E01 320 ID 128 WW 288 W16 144 MK 128 wt 16 cm1 640 cm2 640 "
+                 "l1b 40 AR 1120 yb 512"),
+    ("float16", "VAL 128 TT 32 SL 32 b2 16 C3 640 S3 640 C4 640 S4 640 kg256 256 G3 640 G4 640"),
+    ("uint16", "LA 32 LB 32 L16 8 LM2 2 L256 16 LM3 16 l1s 40 l1 32 l2 40 i3 40 m4 40 i4 40 vn 40"),
 ):
     _w = _bufs.split()
     for _k in range(0, len(_w), 2):
         SCRATCH[_w[_k]] = ("sbuf", [128, int(_w[_k + 1])], _dt)
 for _k in "pS pT pN pA p1 p2 pB pD".split():
     SCRATCH[_k] = ("psum", [128, 512], "float32")
-SEMAPHORES = ["s%d" % i for i in range(NS)] + ["rk", "rq", "rl", "ra", "left"]
+SEMAPHORES = ["s%d" % i for i in range(NS)] + ["rk", "rq", "rl", "rqn", "rln", "ra", "left"]
 
 A = AluOpType
 F = ActivationFunctionType
 
-PLAN = """Ta Tb c2o Tc c2a c2b Td Te l2a l2o l2b L3a L3b L3o i3a k3a i3b i3o k3b k3o m4a L4a m4b m4o L4b
- i4a L4o k4a i4b k4b vna i4o vea vnb k4o veb send Tl vno veo"""
+PLAN = """Ta Tb c2o Tc c2a c2b c2c Td l2a Te l2b L3a l2c L3b l2o L3c i3a L3o i3b k3a i3c k3b i3o k3c m4a k3o m4b L4a m4c L4b
+ m4o L4c i4a L4o i4b k4a i4c k4b i4o k4c vna k4o vnb vea senda vnc veb sendb vno vec sendc Tl veo"""
+CUTS = (0, 160, 320, 480)
+KV = (64, 64, 64, 64)
+VV = (64, 64, 64, 64)
+LS = "l2b l2o m4a m4b m4o"
+KGV = 6
+NEAR = ()
+ALONE = ("ra",)
+NEAR_STEP = 1
 QL_Q = "sysysysy"
-G_FIRST = 0
-CUT_L = (0, 7, 12, 15)
-CUT_S = (0, 7, 12, 15)
-CUT_K = (0, 10, 16)
-NK_LATE = [(4, 8), (8, 16)]
 NK = [(1, 2), (2, 4)]
+NK_LATE = [(4, 8), (8, 16)]
 FILL_0 = (160, 160)
-FILL_S = (224, 512, 416, 448)
+FILL_S = (224, 192, 512, 416, 448)
 FILL_E = 512
-K3V = 256
-X0_AT = 3
-LATE_AT = 3
-X0_PE = 1
-X0_S = 0
-NK_PRE = 1
-FILL_1 = 192
-STORE = 1
-X0_PRE = 256
 FILL_G = 832
 FILL_V = (128, 512)
 FILL_Q = (256, 512)
-LATE_Q = "yys"
-L1_S = 1
-RA2 = 0
+X0_PRE = 256
 Q8_S = 320
-DELAY_W = 0
-DELAY_Q = 0
-KG = 12
-KV = 8
-CUT_A = ((0, 10, 16), (0, 10, 16))
-CUT_B = ((0, 10, 14), (0, 10, 14))
-FILL_D = 0
-NK_WAIT = 0
-INSIDE = ()
+LATE_Q = "yys"
+K3V = 160
+KG = 8
 
 
 def rank_program(g, core, T, topo):
@@ -118,16 +105,19 @@ def rank_program(g, core, T, topo):
     others = order(me)
     place = {r: k for k, r in enumerate([me] + others)}
 
-    def engines_of(src, dst):
+    def engines_of(src, dst, sem):
         away = [d for d in T.cores if topo.chip(d) != topo.chip(src)]
         ae = topo.engines(src, away[0])
         if dst in away:
             n = len(ae) // len(away)
-            return ae[away.index(dst) * n:away.index(dst) * n + n]
-        return [e for e in topo.engines(src, dst) if e not in ae][::2]
+            return ae if sem in ALONE else ae[away.index(dst) * n:away.index(dst) * n + n]
+        return [e for e in topo.engines(src, dst) if e not in ae][::NEAR_STEP]
+
+    def near(x, y, sem):
+        return sem + "n" if sem in NEAR and topo.chip(T.cores[x]) == topo.chip(T.cores[y]) else sem
 
     def arrived(q, sem):
-        q.wait_ge(T.sem[sem], sum(len(engines_of(T.cores[r], core)) for r in others))
+        q.wait_ge(T.sem[sem], sum(len(engines_of(T.cores[r], core, sem[:2])) for r in others if near(r, me, sem[:2]) == sem))
 
     sent = []
 
@@ -136,36 +126,29 @@ def rank_program(g, core, T, topo):
         for r in others:
             d = T.cores[r]
             a = topo.addr(d)
-            tr.append(RemoteDMATransfer(dst_ids=[DstId(rid=a[0], pnc=a[1])], dma_engine_mask=sum(1 << e for e in engines_of(core, d)),
-                                        remote_sem=T.sem[sem], src=src(place[r]), dst=dst(1 + order(r).index(me))))
+            tr.append(RemoteDMATransfer(dst_ids=[DstId(rid=a[0], pnc=a[1])], dma_engine_mask=sum(1 << e for e in engines_of(core, d, sem)),
+                                        remote_sem=T.sem[near(r, me, sem)], src=src(place[r]), dst=dst(1 + order(r).index(me))))
         g.remote_dma_fused(tr, local_sem=T.sem.left)
-        sent.append(sum(len(engines_of(core, T.cores[r])) for r in others))
+        sent.append(sum(len(engines_of(core, T.cores[r], sem)) for r in others))
 
     SX = T.QS[:, 480:1120]
     RX = T.AR[:, 480:1120]
 
     d_sp = dmas((s, T.spi[:], T.spl[:]))
-    if X0_PE:
-        d_q8 = dmas((sy, T.q8i[:], T.q[:]))
+    d_q8 = dmas((sy, T.q8i[:], T.q[:]))
     d_ql = dmas(*[(queues[QL_Q[G]], T.ql[32 * (G // 2):32 * (G // 2) + 32, 16 * (G % 2):16 * (G % 2) + 16], T.q[16 * G:16 * G + 16, :]) for G in range(8)])
     d_k1 = dmas((sy, T.k1i[:], T.nk[:, 0:2]))
     d_b0 = dmas((sy, T.b0i[:], T.beg[:, 0:2]))
-    d_w = [dmas((sy, T.W[0::16, 0:4096], T.kid[:, 0:4096]), *[(sy, T.W[o::st, 0:4096], T.nk[o::st, :]) for o, st in NK[:NK_PRE]])]
-    if not X0_PE:
-        d_x0 = dmas(*[(s if o < X0_S else sy, T.X0[o::16, :], T.q[:]) for o in range(16)])
-    if not NK_WAIT:
-        d_w += [dmas(*[(sy, T.W[o::st, 0:4096], T.nk[o::st, :]) for o, st in NK[NK_PRE:]])]
+    d_w = [dmas((sy, T.W[0::16, 0:4096], T.kid[:, 0:4096]), *[(sy, T.W[o::st, 0:4096], T.nk[o::st, :]) for o, st in NK])]
 
     t_ones = incs(v.memset(T.ones[:], 1.0))
-    t_src = t_z0 = incs(v.memset(T.W[:, 8192 - FILL_E:8208], 0))
+    t_z0 = incs(v.memset(T.W[:, 8192 - FILL_E:8208], 0))
     t_rst = incs(v.memset(T.GE[:], 0.0), v.memset(T.CB[:], 0.0), v.memset(T.RST[:], 1.0))
     t_sx0 = [incs(v.memset(T.QS[:, 480:480 + FILL_Q[0]], 0))]
     z = []
-    MID = 4096 + FILL_G + FILL_V[-1] + sum(FILL_S[LATE_AT:])
-    ends = {False: MID + FILL_D, True: 4096}
-    assert FILL_1 + sum(FILL_0 + FILL_S + FILL_V) + FILL_G + FILL_E + FILL_D == 4096
-    if FILL_D:
-        d_w.append(dmas(*[(sy, T.W[o::st, MID:MID + FILL_D], T.nk[o::st, 0:FILL_D]) for o, st in ((1, 2), (2, 4), (8, 16))]))
+    MID = 4096 + FILL_G + FILL_V[-1] + FILL_S[-1]
+    ends = {False: MID, True: 4096}
+    assert sum(FILL_0 + FILL_S + FILL_V) + FILL_G + FILL_E == 4096
 
     def fill(q, n, late=False):
         a = ends[late]
@@ -186,15 +169,14 @@ def rank_program(g, core, T, topo):
     W("s", t_ones)
     for n in FILL_0:
         fill("s", n)
-    W("s", t_src)
+    W("s", t_z0)
     fill("s", FILL_S[0])
     W("s", p_bd)
     s_bd = incs(s.activation(T.BD[:], T.pB[:, 0:128], F.Copy))
     s_bm = incs(s.activation(T.BDm[:], T.pB[:, 0:128], F.Copy, scale=-1.0))
-    if X0_PE:
-        W("s", d_q8)
-        s_q8 = incs(s.activation(T.q8f[:, 0:Q8_S], T.q8i[:, 0:Q8_S], F.Copy))
-    fill("s", FILL_1)
+    W("s", d_q8)
+    s_q8 = incs(s.activation(T.q8f[:, 0:Q8_S], T.q8i[:, 0:Q8_S], F.Copy))
+    fill("s", FILL_S[1])
     c_id = sel(T.ID[:], T.ones[:, 0:128], [[-1, 128]], A.is_equal, 0, 1)
     c_nl = sel(T.NL[:], T.BD[:], [[1, 128]], A.is_gt, 0, -1, s_bd)
     W("s", c_nl)
@@ -203,60 +185,50 @@ def rank_program(g, core, T, topo):
     s_b0 = incs(s.activation(T.b0f[:], T.b0i[:], F.Copy))
 
     W("v", t_rst)
-    t_rst = t_ge0 = incs(v.memset(T.RST[:, 0:128:32], 0.0), v.memset(T.GE[:, 0, 1:33], 1.0), on=t_rst)
+    t_rst = incs(v.memset(T.RST[:, 0:128:32], 0.0), v.memset(T.GE[:, 0, 1:33], 1.0), on=t_rst)
     W("v", d_sp)
     t_spf = incs(v.tensor_copy(T.spf[:], T.spi[:]))
     t_cb = incs(*[v.memset(T.CB[:, r, 0:1], CAP / 16 * place[r]) for r in others])
-    t_q8 = []
-    if X0_PE and Q8_S < 512:
-        W("v", d_q8)
-        t_q8 = [incs(v.tensor_copy(T.q8f[:, Q8_S:512], T.q8i[:, Q8_S:512]))]
+    W("v", d_q8)
+    t_q8 = incs(v.tensor_copy(T.q8f[:, Q8_S:512], T.q8i[:, Q8_S:512]))
     W("v", d_ql)
     t_qt = incs(v.transpose(T.qT[:], T.ql[:]))
     W("v", d_k1)
     t_k1 = incs(v.tensor_copy(T.K1A[:, 0:2], T.k1i[:]))
-    if NK_WAIT:
-        W("y", t_k1)
-        d_w += [dmas(*[(sy, T.W[o::st, 0:4096], T.nk[o::st, :]) for o, st in NK[NK_PRE:]])]
-    fill("g", G_FIRST, True)
     W("g", t_k1)
     exchange(lambda k: T.K1A[:, 0:2], lambda k: T.K1A[:, 4 * k:4 * k + 2], "rk")
-    fill("g", FILL_G - G_FIRST, True)
+    fill("g", FILL_G, True)
     W("t", t_spf, c_r8)
     p_sp = incs(te.matmul(T.pS[:, 0:4], T.R8[:], T.spf[:], True, True))
-    W("t", s_bd, t_cb)
+    W("t", s_bd, t_cb, t_rst)
     te.matmul(T.pN[:, 0:128], T.BD[:], T.CB[:], True, False)
-    if X0_PRE and X0_PE:
-        W("t", s_q8, *(t_q8 if X0_PRE > Q8_S else []))
-        p_x0 = te.matmul(T.pD[:, 0:X0_PRE], T.R8[:], T.q8f[:, 0:X0_PRE], True, True)
-        if X0_PRE == 512:
-            p_x0 = incs(p_x0)
-    W("v", t_ge0, p_sp, t_qt)
+    te.matmul(T.pN[:, 0:32], T.BD[:], T.GE[:, 0, 0:32], False, False)
+    W("t", s_q8)
+    te.matmul(T.pD[:, 0:X0_PRE], T.R8[:], T.q8f[:, 0:X0_PRE], True, True)
+    W("v", t_rst, p_sp, t_qt)
     t_ge = incs(*[v.tensor_scalar(T.GE[:, r, 1:33], T.qT[:], T.pS[:, r:r + 1], None, A.is_ge) for r in (1, 2, 3)])
-    now, nxt, now0, nxt0 = T.GE[:, 0:4, 1:33], T.GE[:, 1:5, 1:33], T.GE[:, 0:4, 0:32], T.GE[:, 1:5, 0:32]
-    W("t", t_ge0, s_bm, c_nl, t_ge)
-    for wt, x in ((T.BD, now0), (T.BDm, nxt0), (T.NL, now), (T.NL, nxt0)):
-        te.matmul(T.pN[:, 0:128], wt[:], x, False, False)
+    W("t", s_bm, c_nl)
+    te.matmul(T.pN[:, 0:32], T.NL[:], T.GE[:, 0, 1:33], False, False)
+    W("t", t_ge)
+    for wt, a, c0 in ((T.BD, 32, 0), (T.BDm, 0, 0), (T.NL, 32, 1), (T.NL, 0, 0)):
+        te.matmul(T.pN[:, a:a + 96], wt[:], T.GE[:, 1:4, c0:c0 + 32], False, False)
     W("t", s_nl)
-    te.matmul(T.pN[:, 0:128], T.NLm[:], nxt, False, False)
-    p_e = incs(te.matmul(T.pN[:, 0:128], T.NLm[:], now0, False, True))
-    if X0_PE and X0_PRE < 512:
-        W("t", s_q8, *t_q8)
-        p_x0 = incs(te.matmul(T.pD[:, X0_PRE:512], T.R8[:], T.q8f[:, X0_PRE:512], True, True))
+    te.matmul(T.pN[:, 0:96], T.NLm[:], T.GE[:, 1:4, 1:33], False, False)
+    p_e = incs(te.matmul(T.pN[:, 0:128], T.NLm[:], T.GE[:, 0:4, 0:32], False, True))
+    W("t", t_q8)
+    p_x0 = incs(te.matmul(T.pD[:, X0_PRE:512], T.R8[:], T.q8f[:, X0_PRE:512], True, True))
     W("t", t_ones)
     p_io = incs(te.matmul(T.p2[:, 0:1], T.NL[:], T.ones[:, 0:1], True, True))
     W("t", s_b0)
     p_b0 = incs(te.matmul(T.p1[:, 0:2], T.R8[:], T.b0f[:], True, True))
-    for n in FILL_S[1:X0_AT]:
+    for n in FILL_S[2:-1]:
         fill("s", n)
-    if X0_PE:
-        W("s", p_x0)
-        d_x0 = incs(s.activation(T.X0[:], T.pD[:], F.Copy), on=p_x0)
+    W("s", p_x0)
+    s_x0 = incs(s.activation(T.X0[:], T.pD[:], F.Copy), on=p_x0)
     t_sx0 += [incs(v.memset(T.QS[:, 480 + FILL_Q[0]:480 + FILL_Q[1]], 0))]
     W("v", t_ge)
-    t_mk = incs(v.tensor_tensor(T.MK[:], now, nxt, A.subtract))
-    Wk, Wc = T.WW[:, 0:144], T.WW[:, 144:288]
-    W("v", t_rst, p_e)
+    t_mk = incs(v.tensor_tensor(T.MK[:], T.GE[:, 0:4, 1:33], T.GE[:, 1:5, 1:33], A.subtract))
+    W("v", p_e)
     t_u = incs(v.tensor_tensor_scan(T.pT[:, 0:128], T.RST[:], T.pN[:, 0:128], 0.0, A.mult, A.add))
     t_sx0 += [incs(v.memset(T.QS[:, 480 + FILL_Q[1]:1120], 0))]
     fill("v", FILL_V[0])
@@ -268,37 +240,32 @@ def rank_program(g, core, T, topo):
     W("v", p_a)
     t_la = incs(v.tensor_copy(T.LA[:], T.pA[:, 0:32]))
     t_w0 = incs(v.memset(T.WW[:], 0.0))
+    Wk, Wc = T.WW[:, 0:144], T.WW[:, 144:288]
     c = sel(T.wt[:, 0:9], T.ones[:, 0:9], [[-16, 9]], A.is_ge, -1, 1)
     c_wc = sel(Wc[:, 15:144:16], T.wt[:, 0:9], [[16, 9]], A.is_ge, 15, -1, c, t_w0)
     c_wk = sel(Wk[:, 15:144:16], T.ones[:, 0:9], [[-16, 9]], A.is_equal, 0, 1)
-    W("v", d_x0, t_la, *t_sx0)
+    W("v", s_x0, t_la, *t_sx0)
     t_sc = incs(v.tensor_copy(SX.indirect(T.LA[:, 0:32]), T.X0[:]))
 
-    for n in FILL_S[X0_AT:LATE_AT]:
-        fill("s", n)
-    for n in FILL_S[LATE_AT:]:
-        fill("s", n, True)
+    fill("s", FILL_S[-1], True)
     for a, b in ((MID, 8192), (4096, MID)):
         qs = "yyy" if a == MID else LATE_Q
-        for q in set(qs):
+        for q in sorted(set(qs)):
             W(q, t_z0, *[tk for lo, hi, tk in z if lo < b and hi > a])
         d_w.append(dmas((queues[qs[0]], T.W[0::16, a:b], T.kid[:, a:b]), *[(queues[qs[o - 13]], T.W[o::16, a:b], T.beg[:, a - 4096:b - 4096]) for o in (14, 15)],
                         *[(sy, T.W[o::st, 0:4096], T.nk[o::st, :]) for o, st in NK_LATE if a == MID]))
     W("s", t_ones, p_io)
-    s_io = incs(s.activation(T.ioI[:], T.p2[:, 0:1], F.Copy, bias=-8192.0), s.activation(T.onef[:], T.ones[:, 0:1], F.Copy))
-    c = incs(s.activation(T.mku[:], T.p2[:, 0:1], F.Relu, bias=14.0, scale=-1.0), s.activation(T.mkt[:], T.p2[:, 0:1], F.Copy, bias=-4110.5),
-             s.activation(T.ioB[:], T.p2[:, 0:1], F.Copy, bias=2 * HALF))
-    s_mk = incs(s.activation(T.mk0[:], T.p2[:, 0:1], F.Relu, bias=1.0, scale=-1.0))
+    c = incs(s.activation(T.ioI[:], T.p2[:, 0:1], F.Copy, bias=-8192.0), s.activation(T.mku[:], T.p2[:, 0:1], F.Relu, bias=14.0, scale=-1.0))
+    s_mk = incs(s.activation(T.mkt[:], T.p2[:, 0:1], F.Copy, bias=-4110.5), s.activation(T.mk0[:], T.p2[:, 0:1], F.Relu, bias=1.0, scale=-1.0),
+                s.activation(T.ioB[:], T.p2[:, 0:1], F.Copy, bias=2 * HALF))
+    W("s", p_b0, c)
+    c = incs(s.activation(T.mkb[:], T.mku[:], F.Relu, bias=0.5, scale=-1.0), s.activation(T.e0[:], T.p1[:, 0:1], F.Identity, bias=T.ioI[:, 0:1]), on=c)
+    s_on = incs(s.activation(T.onef[:], T.ones[:, 0:1], F.Copy))
     W("s", t_la)
     s_sl = incs(s.activation(T.SL[:], T.LA[:], F.Copy))
-    W("s", c, s_io, p_b0)
-    c = incs(s.activation(T.mkb[:], T.mku[:], F.Relu, bias=0.5, scale=-1.0), on=c)
-    e = incs(s.activation(T.e0[:], T.p1[:, 0:1], F.Identity, bias=T.ioI[:, 0:1]))
-    W("s", c_wc)
-    s_16 = incs(s.activation(T.W16[:], Wc, F.Copy, scale=16.0))
-    W("s", c, e)
-    s_bi = incs(s.activation(T.bib[:], T.mkt[:], F.Copy, scale=T.mkb[:, 0:1]), on=c)
-    s_l16 = incs(s.activation(T.L16[:], T.BD[:, 0:128:16], F.Copy, bias=8192.0, scale=T.e0[:, 0:1]), on=e)
+    W("s", s_mk, c)
+    s_bi = incs(s.activation(T.bib[:], T.mkt[:], F.Copy, scale=T.mkb[:, 0:1]))
+    s_l16 = incs(s.activation(T.L16[:], T.BD[:, 0:128:16], F.Copy, bias=8192.0, scale=T.e0[:, 0:1]), on=c)
 
     W("g", t_sc)
     exchange(lambda k: SX[:, CAP * k:CAP * k + CAP], lambda k: T.QS[:, CAP * k - CAP:CAP * k], "rq")
@@ -309,22 +276,17 @@ def rank_program(g, core, T, topo):
         return v.tensor_scalar(T.cm1[:, CAP * k + u:CAP * k + CAP:n], SX[:, CAP * k + u:CAP * k + CAP:n], T.K1A[:, 4 * k:4 * k + 1],
                                -2.0 if k else 1.0, A.is_ge, A.mult)
 
-    nv = 3 - L1_S
-    t_c1 = [incs(*[level1(k, u, 2) for k in range(1, nv + 1)]) for u in range(2)]
+    t_c1 = [incs(*[level1(k, u, 2) for k in (1, 2)]) for u in range(2)]
     t_c0 = incs(level1(0, 0, 1))
-    W("t", c_wc, t_ge)
-    if L1_S:
-        arrived(s, "rk")
-        W("s", t_sc)
-        c = incs(s.activation(T.cm1[:, 480:640], SX[:, 480:640], F.Sign, bias=T.K1A[:, 12:13], scale=-1.0))
-        W("t", c, t_c1[0])
+    arrived(s, "rk")
+    W("s", t_sc)
+    c = incs(s.activation(T.cm1[:, 480:640], SX[:, 480:640], F.Sign, bias=T.K1A[:, 12:13], scale=-1.0))
+    W("t", c_wc, t_ge, c, t_c1[0])
     conv(T.pS[:, 0:30], Wc, lambda i: T.cm1[:, CAP + i:640:16], True, False, turn=range(0, 16, 2))
     te.matmul(T.pS[:, 0:20], T.BD[:], T.ones[:, 0:20], False, False)
     W("t", t_c1[1])
     p_c1 = incs(conv(T.pS[:, 0:30], Wc, lambda i: T.cm1[:, CAP + i:640:16], False, True, turn=range(1, 16, 2)))
     W("v", p_c1)
-    for k in range(DELAY_Q):
-        W("v", incs(v.tensor_copy(T.sm1[:, k:k + 1], T.ones[:, 0:1])))
     t_l1 = incs(v.tensor_scalar(T.l1s[:, 10:40], T.pS[:, 0:30], -0.5, 7.75, A.mult, A.add), on=p_c1)
     W("g", t_l1)
     exchange(lambda k: T.l1s[:, 10 * k:10 * k + 10], lambda k: T.l1[:, 10 * k - 10:10 * k], "rl")
@@ -334,40 +296,41 @@ def rank_program(g, core, T, topo):
     arrived(sy, "rl")
     d_vec = dmas((sy, T.vcs[:], T.vec[:]))
 
-    B = {"f": (0, 480, T.pD, "f"), "o": (480, 640, T.pN, "o"), "a": (0, 256, T.pD, "a"), "b": (256, 480, T.pT, "b")}
+    names = "abc"[:len(CUTS) - 1] + "o"
+    B = {x: (lo, hi, bank, k) for k, (x, lo, hi, bank) in enumerate(zip(names, CUTS, CUTS[1:] + (640,), (T.pD, T.pT, T.pS)[:len(CUTS) - 1] + (T.pN,)))}
+    own = B["o"]
     tok = {}
 
     def cols(x, b):
         return x[:, b[0]:b[1]]
 
-    def wide(b, n):
-        return {"f": n, "o": 10, "a": 16, "b": n - 16}[b[3]]
+    def lst(x, b):
+        return x[:, b[0] // 16:b[1] // 16]
 
-    def lst(x, b, n=30):
-        a = 32 if b[3] == "o" else b[0] // 16
-        return x[:, a:a + wide(b, n)]
+    def bank(b):
+        return b[2][:, 0:(b[1] - b[0]) // 16]
 
-    def bank(b, n=30):
-        return b[2][:, 0:wide(b, n)]
-
-    def rhs(x, b, i):
-        return x[:, b[0] + i:b[1]:16] if b[3] == "o" else x[:, 32 * i:32 * i + 32] if b[3] == "f" else x[:, b[0] + 16 * i:b[0] + 16 * i + 16]
-
-    def lists(b, name, add, n=30):
+    def lists(b, name, add):
+        if name + names[b[3]] in LS:
+            W("s", tok["p", b])
+            tok[name, b] = incs(s.activation(lst(T[name], b), bank(b), F.Copy, bias=add), on=tok["p", b])
+            return
         W("v", tok["p", b])
-        tok[name, b] = incs(v.tensor_scalar(lst(T[name], b, n), bank(b, n), add, None, A.add), on=tok["p", b])
+        tok[name, b] = incs(v.tensor_scalar(lst(T[name], b), bank(b), add, None, A.add), on=tok["p", b])
 
     def c2(b):
-        l1 = lst(T.l1, b) if b[3] != "o" else T.l1s[:, 0:10]
         W("v", tok["l0"], tok["K2"])
-        if b[3] in "fa":
-            arrived(v, "rq")
-            arrived(v, "rl")
-        c = incs(v.tensor_tensor(cols(T.cm2, b), T.K2[:, 0:16].indirect(l1), cols(T.QS, b), A.is_le))
-        lb = incs(v.tensor_copy(lst(T.l1b, b), l1))
-        W("t", t_val, s_16, c)
+        kind = "o" if b is own else "n" if NEAR and b[0] >= 2 * CAP else ""
+        if ("lb", kind) not in tok and b is not own:
+            arrived(v, "rq" + kind)
+            arrived(v, "rl" + kind)
+        c = incs(v.tensor_tensor(cols(T.cm2, b), T.K2[:, 0:16].indirect(T.l1s[:, 0:10] if b is own else lst(T.l1, b)), cols(T.QS, b), A.is_le))
+        if ("lb", kind) not in tok:
+            lo, hi = {"o": (30, 40), "n": (20, 30), "": (0, 20 if NEAR else 30)}[kind]
+            tok["lb", kind] = incs(v.tensor_copy(T.l1b[:, lo:hi], T.l1s[:, 0:10] if b is own else T.l1[:, lo:hi]))
+        W("t", t_val, t_l1, tok["W16"], c)
         conv(bank(b), T.W16, lambda i: T.cm2[:, b[0] + i:b[1]:16], True, False)
-        W("t", lb)
+        W("t", tok["lb", kind])
         tok["p", b] = incs(te.matmul(bank(b), T.ID[:], lst(T.l1b, b), False, True), on=c)
 
     def starts(out, win, l):
@@ -376,20 +339,12 @@ def rank_program(g, core, T, topo):
     def level(b, lin, win, nodes, C, S, *deps):
         W("s", *deps[:1], tok[lin, b])
         W("v", *deps[1:], tok[lin, b])
-        parts = []
-        for u, cut in enumerate({"o": ((0, 16), (0, 16)), "f": (CUT_L, CUT_S), "a": CUT_A, "b": CUT_B}[b[3]]):
-            for lo, hi in zip(cut, cut[1:]):
-                c0, c1 = (32 * lo, 32 * hi) if b[3] == "f" else b[0:2] if b[3] == "o" else (b[0] + 16 * lo, b[0] + 16 * hi)
-                l = lst(T[lin], b) if b[3] == "o" else T[lin][:, c0 // 16:c1 // 16]
-                x = incs(starts(S[:, c0:c1], win, l)) if u else incs(v.tensor_tensor(C[:, c0:c1], nodes.indirect(l), T.QS[:, c0:c1], A.is_le), on=tok[lin, b] if lo == 0 else None)
-                parts.append((hi, -lo, x, (C, S)[u]))
-                if u == 0 and b[3] == "f" and hi == cut[-2] and lin in INSIDE:
-                    steps[lin](B["o"])
-        parts.sort(key=lambda p: (p[0], -p[1]))
-        for k, (hi, lo, x, Z) in enumerate(parts):
-            W("t", x)
-            ins = conv(bank(b, 32), Wc, lambda i: rhs(Z, b, i), k == 0, k == len(parts) - 1, turn=range(-lo, hi))
-        tok["p", b] = incs(ins, on=x)
+        x = incs(v.tensor_tensor(cols(C, b), nodes.indirect(lst(T[lin], b)), cols(T.QS, b), A.is_le), on=tok[lin, b])
+        y = incs(starts(cols(S, b), win, lst(T[lin], b)))
+        W("t", x)
+        conv(bank(b), Wc, lambda i: C[:, b[0] + i:b[1]:16], True, False)
+        W("t", y)
+        tok["p", b] = incs(conv(bank(b), Wc, lambda i: S[:, b[0] + i:b[1]:16], False, True), on=y)
 
     def kid_s(out, l):
         return s.activation(out, T.W[:, 0:8192].indirect(l), F.Copy, bias=-HALF, scale=T.mk0[:, 0:1])
@@ -397,59 +352,38 @@ def rank_program(g, core, T, topo):
     def kid_v(out, l):
         return v.tensor_scalar(out, T.W[:, 0:8192].indirect(l), T.mk0[:, 0:1], -HALF, A.mult, A.add)
 
+    def shared(b, lin, out, n, on_v, on_s, *deps):
+        c = []
+        for q, lo, hi, f in (("v", b[0], b[0] + n, on_v), ("s", b[0] + n, b[1], on_s)):
+            if hi > lo:
+                W(q, *deps, tok[lin, b])
+                c.append(f(out[:, lo:hi], T[lin][:, lo // 16:hi // 16]))
+        return incs(*c)
+
     def kids(b, lin, G):
-        W("s", tok[lin, b])
-        W("t", c_wk)
-        L = T[lin]
-        if b[3] == "f":
-            W("v", s_mk, tok[lin, b])
-            c = [[incs((kid_v, kid_s)[u](G[:, 32 * lo + u:32 * hi:2], L[:, 16 * u + lo:16 * u + hi])) for u in range(2)] for lo, hi in zip(CUT_K, CUT_K[1:])]
-            tok["p", b] = incs(conv(bank(b), Wk, lambda i: G[:, 32 * i:32 * i + 30], before=lambda i: c[max(k for k in range(len(CUT_K)) if CUT_K[k] <= i)]), on=c[-1][1])
-            return
-        if b[3] != "o":
-            a, m = b[0], b[0] + 16 * KV
-            W("v", s_mk, tok[lin, b])
-            c = [incs(kid_v(G[:, a:m], L[:, a // 16:m // 16]), on=tok[lin, b]), incs(kid_s(G[:, m:a + 256], L[:, m // 16:a // 16 + 16]))]
-            tok["p", b] = incs(conv(bank(b), Wk, lambda i: G[:, a + 16 * i:a + 16 * i + wide(b, 30)], before=lambda i: [c[i >= KV]]), on=c[1])
-            return
-        c = incs(kid_s(G[:, 512:672], lst(L, b)), on=tok[lin, b])
-        W("t", c)
-        tok["p", b] = incs(conv(bank(b), Wk, lambda i: G[:, 512 + i:672:16]), on=c)
+        c = shared(b, lin, G, KV[b[3]], kid_v, kid_s, s_mk)
+        W("t", c_wk, c)
+        tok["p", b] = incs(conv(bank(b), Wk, lambda i: G[:, b[0] + i:b[1]:16]), on=c)
 
     def vectors(b):
         win = T.vcs[:, 0:4096]
-        W("s", d_vec, tok["vn", b])
-        if b[3] == "o":
-            tok["ve", b] = [incs(s.activation(cols(T.AR, b), win.indirect(lst(T.vn, b)), F.Copy))]
-            return
-        W("v", d_vec, tok["vn", b])
-        if b[3] != "f":
-            m = b[0] + 128
-            tok["ve", b] = [incs(s.activation(T.AR[:, m:b[1]], win.indirect(T.vn[:, m // 16:b[1] // 16]), F.Copy)),
-                            incs(v.tensor_copy(T.AR[:, b[0]:m], win.indirect(T.vn[:, b[0] // 16:m // 16])), on=tok["vn", b])]
-            return
-        if RA2:
-            tok["ve", b] = [incs(v.tensor_copy(T.AR[:, 0:160], win.indirect(T.vn[:, 0:10])), s.activation(T.AR[:, 160:320], win.indirect(T.vn[:, 10:20]), F.Copy)),
-                            incs(v.tensor_copy(T.AR[:, 320:416], win.indirect(T.vn[:, 20:26])), s.activation(T.AR[:, 416:480], win.indirect(T.vn[:, 26:30]), F.Copy))]
-            return
-        tok["ve", b] = [incs(s.activation(T.AR[:, 256:480], win.indirect(T.vn[:, 16:30]), F.Copy)),
-                        incs(v.tensor_copy(T.AR[:, 0:256], win.indirect(T.vn[:, 0:16])), on=tok["vn", b])]
+        tok["ve", b] = shared(b, "vn", T.AR, VV[b[3]], lambda o, l: v.tensor_copy(o, win.indirect(l)), lambda o, l: s.activation(o, win.indirect(l), F.Copy), d_vec)
 
     steps = {"c2": c2, "l2": lambda b: lists(b, "l2", 0.0),
              "L3": lambda b: level(b, "l2", T.b3w[:, 0:256], T.K3[:, 0:256], T.C3, T.S3, tok["b3"], *tok["K3"]),
-             "i3": lambda b: lists(b, "i3", 2 * HALF, 32), "k3": lambda b: kids(b, "i3", T.G3),
+             "i3": lambda b: lists(b, "i3", 2 * HALF), "k3": lambda b: kids(b, "i3", T.G3),
              "m4": lambda b: lists(b, "m4", HALF),
              "L4": lambda b: level(b, "m4", T.W[:, 4096:8192], T.W[:, 0:4096], T.C4, T.S4),
-             "i4": lambda b: lists(b, "i4", 2 * HALF, 32), "k4": lambda b: kids(b, "i4", T.G4),
+             "i4": lambda b: lists(b, "i4", 2 * HALF), "k4": lambda b: kids(b, "i4", T.G4),
              "vn": lambda b: lists(b, "vn", HALF), "ve": vectors}
 
     def table(x):
         if x == "a":
             W("s", s_l16, s_mk, *d_w)
-            for k in range(DELAY_W):
-                W("s", incs(s.activation(T.sm1[:, k:k + 1], T.ones[:, 0:1], F.Copy)))
             c = incs(s.activation(T.kgx[:], T.W[:, 0:8208].indirect(T.L16[:]), F.Copy, scale=T.mk0[:, 0:1]))
-            W("t", c)
+            W("s", c_wc)
+            tok["W16"] = incs(s.activation(T.W16[:], Wc, F.Copy, scale=16.0))
+            W("t", s_on, c)
             tok["p_m2"] = incs(te.matmul(T.p2[:, 0:1], T.kgx[:], T.onef[:], True, True), on=c)
             W("t", t_la, t_c0)
             c = incs(conv(T.pA[:, 0:10], Wc, lambda i: T.cm1[:, i:CAP:16]), on=t_c0)
@@ -468,7 +402,9 @@ def rank_program(g, core, T, topo):
             W("s", tok["p_b2"])
             c = incs(s.activation(T.L256[:], T.p1[:, 0:16], F.Identity, bias=T.ioB[:, 0:1]), on=tok["p_b2"])
             W("s", c)
-            c = [incs(kid_s(T.kg256[:, 16 * lo:16 * hi], T.L256[:, lo:hi])) for lo, hi in ((0, KG), (KG, 16))]
+            if KGV:
+                W("v", s_mk, c)
+            c = [incs((kid_v if KGV and lo else kid_s)(T.kg256[:, 16 * lo:16 * hi], T.L256[:, lo:hi])) for lo, hi in ((0, KG), (KG, 16)) if hi > lo]
             W("t", c_wk)
             tok["p_m3"] = incs(conv(T.p2[:, 0:16], Wk, lambda i: T.kg256[:, 16 * i:16 * i + 16], before=lambda i: [c[i >= KG]]))
         if x == "d":
@@ -477,39 +413,29 @@ def rank_program(g, core, T, topo):
             W("s", tok["LM3"])
             tok["b3"] = incs(s.activation(T.b3w[:], T.W[:, 4096:8192].indirect(T.LM3[:, 0:16]), F.Copy))
             tok["K3"] = [incs(s.activation(T.K3[:, K3V:256], T.W[:, 0:4096].indirect(T.LM3[:, K3V // 16:16]), F.Copy))] if K3V < 256 else []
+        if x == "e":
+            W("v", tok["LM3"])
+            tok["K3"].append(incs(v.tensor_copy(T.K3[:, 0:K3V], T.W[:, 0:4096].indirect(T.LM3[:, 0:K3V // 16]))))
         if x == "l":
             W("t", t_tt, *c_e)
             c = incs(*[te.matmul(T.pB[:, 16 * h:16 * h + 16], T.E01[:, 160 * h + 16 - 16 * u:160 * h + 144 - 16 * u], T.TT[:, 16 * u:16 * u + 16], u == 0, u == 1)
                        for h in range(2) for u in range(2)][1::2])
             W("s", c)
             tok["LB"] = incs(s.activation(T.LB[:], T.pB[:, 0:32], F.Copy), on=c)
-        if x == "e" and K3V:
-            W("v", tok["LM3"])
-            tok["K3"].append(incs(v.tensor_copy(T.K3[:, 0:K3V], T.W[:, 0:4096].indirect(T.LM3[:, 0:K3V // 16]))))
 
     for x in PLAN.split():
-        if x == "send":
-            if ("ve", B["a"]) in tok:
-                tok["ve", B["f"]] = tok["ve", B["a"]] + tok["ve", B["b"]]
-            for tk, to in zip(tok["ve", B["f"]], (others[:2], others[2:])) if RA2 else ((tok["ve", B["f"]][0], others),):
-                W("g", tk, *([] if RA2 else tok["ve", B["f"]]))
-                exchange(lambda k: T.AR[:, CAP * k - CAP:CAP * k], lambda k: RX[:, CAP * k:CAP * k + CAP], "ra", to)
+        if x[:4] == "send":
+            W("g", *[tok["ve", B[y]] for y in x[4:]])
+            exchange(lambda k: T.AR[:, CAP * k - CAP:CAP * k], lambda k: RX[:, CAP * k:CAP * k + CAP], "ra", [others[B[y][3]] for y in x[4:]])
         elif x[0] == "T":
             table(x[1])
         else:
             steps[x[:2]](B[x[2]])
 
-    W("v", tok["LB"], *tok["ve", B["o"]], *tok["ve", B["f"]])
-    W("s", tok["LB"], *tok["ve", B["o"]], *tok["ve", B["f"]])
-    arrived(v, "ra")
-    arrived(s, "ra")
-    if STORE == 2:
-        for a in (0, 256):
-            W("y", incs(v.tensor_copy(T.yb[:, a:a + 128], RX.indirect(T.LB[:, a // 16:a // 16 + 8]))),
-              incs(s.activation(T.yb[:, a + 128:a + 256], RX.indirect(T.LB[:, a // 16 + 8:a // 16 + 16]), F.Copy)))
-            dmas((sy, T.y[:, a:a + 256], T.yb[:, a:a + 256]))
-    else:
-        W("y", incs(v.tensor_copy(T.yb[:, 0:256], RX.indirect(T.LB[:, 0:16])), s.activation(T.yb[:, 256:512], RX.indirect(T.LB[:, 16:32]), F.Copy)))
-        dmas((sy, T.y[:], T.yb[:]))
+    for q in "vs":
+        W(q, tok["LB"], *[tok["ve", b] for b in B.values()])
+        arrived(queues[q], "ra")
+    W("y", incs(v.tensor_copy(T.yb[:, 0:256], RX.indirect(T.LB[:, 0:16])), s.activation(T.yb[:, 256:512], RX.indirect(T.LB[:, 16:32]), F.Copy)))
+    dmas((sy, T.y[:], T.yb[:]))
     g.wait_ge(T.sem.left, sum(sent))
     W("g", *[t for t in every if t not in waited])

from concourse.bass import DstId, RemoteDMATransfer
from concourse.mybir import dt, AluOpType, AxisListType, ActivationFunctionType

CAP = 160
NS = 140
HALF = 2048.0

SCRATCH = {
    "spi": ("sbuf", [8, 4], "int32"),
    "spf": ("sbuf", [8, 4], "float32"),
    "q8i": ("sbuf", [8, 512], "int32"),
    "q8f": ("sbuf", [8, 512], "float32"),
    "b0i": ("sbuf", [8, 2], "int32"),
    "b0f": ("sbuf", [8, 2], "float32"),
    "R8b": ("sbuf", [8, 128], "bfloat16"),
    "R8": ("sbuf", [8, 128], "float32"),
    "GE": ("sbuf", [128, 5, 33], "bfloat16"),
    "CB": ("sbuf", [128, 4, 32], "bfloat16"),
}
for _dt, _bufs in (
    ("int32", "ql 32 qT 32 X0 512 W 8208 k1i 2 QS 1120 K2 16 K3 256 b3w 256"),
    ("float32", "K1A 16 kgx 128 onef 1 e0 1 ioI 1 ioB 1 mk0 1 mku 1 mkb 1 mkt 1 bib 1"),
    ("bfloat16", "vcs 4096 ones 160 RST 128 BD 128 BDm 128 NL 128 NLm 128 E01 320 ID 128 WW 288 W16 144 MK 128 wt 16 cm1 640 cm2 640 "
                 "l1b 40 AR 1120 yb 512"),
    ("float16", "VAL 128 TT 32 SL 32 b2 16 C3 640 S3 640 C4 640 S4 640 kg256 256 G3 640 G4 640"),
    ("uint16", "LA 32 LB 32 L16 8 LM2 2 L256 16 LM3 16 l1s 40 l1 32 l2 40 i3 40 m4 40 i4 40 vn 40"),
):
    _w = _bufs.split()
    for _k in range(0, len(_w), 2):
        SCRATCH[_w[_k]] = ("sbuf", [128, int(_w[_k + 1])], _dt)
for _k in "pS pT pN pA p1 p2 pB pD".split():
    SCRATCH[_k] = ("psum", [128, 512], "float32")
SEMAPHORES = ["s%d" % i for i in range(NS)] + ["rk", "rq", "rl", "rqn", "rln", "ra", "left"]

A = AluOpType
F = ActivationFunctionType

PLAN = """Ta Tb c2o Tc c2a c2b c2c Td l2a Te l2b L3a l2c L3b l2o L3c i3a L3o i3b k3a i3c k3b i3o k3c m4a k3o m4b L4a m4c L4b
 m4o L4c i4a L4o i4b k4a i4c k4b i4o k4c vna k4o vnb vea senda vnc veb sendb vno vec sendc Tl veo"""
CUTS = (0, 160, 320, 480)
KV = (64, 64, 64, 64)
VV = (64, 64, 64, 64)
LS = "l2b l2o m4a m4b m4o"
KGV = 6
NEAR = ()
ALONE = ("ra",)
NEAR_STEP = 1
QL_Q = "sysysysy"
NK = [(1, 2), (2, 4)]
NK_LATE = [(4, 8), (8, 16)]
FILL_0 = (160, 160)
FILL_S = (224, 192, 512, 416, 448)
FILL_E = 512
FILL_G = 832
FILL_V = (128, 512)
FILL_Q = (256, 512)
X0_PRE = 256
Q8_S = 320
LATE_Q = "yys"
K3V = 160
KG = 8


def rank_program(g, core, T, topo):
    me = T.rank_of(core)
    if me is None:
        return
    v, s, te, sy = g.vector, g.scalar, g.tensor, g.sync
    queues = {"g": g, "v": v, "s": s, "t": te, "y": sy}
    used = [0]
    seen = {}
    waited = {}
    every = []

    def incs(*ins, n=1, on=None):
        name, base = on or ("s%d" % used[0], 0)
        used[0] += on is None
        for x in ins:
            x.then_inc(T.sem[name], n)
        tok = (name, base + n * len(ins))
        every.append(tok)
        return tok

    def dmas(*calls):
        return incs(*[q.dma_start(out, in_) for q, out, in_ in calls], n=16)

    def W(key, *toks):
        for tok in toks:
            if (key, tok) in seen:
                continue
            seen[(key, tok)] = True
            waited[tok] = True
            queues[key].wait_ge(T.sem[tok[0]], tok[1])

    def conv(out, wt, src, start=True, stop=True, before=lambda i: (), turn=range(16)):
        ins = None
        for i in turn:
            W("t", *before(i))
            ins = te.matmul(out, wt[:, 15 - i:143 - i], src(i), start and i == turn[0], stop and i == turn[-1])
        return ins

    def order(x):
        return sorted([r for r in range(4) if r != x], key=lambda r: topo.chip(T.cores[r]) == topo.chip(T.cores[x]))

    others = order(me)
    place = {r: k for k, r in enumerate([me] + others)}

    def engines_of(src, dst, sem):
        away = [d for d in T.cores if topo.chip(d) != topo.chip(src)]
        ae = topo.engines(src, away[0])
        if dst in away:
            n = len(ae) // len(away)
            return ae if sem in ALONE else ae[away.index(dst) * n:away.index(dst) * n + n]
        return [e for e in topo.engines(src, dst) if e not in ae][::NEAR_STEP]

    def near(x, y, sem):
        return sem + "n" if sem in NEAR and topo.chip(T.cores[x]) == topo.chip(T.cores[y]) else sem

    def arrived(q, sem):
        q.wait_ge(T.sem[sem], sum(len(engines_of(T.cores[r], core, sem[:2])) for r in others if near(r, me, sem[:2]) == sem))

    sent = []

    def exchange(src, dst, sem, others=others):
        tr = []
        for r in others:
            d = T.cores[r]
            a = topo.addr(d)
            tr.append(RemoteDMATransfer(dst_ids=[DstId(rid=a[0], pnc=a[1])], dma_engine_mask=sum(1 << e for e in engines_of(core, d, sem)),
                                        remote_sem=T.sem[near(r, me, sem)], src=src(place[r]), dst=dst(1 + order(r).index(me))))
        g.remote_dma_fused(tr, local_sem=T.sem.left)
        sent.append(sum(len(engines_of(core, T.cores[r], sem)) for r in others))

    SX = T.QS[:, 480:1120]
    RX = T.AR[:, 480:1120]

    d_sp = dmas((s, T.spi[:], T.spl[:]))
    d_q8 = dmas((sy, T.q8i[:], T.q[:]))
    d_ql = dmas(*[(queues[QL_Q[G]], T.ql[32 * (G // 2):32 * (G // 2) + 32, 16 * (G % 2):16 * (G % 2) + 16], T.q[16 * G:16 * G + 16, :]) for G in range(8)])
    d_k1 = dmas((sy, T.k1i[:], T.nk[:, 0:2]))
    d_b0 = dmas((sy, T.b0i[:], T.beg[:, 0:2]))
    d_w = [dmas((sy, T.W[0::16, 0:4096], T.kid[:, 0:4096]), *[(sy, T.W[o::st, 0:4096], T.nk[o::st, :]) for o, st in NK])]

    t_ones = incs(v.memset(T.ones[:], 1.0))
    t_z0 = incs(v.memset(T.W[:, 8192 - FILL_E:8208], 0))
    t_rst = incs(v.memset(T.GE[:], 0.0), v.memset(T.CB[:], 0.0), v.memset(T.RST[:], 1.0))
    t_sx0 = [incs(v.memset(T.QS[:, 480:480 + FILL_Q[0]], 0))]
    z = []
    MID = 4096 + FILL_G + FILL_V[-1] + FILL_S[-1]
    ends = {False: MID, True: 4096}
    assert sum(FILL_0 + FILL_S + FILL_V) + FILL_G + FILL_E == 4096

    def fill(q, n, late=False):
        a = ends[late]
        ends[late] += n
        if n:
            out = T.W[:, a:a + n]
            z.append((a, a + n, incs(v.memset(out, 0) if q == "v" else g.iota(out, [[0, n]], 0, 0) if q == "g" else
                                     s.activation(out, T.ones[:, 0:n] if n <= 160 else T.pD[:, 0:n] if late else T.W[:, 7680:7680 + n], F.Copy))))

    def sel(out, in_, pattern, op, base, cm, *deps):
        W("g", *deps)
        return incs(g.affine_select(out, in_, pattern, op, 0.0, base, cm))

    c_rb = sel(T.R8b[:], T.ones[0:8, 0:128], [[-1, 8], [0, 16]], A.is_equal, 0, 1, t_ones)
    W("t", c_rb)
    p_bd = incs(te.matmul(T.pB[:, 0:128], T.R8b[:], T.R8b[:], True, True))
    c_r8 = sel(T.R8[:], T.ones[0:8, 0:128], [[-1, 8], [0, 16]], A.is_equal, 0, 1)
    W("s", t_ones)
    for n in FILL_0:
        fill("s", n)
    W("s", t_z0)
    fill("s", FILL_S[0])
    W("s", p_bd)
    s_bd = incs(s.activation(T.BD[:], T.pB[:, 0:128], F.Copy))
    s_bm = incs(s.activation(T.BDm[:], T.pB[:, 0:128], F.Copy, scale=-1.0))
    W("s", d_q8)
    s_q8 = incs(s.activation(T.q8f[:, 0:Q8_S], T.q8i[:, 0:Q8_S], F.Copy))
    fill("s", FILL_S[1])
    c_id = sel(T.ID[:], T.ones[:, 0:128], [[-1, 128]], A.is_equal, 0, 1)
    c_nl = sel(T.NL[:], T.BD[:], [[1, 128]], A.is_gt, 0, -1, s_bd)
    W("s", c_nl)
    s_nl = incs(s.activation(T.NLm[:], T.NL[:], F.Copy, scale=-1.0))
    W("s", d_b0)
    s_b0 = incs(s.activation(T.b0f[:], T.b0i[:], F.Copy))

    W("v", t_rst)
    t_rst = incs(v.memset(T.RST[:, 0:128:32], 0.0), v.memset(T.GE[:, 0, 1:33], 1.0), on=t_rst)
    W("v", d_sp)
    t_spf = incs(v.tensor_copy(T.spf[:], T.spi[:]))
    t_cb = incs(*[v.memset(T.CB[:, r, 0:1], CAP / 16 * place[r]) for r in others])
    W("v", d_q8)
    t_q8 = incs(v.tensor_copy(T.q8f[:, Q8_S:512], T.q8i[:, Q8_S:512]))
    W("v", d_ql)
    t_qt = incs(v.transpose(T.qT[:], T.ql[:]))
    W("v", d_k1)
    t_k1 = incs(v.tensor_copy(T.K1A[:, 0:2], T.k1i[:]))
    W("g", t_k1)
    exchange(lambda k: T.K1A[:, 0:2], lambda k: T.K1A[:, 4 * k:4 * k + 2], "rk")
    fill("g", FILL_G, True)
    W("t", t_spf, c_r8)
    p_sp = incs(te.matmul(T.pS[:, 0:4], T.R8[:], T.spf[:], True, True))
    W("t", s_bd, t_cb, t_rst)
    te.matmul(T.pN[:, 0:128], T.BD[:], T.CB[:], True, False)
    te.matmul(T.pN[:, 0:32], T.BD[:], T.GE[:, 0, 0:32], False, False)
    W("t", s_q8)
    te.matmul(T.pD[:, 0:X0_PRE], T.R8[:], T.q8f[:, 0:X0_PRE], True, True)
    W("v", t_rst, p_sp, t_qt)
    t_ge = incs(*[v.tensor_scalar(T.GE[:, r, 1:33], T.qT[:], T.pS[:, r:r + 1], None, A.is_ge) for r in (1, 2, 3)])
    W("t", s_bm, c_nl)
    te.matmul(T.pN[:, 0:32], T.NL[:], T.GE[:, 0, 1:33], False, False)
    W("t", t_ge)
    for wt, a, c0 in ((T.BD, 32, 0), (T.BDm, 0, 0), (T.NL, 32, 1), (T.NL, 0, 0)):
        te.matmul(T.pN[:, a:a + 96], wt[:], T.GE[:, 1:4, c0:c0 + 32], False, False)
    W("t", s_nl)
    te.matmul(T.pN[:, 0:96], T.NLm[:], T.GE[:, 1:4, 1:33], False, False)
    p_e = incs(te.matmul(T.pN[:, 0:128], T.NLm[:], T.GE[:, 0:4, 0:32], False, True))
    W("t", t_q8)
    p_x0 = incs(te.matmul(T.pD[:, X0_PRE:512], T.R8[:], T.q8f[:, X0_PRE:512], True, True))
    W("t", t_ones)
    p_io = incs(te.matmul(T.p2[:, 0:1], T.NL[:], T.ones[:, 0:1], True, True))
    W("t", s_b0)
    p_b0 = incs(te.matmul(T.p1[:, 0:2], T.R8[:], T.b0f[:], True, True))
    for n in FILL_S[2:-1]:
        fill("s", n)
    W("s", p_x0)
    s_x0 = incs(s.activation(T.X0[:], T.pD[:], F.Copy), on=p_x0)
    t_sx0 += [incs(v.memset(T.QS[:, 480 + FILL_Q[0]:480 + FILL_Q[1]], 0))]
    W("v", t_ge)
    t_mk = incs(v.tensor_tensor(T.MK[:], T.GE[:, 0:4, 1:33], T.GE[:, 1:5, 1:33], A.subtract))
    W("v", p_e)
    t_u = incs(v.tensor_tensor_scan(T.pT[:, 0:128], T.RST[:], T.pN[:, 0:128], 0.0, A.mult, A.add))
    t_sx0 += [incs(v.memset(T.QS[:, 480 + FILL_Q[1]:1120], 0))]
    fill("v", FILL_V[0])
    W("v", t_mk, t_u)
    t_val = incs(v.tensor_tensor(T.VAL[:], T.MK[:], T.pT[:, 0:128], A.mult))
    fill("v", FILL_V[1], True)
    W("t", c_id, t_val)
    p_a = incs([te.matmul(T.pA[:, 0:32], T.ID[:], T.VAL[:, 32 * r:32 * r + 32], r == 0, r == 3) for r in range(4)][-1])
    W("v", p_a)
    t_la = incs(v.tensor_copy(T.LA[:], T.pA[:, 0:32]))
    t_w0 = incs(v.memset(T.WW[:], 0.0))
    Wk, Wc = T.WW[:, 0:144], T.WW[:, 144:288]
    c = sel(T.wt[:, 0:9], T.ones[:, 0:9], [[-16, 9]], A.is_ge, -1, 1)
    c_wc = sel(Wc[:, 15:144:16], T.wt[:, 0:9], [[16, 9]], A.is_ge, 15, -1, c, t_w0)
    c_wk = sel(Wk[:, 15:144:16], T.ones[:, 0:9], [[-16, 9]], A.is_equal, 0, 1)
    W("v", s_x0, t_la, *t_sx0)
    t_sc = incs(v.tensor_copy(SX.indirect(T.LA[:, 0:32]), T.X0[:]))

    fill("s", FILL_S[-1], True)
    for a, b in ((MID, 8192), (4096, MID)):
        qs = "yyy" if a == MID else LATE_Q
        for q in sorted(set(qs)):
            W(q, t_z0, *[tk for lo, hi, tk in z if lo < b and hi > a])
        d_w.append(dmas((queues[qs[0]], T.W[0::16, a:b], T.kid[:, a:b]), *[(queues[qs[o - 13]], T.W[o::16, a:b], T.beg[:, a - 4096:b - 4096]) for o in (14, 15)],
                        *[(sy, T.W[o::st, 0:4096], T.nk[o::st, :]) for o, st in NK_LATE if a == MID]))
    W("s", t_ones, p_io)
    c = incs(s.activation(T.ioI[:], T.p2[:, 0:1], F.Copy, bias=-8192.0), s.activation(T.mku[:], T.p2[:, 0:1], F.Relu, bias=14.0, scale=-1.0))
    s_mk = incs(s.activation(T.mkt[:], T.p2[:, 0:1], F.Copy, bias=-4110.5), s.activation(T.mk0[:], T.p2[:, 0:1], F.Relu, bias=1.0, scale=-1.0),
                s.activation(T.ioB[:], T.p2[:, 0:1], F.Copy, bias=2 * HALF))
    W("s", p_b0, c)
    c = incs(s.activation(T.mkb[:], T.mku[:], F.Relu, bias=0.5, scale=-1.0), s.activation(T.e0[:], T.p1[:, 0:1], F.Identity, bias=T.ioI[:, 0:1]), on=c)
    s_on = incs(s.activation(T.onef[:], T.ones[:, 0:1], F.Copy))
    W("s", t_la)
    s_sl = incs(s.activation(T.SL[:], T.LA[:], F.Copy))
    W("s", s_mk, c)
    s_bi = incs(s.activation(T.bib[:], T.mkt[:], F.Copy, scale=T.mkb[:, 0:1]))
    s_l16 = incs(s.activation(T.L16[:], T.BD[:, 0:128:16], F.Copy, bias=8192.0, scale=T.e0[:, 0:1]), on=c)

    W("g", t_sc)
    exchange(lambda k: SX[:, CAP * k:CAP * k + CAP], lambda k: T.QS[:, CAP * k - CAP:CAP * k], "rq")
    arrived(v, "rk")
    W("v", t_k1, t_sc)

    def level1(k, u, n):
        return v.tensor_scalar(T.cm1[:, CAP * k + u:CAP * k + CAP:n], SX[:, CAP * k + u:CAP * k + CAP:n], T.K1A[:, 4 * k:4 * k + 1],
                               -2.0 if k else 1.0, A.is_ge, A.mult)

    t_c1 = [incs(*[level1(k, u, 2) for k in (1, 2)]) for u in range(2)]
    t_c0 = incs(level1(0, 0, 1))
    arrived(s, "rk")
    W("s", t_sc)
    c = incs(s.activation(T.cm1[:, 480:640], SX[:, 480:640], F.Sign, bias=T.K1A[:, 12:13], scale=-1.0))
    W("t", c_wc, t_ge, c, t_c1[0])
    conv(T.pS[:, 0:30], Wc, lambda i: T.cm1[:, CAP + i:640:16], True, False, turn=range(0, 16, 2))
    te.matmul(T.pS[:, 0:20], T.BD[:], T.ones[:, 0:20], False, False)
    W("t", t_c1[1])
    p_c1 = incs(conv(T.pS[:, 0:30], Wc, lambda i: T.cm1[:, CAP + i:640:16], False, True, turn=range(1, 16, 2)))
    W("v", p_c1)
    t_l1 = incs(v.tensor_scalar(T.l1s[:, 10:40], T.pS[:, 0:30], -0.5, 7.75, A.mult, A.add), on=p_c1)
    W("g", t_l1)
    exchange(lambda k: T.l1s[:, 10 * k:10 * k + 10], lambda k: T.l1[:, 10 * k - 10:10 * k], "rl")
    W("v", s_sl)
    t_tt = incs(v.transpose(T.TT[:], T.SL[:]))
    c_e = [sel(T.E01[:, 160 * h:160 * h + 160], T.ones[:], [[-32, 5], [1000, 2], [-2, 16]], A.is_equal, -1000 - h, 1) for h in range(2)]
    arrived(sy, "rl")
    d_vec = dmas((sy, T.vcs[:], T.vec[:]))

    names = "abc"[:len(CUTS) - 1] + "o"
    B = {x: (lo, hi, bank, k) for k, (x, lo, hi, bank) in enumerate(zip(names, CUTS, CUTS[1:] + (640,), (T.pD, T.pT, T.pS)[:len(CUTS) - 1] + (T.pN,)))}
    own = B["o"]
    tok = {}

    def cols(x, b):
        return x[:, b[0]:b[1]]

    def lst(x, b):
        return x[:, b[0] // 16:b[1] // 16]

    def bank(b):
        return b[2][:, 0:(b[1] - b[0]) // 16]

    def lists(b, name, add):
        if name + names[b[3]] in LS:
            W("s", tok["p", b])
            tok[name, b] = incs(s.activation(lst(T[name], b), bank(b), F.Copy, bias=add), on=tok["p", b])
            return
        W("v", tok["p", b])
        tok[name, b] = incs(v.tensor_scalar(lst(T[name], b), bank(b), add, None, A.add), on=tok["p", b])

    def c2(b):
        W("v", tok["l0"], tok["K2"])
        kind = "o" if b is own else "n" if NEAR and b[0] >= 2 * CAP else ""
        if ("lb", kind) not in tok and b is not own:
            arrived(v, "rq" + kind)
            arrived(v, "rl" + kind)
        c = incs(v.tensor_tensor(cols(T.cm2, b), T.K2[:, 0:16].indirect(T.l1s[:, 0:10] if b is own else lst(T.l1, b)), cols(T.QS, b), A.is_le))
        if ("lb", kind) not in tok:
            lo, hi = {"o": (30, 40), "n": (20, 30), "": (0, 20 if NEAR else 30)}[kind]
            tok["lb", kind] = incs(v.tensor_copy(T.l1b[:, lo:hi], T.l1s[:, 0:10] if b is own else T.l1[:, lo:hi]))
        W("t", t_val, t_l1, tok["W16"], c)
        conv(bank(b), T.W16, lambda i: T.cm2[:, b[0] + i:b[1]:16], True, False)
        W("t", tok["lb", kind])
        tok["p", b] = incs(te.matmul(bank(b), T.ID[:], lst(T.l1b, b), False, True), on=c)

    def starts(out, win, l):
        return s.activation(out, win.indirect(l), F.Identity, bias=T.bib[:, 0:1], scale=T.mkb[:, 0:1])

    def level(b, lin, win, nodes, C, S, *deps):
        W("s", *deps[:1], tok[lin, b])
        W("v", *deps[1:], tok[lin, b])
        x = incs(v.tensor_tensor(cols(C, b), nodes.indirect(lst(T[lin], b)), cols(T.QS, b), A.is_le), on=tok[lin, b])
        y = incs(starts(cols(S, b), win, lst(T[lin], b)))
        W("t", x)
        conv(bank(b), Wc, lambda i: C[:, b[0] + i:b[1]:16], True, False)
        W("t", y)
        tok["p", b] = incs(conv(bank(b), Wc, lambda i: S[:, b[0] + i:b[1]:16], False, True), on=y)

    def kid_s(out, l):
        return s.activation(out, T.W[:, 0:8192].indirect(l), F.Copy, bias=-HALF, scale=T.mk0[:, 0:1])

    def kid_v(out, l):
        return v.tensor_scalar(out, T.W[:, 0:8192].indirect(l), T.mk0[:, 0:1], -HALF, A.mult, A.add)

    def shared(b, lin, out, n, on_v, on_s, *deps):
        c = []
        for q, lo, hi, f in (("v", b[0], b[0] + n, on_v), ("s", b[0] + n, b[1], on_s)):
            if hi > lo:
                W(q, *deps, tok[lin, b])
                c.append(f(out[:, lo:hi], T[lin][:, lo // 16:hi // 16]))
        return incs(*c)

    def kids(b, lin, G):
        c = shared(b, lin, G, KV[b[3]], kid_v, kid_s, s_mk)
        W("t", c_wk, c)
        tok["p", b] = incs(conv(bank(b), Wk, lambda i: G[:, b[0] + i:b[1]:16]), on=c)

    def vectors(b):
        win = T.vcs[:, 0:4096]
        tok["ve", b] = shared(b, "vn", T.AR, VV[b[3]], lambda o, l: v.tensor_copy(o, win.indirect(l)), lambda o, l: s.activation(o, win.indirect(l), F.Copy), d_vec)

    steps = {"c2": c2, "l2": lambda b: lists(b, "l2", 0.0),
             "L3": lambda b: level(b, "l2", T.b3w[:, 0:256], T.K3[:, 0:256], T.C3, T.S3, tok["b3"], *tok["K3"]),
             "i3": lambda b: lists(b, "i3", 2 * HALF), "k3": lambda b: kids(b, "i3", T.G3),
             "m4": lambda b: lists(b, "m4", HALF),
             "L4": lambda b: level(b, "m4", T.W[:, 4096:8192], T.W[:, 0:4096], T.C4, T.S4),
             "i4": lambda b: lists(b, "i4", 2 * HALF), "k4": lambda b: kids(b, "i4", T.G4),
             "vn": lambda b: lists(b, "vn", HALF), "ve": vectors}

    def table(x):
        if x == "a":
            W("s", s_l16, s_mk, *d_w)
            c = incs(s.activation(T.kgx[:], T.W[:, 0:8208].indirect(T.L16[:]), F.Copy, scale=T.mk0[:, 0:1]))
            W("s", c_wc)
            tok["W16"] = incs(s.activation(T.W16[:], Wc, F.Copy, scale=16.0))
            W("t", s_on, c)
            tok["p_m2"] = incs(te.matmul(T.p2[:, 0:1], T.kgx[:], T.onef[:], True, True), on=c)
            W("t", t_la, t_c0)
            c = incs(conv(T.pA[:, 0:10], Wc, lambda i: T.cm1[:, i:CAP:16]), on=t_c0)
            W("v", c)
            tok["l0"] = incs(v.tensor_copy(T.l1s[:, 0:10], T.pA[:, 0:10]), on=c)
        if x == "b":
            W("s", tok["p_m2"])
            tok["LM2"] = incs(s.activation(T.LM2[:, 0:1], T.p2[:, 0:1], F.Copy), on=tok["p_m2"])
            W("s", s_bi, tok["LM2"])
            c = incs(starts(T.b2[:], T.W[:, 4096:8192], T.LM2[:, 0:1]))
            W("t", c)
            tok["p_b2"] = incs(te.matmul(T.p1[:, 0:16], T.BD[:], T.b2[:], True, True), on=c)
            W("v", *d_w, tok["LM2"])
            tok["K2"] = incs(v.tensor_copy(T.K2[:], T.W[:, 0:4096].indirect(T.LM2[:, 0:1])))
        if x == "c":
            W("s", tok["p_b2"])
            c = incs(s.activation(T.L256[:], T.p1[:, 0:16], F.Identity, bias=T.ioB[:, 0:1]), on=tok["p_b2"])
            W("s", c)
            if KGV:
                W("v", s_mk, c)
            c = [incs((kid_v if KGV and lo else kid_s)(T.kg256[:, 16 * lo:16 * hi], T.L256[:, lo:hi])) for lo, hi in ((0, KG), (KG, 16)) if hi > lo]
            W("t", c_wk)
            tok["p_m3"] = incs(conv(T.p2[:, 0:16], Wk, lambda i: T.kg256[:, 16 * i:16 * i + 16], before=lambda i: [c[i >= KG]]))
        if x == "d":
            W("s", tok["p_m3"])
            tok["LM3"] = incs(s.activation(T.LM3[:], T.p2[:, 0:16], F.Copy, bias=HALF), on=tok["p_m3"])
            W("s", tok["LM3"])
            tok["b3"] = incs(s.activation(T.b3w[:], T.W[:, 4096:8192].indirect(T.LM3[:, 0:16]), F.Copy))
            tok["K3"] = [incs(s.activation(T.K3[:, K3V:256], T.W[:, 0:4096].indirect(T.LM3[:, K3V // 16:16]), F.Copy))] if K3V < 256 else []
        if x == "e":
            W("v", tok["LM3"])
            tok["K3"].append(incs(v.tensor_copy(T.K3[:, 0:K3V], T.W[:, 0:4096].indirect(T.LM3[:, 0:K3V // 16]))))
        if x == "l":
            W("t", t_tt, *c_e)
            c = incs(*[te.matmul(T.pB[:, 16 * h:16 * h + 16], T.E01[:, 160 * h + 16 - 16 * u:160 * h + 144 - 16 * u], T.TT[:, 16 * u:16 * u + 16], u == 0, u == 1)
                       for h in range(2) for u in range(2)][1::2])
            W("s", c)
            tok["LB"] = incs(s.activation(T.LB[:], T.pB[:, 0:32], F.Copy), on=c)

    for x in PLAN.split():
        if x[:4] == "send":
            W("g", *[tok["ve", B[y]] for y in x[4:]])
            exchange(lambda k: T.AR[:, CAP * k - CAP:CAP * k], lambda k: RX[:, CAP * k:CAP * k + CAP], "ra", [others[B[y][3]] for y in x[4:]])
        elif x[0] == "T":
            table(x[1])
        else:
            steps[x[:2]](B[x[2]])

    for q in "vs":
        W(q, tok["LB"], *[tok["ve", b] for b in B.values()])
        arrived(queues[q], "ra")
    W("y", incs(v.tensor_copy(T.yb[:, 0:256], RX.indirect(T.LB[:, 0:16])), s.activation(T.yb[:, 256:512], RX.indirect(T.LB[:, 16:32]), F.Copy)))
    dmas((sy, T.y[:], T.yb[:]))
    g.wait_ge(T.sem.left, sum(sent))
    W("g", *[t for t in every if t not in waited])
